import numpy as np
import ml_dtypes


def mxq(x, axis, fmt="e4m3"):
    dtype, down = {"e4m3": (ml_dtypes.float8_e4m3fn, 7), "e5m2": (ml_dtypes.float8_e5m2, 14)}[fmt]
    v = np.moveaxis(np.asarray(x, np.float32).astype(ml_dtypes.bfloat16).astype(np.float64), axis, -1)
    blocks = v.reshape(v.shape[:-1] + (-1, 32))
    amax = np.abs(blocks).max(-1, keepdims=True)
    byte = np.maximum(np.where(amax > 0, np.frexp(amax)[1] - 1 + 127, 0) - down, 1)
    scale = np.exp2(byte - 127.0)
    codes = (blocks / scale).astype(np.float32).astype(dtype).astype(np.float64)
    return np.moveaxis((codes * scale).reshape(v.shape), -1, axis)


WIDE = False


def mx_kscale(k):
    if not WIDE:
        return np.ones(k)
    levels = np.array([10, -10, 5, -5, 0])
    if k % 512:
        return np.exp2(np.random.permutation(np.resize(levels, k // 32))).repeat(32)
    a = np.empty((k // 512, 16))
    for p in range(k // 512):
        a[p, :8] = np.random.permutation(np.resize(levels, 8))
        for g in range(8):
            far = levels[np.abs(levels - a[p, g]) >= 10]
            a[p, g + 8] = far[np.random.randint(len(far))]
    return np.exp2(a.ravel()).repeat(32)


BF16 = ml_dtypes.bfloat16


def bf(x):
    return np.asarray(x, np.float32).astype(BF16)


def f64(x):
    return np.asarray(x).astype(np.float64)


E2M1 = np.array([0.0, 0.5, 1.0, 1.5, 2.0, 3.0, 4.0, 6.0, -0.0, -0.5, -1.0, -1.5, -2.0, -3.0, -4.0, -6.0])


def pack_weight(w, fmt):
    k, n = w.shape
    w = f64(bf(w)).reshape(k // 32, 32, n)
    amax = np.abs(w).max(1)
    if fmt == "e4m3":
        byte = np.frexp(amax)[1] - 1 + 127 - 7
    else:
        mant, ex = np.frexp(amax / 6.0)
        byte = np.where(mant > 0.5, ex, ex - 1) + 127
    byte = np.clip(np.where(amax > 0, byte, 1), 1, 254)
    scaled = (w * np.exp2(127.0 - byte)[:, None, :]).reshape(k, n).astype(np.float32)
    by_word = np.ascontiguousarray(scaled.reshape(k // 512, 128, 4, n).transpose(0, 1, 3, 2))
    if fmt == "e4m3":
        words = by_word.astype(ml_dtypes.float8_e4m3fn).view(np.uint8)
    else:
        c = by_word.astype(ml_dtypes.float4_e2m1fn).view(np.uint8) & 0xF
        words = c[..., 0::2] | (c[..., 1::2] << 4)
    return np.ascontiguousarray(words), np.ascontiguousarray(byte.astype(np.uint8).reshape(k // 512, 16, n))


def unpack_weight(words, scales, fmt):
    g, p, n, _ = words.shape
    if fmt == "e4m3":
        vals = np.ascontiguousarray(words).view(ml_dtypes.float8_e4m3fn).astype(np.float64)
    else:
        nib = np.empty((g, p, n, 4), np.uint8)
        nib[..., 0::2] = words & 0xF
        nib[..., 1::2] = words >> 4
        vals = E2M1[nib]
    vals = vals * np.repeat(np.exp2(scales.astype(np.float64) - 127.0), 8, axis=1)[..., None]
    return vals.transpose(0, 1, 3, 2).reshape(g * 512, n)
def pack4(w):
    words, scales = pack_weight(w, "e2m1")
    return words.reshape(words.shape[0], 128, -1), scales


def unpack4(words, scales):
    return unpack_weight(words.reshape(words.shape[0], 128, -1, 2), scales, "e2m1")


M, K, N, R, T = 3072, 1024, 1024, 512, 128


def draw0():
    s, t, u = mx_kscale(K), mx_kscale(N), mx_kscale(M)
    jl = np.random.standard_normal((N, R)) / np.sqrt(N) / t[:, None]
    jl_words, jl_scales = pack4(jl)
    return {"a": bf(np.random.standard_normal((M, K)) * s),
            "rinv": bf(np.random.standard_normal((K, N)) / np.sqrt(K) / s[:, None] * t),
            "w": bf(np.exp(0.3 * np.random.standard_normal(M)) * u),
            "jl_words": jl_words,
            "jl_scales": jl_scales,
            "b": bf(np.random.standard_normal((T, M)) / np.sqrt(M) / u)}


def core(a, rinv, w, jl_words, jl_scales, b):
    h = mxq(f64(a), 1, "e4m3") @ mxq(f64(rinv), 0, "e4m3")
    h = h * f64(w)[:, None]
    y = mxq(h, 1, "e4m3") @ unpack4(jl_words, jl_scales)
    lev = np.mean(np.square(y), axis=1)
    c = mxq(f64(b), 1, "e4m3") @ mxq(h, 0, "e4m3")
    return y, lev, c


def e4m3fn_bytes(y):
    return np.clip(np.asarray(y, np.float64), -448.0, 448.0).astype(np.float32).astype(ml_dtypes.float8_e4m3fn).view(np.uint8)


def e4m3fn_values(b):
    return np.asarray(b, np.uint8).view(ml_dtypes.float8_e4m3fn).astype(np.float64)


def setup_inputs():
    d = draw0()
    x0 = np.asarray(d['a']).astype(np.float64)
    s = (np.max(np.abs(x0), axis=(0,), keepdims=True) / 448.0).astype(np.float32)
    out = {}
    for k, v in d.items():
        if k == 'a':
            out['a_bytes'] = e4m3fn_bytes(x0 / s.astype(np.float64))
            out['a_scale'] = s
        else:
            out[k] = v
    return out


def reference(a_bytes, a_scale, rinv, w, jl_words, jl_scales, b):
    return core(e4m3fn_values(a_bytes) * a_scale.astype(np.float64), rinv, w, jl_words, jl_scales, b)

@@ -1,0 +1,469 @@
+from contextlib import ExitStack
+
+import concourse.mybir as mybir
+from concourse.masks import make_identity
+
+M, K, N, R, T = 3072, 1024, 1024, 512, 128
+FLOPS = 2 * M * K * N + 2 * M * N * R + 2 * T * M * N
+
+F32 = mybir.dt.float32
+BF16 = mybir.dt.bfloat16
+I32 = mybir.dt.int32
+U32 = mybir.dt.uint32
+U8 = mybir.dt.uint8
+FP8 = mybir.dt.float8_e4m3fn
+FP8X4 = mybir.dt.float8_e4m3fn_x4
+FP4X4 = mybir.dt.float4_e2m1fn_x4
+MULT = mybir.AluOpType.mult
+COPY = mybir.ActivationFunctionType.Copy
+SQUARE = mybir.ActivationFunctionType.Square
+
+P = 128
+X_DMA = ["a0", "r00", "r01", "a1", "r10", "r11", "a2", "j", "a3", "a4", "a5", "a6", "a7", "b", "a8", "a9", "a10", "a11"]
+X_SC = "vs"
+X_A2 = ("1111", 0, 24)
+MODE = 2
+X_WV = 1
+PTR, PH, PY = 3, 3, 2
+ORDER = [("EH1", 3, 1), ("EA1", 0, 1), ("M11", 2, 1), ("Y1", 5, 1), ("EY0", 6, 1), ("LV0", 6, 1), ("W0", -1, 1), ("P", -4, 1), ("M00", 1, 1), ("F01", 2, 1), ("BQ", 1, 1), ("F11", 2, 1), ("QH", 4, 1), ("M10", 1, 1), ("EY1", 5, 1), ("IC1", 5, 1), ("QC0", 4, 1), ("B", 0, 1), ("QC1", 7, 1), ("W1", -1, 1), ("TH0", 2, 1), ("R", 0, 1), ("IC0", 2, 1), ("TH1", 2, 1), ("F00", 1, 1), ("LV1", 5, 1), ("MS", -2, 1), ("EH0", 2, 1), ("QA", 0, 1), ("TA0", -1, 1), ("EA0", -1, 1), ("Y0", 5, 1), ("TA1", -1, 1), ("F10", 1, 1), ("M01", 1, 1)]
+RINV = [(-2, "I", 0, 0, 0, "s"), (1, "I", 1, 0, 0, "s"), (1, "Q", 1, 1), (-2, "I", 0, 1, 0, "s"), (-2, "I", 0, 1, 1, "s"), (1, "Q", 1, 0), (0, "I", 1, 1, 1, "s"), (-2, "I", 1, 0, 1, "s"), (0, "I", 1, 1, 0, "s"), (0, "Q", 0, 1), (-1, "I", 0, 0, 1, "v"), (-1, "Q", 0, 0)]
+X_EA = ("vsss", 10, 23)
+X_EH = ("ssss", 10, 20)
+X_EY = ("ssss", 9, 24)
+X_EE = ("svssssss", 10, 46)
+BSTART, BENG, CSTART, CENG = 13, "s", -36, "vs"
+GROUPS = M // 512
+TILES = M // P
+KG = K // 512
+NG = N // 512
+
+
+def tile_weighted_leverage_sketch_s8_kernel(
+    tc, a_bytes, a_scale, rinv, w, jl_words, jl_scales, b, y, lev, c
+):
+    nc = tc.nc
+    with ExitStack() as ctx:
+        keep = ctx.enter_context(tc.tile_pool(name="keep", bufs=1))
+        work = ctx.enter_context(tc.tile_pool(name="work", bufs=3))
+        psum = ctx.enter_context(tc.psum_pool(name="psum", bufs=1))
+        ctx.enter_context(tc.manual_schedule())
+
+        def bank(kind, bufs):
+            return psum.tile([P, 512], F32, name=kind, tag=kind, bufs=bufs)
+
+        scale_v = keep.tile([P, 8], F32, name="scale_v", align_bytes=64)
+        if MODE == 1:
+            nc.sync.dma_start(out=scale_v[:], in_=a_scale.rearrange("o (p c) -> p (o c)", p=P))
+        scale_p = keep.tile([P, KG, 2, 2], F32, name="scale_p", align_bytes=64)
+        nc.scalar.dma_start(out=scale_p[:].rearrange("p g u e -> p g (u e)"), in_=a_scale.rearrange("o (g p t) -> p (o g) t", p=P, t=4))
+        scale_sb = keep.tile([P, 2 * K if MODE == 1 else 8], F32, name="scale_sb", align_bytes=64)
+        w_bf = keep.tile([P, GROUPS, 4], BF16, name="w_bf", align_bytes=64)
+        nc.scalar.dma_start(out=w_bf[:], in_=w.rearrange("(g p t) -> p g t", p=P, t=4))
+
+        ident = keep.tile([P, P], F32, name="ident", align_bytes=64)
+        make_identity(nc, ident[:])
+        jsc = keep.tile([P, NG, R], U8, name="jsc", align_bytes=64)
+        nc.gpsimd.memset(jsc[:].rearrange("p g n -> p (g n)").bitcast(I32), 0)
+        lev_sb = keep.tile([P, 4, P], F32, name="lev_sb", align_bytes=64)
+        nc.gpsimd.memset(lev_sb[:], 0.0)
+
+        warm = keep.tile([P, 1], F32, name="warm")
+        nc.scalar.activation(out=warm[:], in_=ident[:, 0:1], func=SQUARE)
+
+        a_view = a_bytes.rearrange("(g p t) k -> g p t k", p=P, t=4)
+        a8 = {}
+
+        def load_a(pair):
+            g, t0 = pair // 2, 2 * (pair % 2)
+            a8[pair] = keep.tile([P, 2, K], U8, name=f"a8_{pair}", align_bytes=64)
+            nc.sync.dma_start(out=a8[pair][:], in_=a_view[g, :, t0 : t0 + 2, :])
+
+        raw = {}
+
+        def load_rinv(h, g):
+            raw[h, g] = keep.tile([P, 4, 512], BF16, name=f"raw_{h}{g}", align_bytes=64)
+            nc.sync.dma_start(
+                out=raw[h, g][:],
+                in_=rinv.rearrange("(g p t) n -> g p t n", p=P, t=4)[g, :, :, 512 * h : 512 * (h + 1)],
+            )
+
+        jw = keep.tile([P, NG, 2 * R], U8, name="jw", align_bytes=64)
+        jsc_i = jsc[:].rearrange("p g n -> p (g n)").bitcast(I32)
+        b_sb = keep.tile([P, M], BF16, name="b_sb", align_bytes=64)
+        for item in X_DMA:
+            if item[0] == "a":
+                load_a(int(item[1:]))
+            elif item[0] == "r":
+                load_rinv(int(item[1]), int(item[2]))
+            elif item[0] == "b":
+                nc.sync.dma_start(out=b_sb[:], in_=b)
+            else:
+                nc.sync.dma_start(out=jw[:], in_=jl_words.rearrange("g p n -> p g n"))
+                for q in range(4):
+                    nc.sync.dma_start(
+                        out=jsc_i[32 * q : 32 * q + 4, :].rearrange("p (g n) -> p g n", g=NG),
+                        in_=jl_scales[:, 4 * q : 4 * q + 4, :].bitcast(I32).rearrange("g q n -> q g n"),
+                    )
+
+        w_sb = keep.tile([P, GROUPS * 4], F32, name="w_sb", align_bytes=64)
+        nc.gpsimd.tensor_copy(out=w_sb[:], in_=w_bf[:].rearrange("p g t -> p (g t)"))
+
+        rq = keep.tile([P, KG, N], U32, name="rq", align_bytes=64)
+        rs = keep.tile([P, KG, N], U8, name="rs", align_bytes=64)
+        rg = {}
+
+        def interleave_rinv(h, g, u, eng):
+            if (h, g) not in rg:
+                rg[h, g] = keep.tile([P, 512, 4], BF16, name=f"rg_{h}{g}", align_bytes=64)
+            dst = rg[h, g][:].rearrange("p (u q e) t -> p u q t e", u=2, e=2)[:, u]
+            src = raw[h, g][:].rearrange("p t (q u e) -> p u q t e", u=2, e=2)[:, u]
+            if eng == "v":
+                nc.vector.tensor_copy(out=dst, in_=src)
+            else:
+                nc.scalar.copy(out=dst, in_=src)
+            rdone.add((h, g, u))
+
+        rdone = set()
+
+        def quantize_rinv(h, g):
+            assert (h, g, 0) in rdone and (h, g, 1) in rdone
+            cols = slice(512 * h, 512 * (h + 1))
+            nc.vector.quantize_mx(
+                out=rq[:, g, cols].bitcast(FP8X4), scales=rs[:, g, cols], in_=rg[h, g][:].rearrange("p n t -> p (n t)")
+            )
+
+        ag_pair, aq_pair, as_pair, htg_pair, hq_pair, hs_pair = {}, {}, {}, {}, {}, {}
+        ab, atr, ag, aq, asc = {}, {}, {}, {}, {}
+
+        def product(pair):
+            ab[pair] = work.tile([P, 2, K], BF16, name="ab", tag="ab", align_bytes=64)
+            nc.vector.tensor_tensor(
+                out=ab[pair][:].rearrange("p i k -> p (i k)"),
+                in0=a8[pair][:].rearrange("p i k -> p (i k)").bitcast(FP8),
+                in1=scale_sb[:],
+                op=MULT,
+            )
+
+        def claim(pair):
+            if pair < X_WV:
+                return
+            ab[pair] = work.tile([P, 2, K], BF16, name="ab", tag="ab", align_bytes=64)
+            nc.vector.memset(ab[pair][:, :, 0:2], 0.0)
+
+        def widen(pair, i):
+            if pair < X_WV:
+                if i == 0:
+                    ab[pair] = work.tile([P, 2, K], BF16, name="ab", tag="ab", align_bytes=64)
+                nc.vector.tensor_copy(out=ab[pair][:, i, :], in_=a8[pair][:, i, :].bitcast(FP8))
+                return
+            assert pair in ab
+            nc.gpsimd.tensor_copy(out=ab[pair][:, i, :], in_=a8[pair][:, i, :].bitcast(FP8))
+
+        def transpose_a(pair, g):
+            atr[pair, g] = bank("tr", PTR)
+            for u in range(2):
+                for i in range(2):
+                    s = 2 * u + i
+                    words = ab[pair][:, i, :].bitcast(F32)
+                    nc.tensor.transpose(
+                        atr[pair, g][:, s * P : (s + 1) * P], words[:, 256 * g + u : 256 * (g + 1) : 2], ident[:]
+                    )
+
+        def evac_words(dst, src, eng):
+            out = dst.bitcast(F32).rearrange("p (g r u) -> p g r u", g=2, u=2)
+            in_ = src[:].rearrange("p (g u r) -> p g r u", g=2, u=2)
+            if eng == "v":
+                nc.vector.tensor_copy(out=out, in_=in_)
+            else:
+                nc.scalar.copy(out=out, in_=in_)
+
+        def evac_a(pair, g):
+            if pair not in ag:
+                ag[pair] = work.tile([P, KG, 1024], BF16, name="ag", tag="ag", align_bytes=64)
+            if MODE == 2:
+                nc.vector.tensor_tensor(
+                    out=ag[pair][:, g].rearrange("p (c u e) -> p c u e", u=2, e=2),
+                    in0=atr[pair, g][:].bitcast(BF16).rearrange("p (u c e) -> p c u e", u=2, e=2),
+                    in1=scale_p[:, g].unsqueeze(1).to_broadcast([P, 2 * P, 2, 2]),
+                    op=MULT,
+                )
+            else:
+                out = ag[pair][:, g].bitcast(F32).rearrange("p (c u) -> p c u", u=2)
+                in_ = atr[pair, g][:].rearrange("p (u c) -> p c u", u=2)
+                if eng(X_EA, 2 * pair + g) == "v":
+                    nc.vector.tensor_copy(out=out, in_=in_)
+                else:
+                    nc.scalar.copy(out=out, in_=in_)
+
+        def quantize_a(pair):
+            q = work.tile([P, 512], U32, name="aq", tag="aq", align_bytes=64)
+            s = work.tile([P, 512], U8, name="asc", tag="asc", align_bytes=64)
+            nc.vector.quantize_mx(out=q[:].bitcast(FP8X4), scales=s[:], in_=ag[pair][:].rearrange("p g c -> p (g c)"))
+            for i in range(2):
+                aq[2 * pair + i] = q[:].rearrange("p (g i m) -> p i g m", g=KG, i=2)[:, i]
+                asc[2 * pair + i] = s[:].rearrange("p (g i m) -> p i g m", g=KG, i=2)[:, i]
+
+        hps, hb = {}, {}
+
+        def mm_h(i, h):
+            hps[i, h] = bank("h", PH)
+            for g in range(KG):
+                cols = slice(512 * h, 512 * (h + 1))
+                nc.tensor.matmul_mx(
+                    out=hps[i, h][:],
+                    lhsT=aq[i][:, g].bitcast(FP8X4),
+                    lhsT_scale=asc[i][:, g],
+                    rhs=rq[:, g, cols].bitcast(FP8X4),
+                    rhs_scale=rs[:, g, cols],
+                    start=(g == 0),
+                    stop=(g == KG - 1),
+                )
+
+        def evac_h(i, h, eng):
+            gg, t = i // 4, i % 4
+            if gg not in hb:
+                hb[gg] = work.tile([P, 4, N], BF16, name="hb", tag="hb", align_bytes=64)
+            dst = hb[gg][:, t, 512 * h : 512 * (h + 1)]
+            if eng == "v":
+                nc.vector.tensor_scalar(out=dst, in0=hps[i, h][:], scalar1=w_sb[:, i : i + 1], scalar2=None, op0=MULT)
+            else:
+                nc.scalar.activation(out=dst, in_=hps[i, h][:], func=COPY, scale=w_sb[:, i : i + 1])
+
+        htr, htg, hq, hs = {}, {}, {}, {}
+
+        def transpose_h(i):
+            htr[i] = bank("tr", PTR)
+            words = hb[i // 4][:, i % 4, :].bitcast(F32)
+            for s in range(4):
+                nc.tensor.transpose(htr[i][:, s * P : (s + 1) * P], words[:, s * P : (s + 1) * P], ident[:])
+
+        def evac_ht(i, eng):
+            if i // 2 not in htg_pair:
+                htg_pair[i // 2] = work.tile([P, 2, 1024], BF16, name="htg", tag="htg", align_bytes=64)
+            htg[i] = htg_pair[i // 2][:, i % 2]
+            evac_words(htg[i], htr[i], eng)
+
+        def quantize_ht(pair):
+            for i in range(2):
+                assert 2 * pair + i in htg
+            q = work.tile([P, 512], U32, name="hq", tag="hq", align_bytes=64)
+            s = work.tile([P, 512], U8, name="hs", tag="hs", align_bytes=64)
+            nc.vector.quantize_mx(
+                out=q[:].bitcast(FP8X4), scales=s[:], in_=htg_pair[pair][:].rearrange("p i c -> p (i c)")
+            )
+            for i in range(2):
+                hq[2 * pair + i] = q[:, 256 * i : 256 * (i + 1)]
+                hs[2 * pair + i] = s[:, 256 * i : 256 * (i + 1)]
+
+        yps = {}
+
+        def mm_y(i):
+            yps[i] = bank("y", PY)
+            for g in range(NG):
+                rows = slice(g * P, (g + 1) * P)
+                nc.tensor.matmul_mx(
+                    out=yps[i][:],
+                    lhsT=hq[i][:, rows].bitcast(FP8X4),
+                    lhsT_scale=hs[i][:, rows],
+                    rhs=jw[:, g, :].bitcast(FP4X4),
+                    rhs_scale=jsc[:, g, :],
+                    start=(g == 0),
+                    stop=(g == NG - 1),
+                )
+
+        y_view = y.rearrange("(g p t) n -> g t p n", p=P, t=4)
+
+        def evac_y(i, eng):
+            y_sb = work.tile([P, R], F32, name="y_sb", tag="y_sb", bufs=5, align_bytes=64)
+            if eng == "v":
+                nc.vector.tensor_copy(out=y_sb[:], in_=yps[i][:])
+            else:
+                nc.scalar.copy(out=y_sb[:], in_=yps[i][:])
+            nc.sync.dma_start(out=y_view[i // 4, i % 4], in_=y_sb[:])
+
+        def lev_y(i):
+            sq = work.tile([P, R], BF16, name="sq", tag="sq", align_bytes=64)
+            nc.scalar.activation(
+                out=sq[:], in_=yps[i][:], func=SQUARE, scale=R**-0.5,
+                accum_out=lev_sb[:, i % 4, i // 4 : i // 4 + 1],
+            )
+
+        cg, cq, cs = {}, {}, {}
+
+        def interleave_c(gg, h):
+            cg[gg, h] = work.tile([P, 512, 4], BF16, name="cg", tag="cg", align_bytes=64)
+            nc.vector.tensor_copy(
+                out=cg[gg, h][:].rearrange("p (c i) t -> p c t i", i=4),
+                in_=hb[gg][:, :, 512 * h : 512 * (h + 1)].rearrange("p t (c i) -> p c t i", i=4),
+            )
+
+        def quantize_c(gg, h):
+            cq[gg, h] = keep.tile([P, 512], U32, name=f"cq_{gg}{h}", align_bytes=64)
+            cs[gg, h] = keep.tile([P, 512], U8, name=f"cs_{gg}{h}", align_bytes=64)
+            nc.vector.quantize_mx(
+                out=cq[gg, h][:].bitcast(FP8X4), scales=cs[gg, h][:], in_=cg[gg, h][:].rearrange("p n t -> p (n t)")
+            )
+
+        btr = {}
+        bg = keep.tile([P, 6, P, 4], BF16, name="bg", align_bytes=64)
+        bq = keep.tile([P, 6 * P], U32, name="bq", align_bytes=64)
+        bs = keep.tile([P, 6 * P], U8, name="bs", align_bytes=64)
+
+        def transpose_b(j):
+            btr[j] = bank("tr", PTR)
+            words = b_sb[:].bitcast(F32)
+            for s in range(4):
+                g, u = 2 * j + s // 2, s % 2
+                nc.tensor.transpose(btr[j][:, s * P : (s + 1) * P], words[:, 256 * g + u : 256 * (g + 1) : 2], ident[:])
+
+        def evac_b(j, eng):
+            out = bg[:, 2 * j : 2 * j + 2].rearrange("p g r t -> p (g r t)").bitcast(F32).rearrange(
+                "p (g r u) -> p g r u", g=2, u=2
+            )
+            in_ = btr[j][:].rearrange("p (g u r) -> p g r u", g=2, u=2)
+            if eng == "v":
+                nc.vector.tensor_copy(out=out, in_=in_)
+            else:
+                nc.scalar.copy(out=out, in_=in_)
+
+        def quantize_b(j):
+            cols = slice(256 * j, 256 * (j + 1))
+            nc.vector.quantize_mx(
+                out=bq[:, cols].bitcast(FP8X4), scales=bs[:, cols],
+                in_=bg[:, 2 * j : 2 * j + 2].rearrange("p g r t -> p (g r t)"),
+            )
+
+        cps = {}
+
+        def mm_c(gg, h):
+            if gg == 0:
+                cps[h] = bank("h", PH)
+            rows = slice(gg * P, (gg + 1) * P)
+            nc.tensor.matmul_mx(
+                out=cps[h][:],
+                lhsT=bq[:, rows].bitcast(FP8X4),
+                lhsT_scale=bs[:, rows],
+                rhs=cq[gg, h][:].bitcast(FP8X4),
+                rhs_scale=cs[gg, h][:],
+                start=(gg == 0),
+                stop=(gg == GROUPS - 1),
+            )
+
+        def evac_c(h, eng):
+            c_sb = work.tile([P, 512], F32, name="c_sb", tag="c_sb", align_bytes=64)
+            out = c_sb[:].rearrange("p (q u e) -> p q u e", u=2, e=2)
+            in_ = cps[h][:].rearrange("p (u q e) -> p q u e", u=2, e=2)
+            if eng == "v":
+                nc.vector.tensor_copy(out=out, in_=in_)
+            else:
+                nc.scalar.copy(out=out, in_=in_)
+            nc.sync.dma_start(out=c[:, 512 * h : 512 * (h + 1)], in_=c_sb[:])
+
+        def eng(rule, i):
+            pattern, head, tail = rule
+            return "s" if i < head else "v" if i >= tail else pattern[i % len(pattern)]
+
+        for half in range(2 if MODE == 1 else 0):
+            sps = bank("tr", PTR)
+            for j in range(4):
+                c0 = 4 * half + j
+                nc.tensor.transpose(sps[:, j * P : (j + 1) * P], scale_v[:, c0 : c0 + 1].to_broadcast([P, P]), ident[:])
+            for i in range(2):
+                out = scale_sb[:, K * i : K * (i + 1)].rearrange("p (k c) -> p k c", c=8)[:, :, 4 * half : 4 * half + 4]
+                in_ = sps[:].rearrange("p (c k) -> p k c", c=4)
+                if X_SC[half] == "v":
+                    nc.vector.tensor_copy(out=out, in_=in_)
+                else:
+                    nc.scalar.copy(out=out, in_=in_)
+        done = set()
+        qdone = set()
+
+        def run(tok, pair):
+            d = ""
+            for j, ch in enumerate(tok):
+                if ch in "01":
+                    k, d = tok[:j], tok[j:]
+                    break
+            else:
+                k = tok
+            i = 2 * pair + int(d[0]) if d else 0
+            if k == "P":
+                if MODE == 1:
+                    product(pair)
+            elif k == "MS":
+                if MODE == 2:
+                    claim(pair)
+            elif k == "W":
+                if MODE == 2:
+                    widen(pair, int(d))
+            elif k == "TA":
+                transpose_a(pair, int(d))
+            elif k == "EA":
+                evac_a(pair, int(d))
+            elif k == "QA":
+                quantize_a(pair)
+            elif k == "M":
+                mm_h(i, int(d[1]))
+            elif k == "F":
+                h = int(d[1])
+                evac_h(i, h, eng(X_EE, 2 * i + h))
+                done.add((i, h))
+            elif k == "TH":
+                assert (i, 0) in done and (i, 1) in done
+                transpose_h(i)
+            elif k == "EH":
+                evac_ht(i, eng(X_EH, i))
+            elif k == "QH":
+                quantize_ht(pair)
+            elif k == "Y":
+                mm_y(i)
+            elif k == "EY":
+                evac_y(i, eng(X_EY, i))
+            elif k == "LV":
+                lev_y(i)
+            elif pair % 2 == 1:
+                h = int(d)
+                for j in range(4):
+                    assert (2 * pair + 1 - j, h) in done
+                (interleave_c if k == "IC" else quantize_c)(pair // 2, h)
+                if k == "QC":
+                    qdone.add((pair // 2, h))
+
+        cdone = 0
+        bdone = set()
+        for s in range(-3, TILES // 2 + 9):
+            for tok, lag, per in ORDER:
+                if tok == "R":
+                    for x in [x for x in RINV if x[0] == s]:
+                        if x[1] == "I":
+                            interleave_rinv(x[2], x[3], x[4], x[5])
+                        else:
+                            quantize_rinv(x[2], x[3])
+                elif tok == "B":
+                    if 0 <= s - BSTART < 3:
+                        transpose_b(s - BSTART)
+                        evac_b(s - BSTART, BENG)
+                elif tok == "BQ":
+                    if 0 <= s - BSTART - lag < 3:
+                        quantize_b(s - BSTART - lag)
+                        bdone.add(s - BSTART - lag)
+                elif 0 <= s - lag < TILES // 2:
+                    run(tok, s - lag)
+            while s >= CSTART and cdone < GROUPS and {(cdone, 0), (cdone, 1)} <= qdone and cdone // 2 in bdone:
+                for h in range(2):
+                    mm_c(cdone, h)
+                    if cdone == GROUPS - 1:
+                        evac_c(h, CENG[h])
+                cdone += 1
+        assert cdone == GROUPS
+
+        lev_rows = keep.tile([P, 512], F32, name="lev_rows", align_bytes=64)
+        for t0 in (0, 2):
+            lps = bank("tr", PTR)
+            for j in range(2):
+                nc.tensor.transpose(lps[:, j * P : (j + 1) * P], lev_sb[:, t0 + j, :], ident[:])
+            nc.vector.tensor_copy(
+                out=lev_rows[:GROUPS, :].rearrange("g (p t) -> g p t", t=4)[:, :, t0 : t0 + 2],
+                in_=lps[:GROUPS, : 2 * P].rearrange("g (t p) -> g p t", t=2),
+            )
+        nc.sync.dma_start(out=lev.rearrange("(g m) -> g m", g=GROUPS), in_=lev_rows[:GROUPS, :])

@@ -19,23 +19,11 @@ COPY = mybir.ActivationFunctionType.Copy
 SQUARE = mybir.ActivationFunctionType.Square
 
 P = 128
-X_DMA = ["a0", "r00", "r01", "a1", "r10", "r11", "a2", "j", "a3", "a4", "a5", "a6", "a7", "b", "a8", "a9", "a10", "a11"]
-X_SC = "vs"
-X_A2 = ("1111", 0, 24)
-MODE = 2
-X_WV = 1
-PTR, PH, PY = 3, 3, 2
-ORDER = [("EH1", 3, 1), ("EA1", 0, 1), ("M11", 2, 1), ("Y1", 5, 1), ("EY0", 6, 1), ("LV0", 6, 1), ("W0", -1, 1), ("P", -4, 1), ("M00", 1, 1), ("F01", 2, 1), ("BQ", 1, 1), ("F11", 2, 1), ("QH", 4, 1), ("M10", 1, 1), ("EY1", 5, 1), ("IC1", 5, 1), ("QC0", 4, 1), ("B", 0, 1), ("QC1", 7, 1), ("W1", -1, 1), ("TH0", 2, 1), ("R", 0, 1), ("IC0", 2, 1), ("TH1", 2, 1), ("F00", 1, 1), ("LV1", 5, 1), ("MS", -2, 1), ("EH0", 2, 1), ("QA", 0, 1), ("TA0", -1, 1), ("EA0", -1, 1), ("Y0", 5, 1), ("TA1", -1, 1), ("F10", 1, 1), ("M01", 1, 1)]
-RINV = [(-2, "I", 0, 0, 0, "s"), (1, "I", 1, 0, 0, "s"), (1, "Q", 1, 1), (-2, "I", 0, 1, 0, "s"), (-2, "I", 0, 1, 1, "s"), (1, "Q", 1, 0), (0, "I", 1, 1, 1, "s"), (-2, "I", 1, 0, 1, "s"), (0, "I", 1, 1, 0, "s"), (0, "Q", 0, 1), (-1, "I", 0, 0, 1, "v"), (-1, "Q", 0, 0)]
-X_EA = ("vsss", 10, 23)
-X_EH = ("ssss", 10, 20)
-X_EY = ("ssss", 9, 24)
-X_EE = ("svssssss", 10, 46)
-BSTART, BENG, CSTART, CENG = 13, "s", -36, "vs"
 GROUPS = M // 512
-TILES = M // P
+PAIRS = M // (2 * P)
 KG = K // 512
 NG = N // 512
+BANKS = 8
 
 
 def tile_weighted_leverage_sketch_s8_kernel(
@@ -48,422 +36,404 @@ def tile_weighted_leverage_sketch_s8_kernel(
         psum = ctx.enter_context(tc.psum_pool(name="psum", bufs=1))
         ctx.enter_context(tc.manual_schedule())
 
-        def bank(kind, bufs):
-            return psum.tile([P, 512], F32, name=kind, tag=kind, bufs=bufs)
+        ring = list(range(BANKS))
 
-        scale_v = keep.tile([P, 8], F32, name="scale_v", align_bytes=64)
-        if MODE == 1:
-            nc.sync.dma_start(out=scale_v[:], in_=a_scale.rearrange("o (p c) -> p (o c)", p=P))
+        def take_bank(hold=False):
+            number = ring[0]
+            ring.remove(number)
+            if not hold:
+                ring.append(number)
+            return psum.tile([P, 512], F32, name=f"bank{number}", tag=f"bank{number}")
+
+        def copy_on(engine, out, in_):
+            if engine == "vector":
+                nc.vector.tensor_copy(out=out, in_=in_)
+            else:
+                nc.scalar.copy(out=out, in_=in_)
+
         scale_p = keep.tile([P, KG, 2, 2], F32, name="scale_p", align_bytes=64)
-        nc.scalar.dma_start(out=scale_p[:].rearrange("p g u e -> p g (u e)"), in_=a_scale.rearrange("o (g p t) -> p (o g) t", p=P, t=4))
-        scale_sb = keep.tile([P, 2 * K if MODE == 1 else 8], F32, name="scale_sb", align_bytes=64)
+        nc.scalar.dma_start(
+            out=scale_p[:].rearrange("p g u e -> p g (u e)"),
+            in_=a_scale.rearrange("o (g p t) -> p (o g) t", p=P, t=4),
+        )
         w_bf = keep.tile([P, GROUPS, 4], BF16, name="w_bf", align_bytes=64)
         nc.scalar.dma_start(out=w_bf[:], in_=w.rearrange("(g p t) -> p g t", p=P, t=4))
 
         ident = keep.tile([P, P], F32, name="ident", align_bytes=64)
         make_identity(nc, ident[:])
-        jsc = keep.tile([P, NG, R], U8, name="jsc", align_bytes=64)
-        nc.gpsimd.memset(jsc[:].rearrange("p g n -> p (g n)").bitcast(I32), 0)
-        lev_sb = keep.tile([P, 4, P], F32, name="lev_sb", align_bytes=64)
-        nc.gpsimd.memset(lev_sb[:], 0.0)
-
-        warm = keep.tile([P, 1], F32, name="warm")
-        nc.scalar.activation(out=warm[:], in_=ident[:, 0:1], func=SQUARE)
+        j_scales = keep.tile([P, NG, R], U8, name="j_scales", align_bytes=64)
+        j_scales_i32 = j_scales[:].rearrange("p g n -> p (g n)").bitcast(I32)
+        nc.vector.memset(j_scales_i32, 0)
+        lev_sb = keep.tile([P, 4, 32], F32, name="lev_sb", align_bytes=64)
+        nc.vector.memset(lev_sb[:], 0.0)
 
         a_view = a_bytes.rearrange("(g p t) k -> g p t k", p=P, t=4)
-        a8 = {}
+        rinv_view = rinv.rearrange("(g p t) n -> g p t n", p=P, t=4)
+        a8, r_raw = {}, {}
 
         def load_a(pair):
-            g, t0 = pair // 2, 2 * (pair % 2)
+            t0 = 2 * (pair % 2)
             a8[pair] = keep.tile([P, 2, K], U8, name=f"a8_{pair}", align_bytes=64)
-            nc.sync.dma_start(out=a8[pair][:], in_=a_view[g, :, t0 : t0 + 2, :])
-
-        raw = {}
+            nc.sync.dma_start(out=a8[pair][:], in_=a_view[pair // 2, :, t0 : t0 + 2, :])
 
         def load_rinv(h, g):
-            raw[h, g] = keep.tile([P, 4, 512], BF16, name=f"raw_{h}{g}", align_bytes=64)
-            nc.sync.dma_start(
-                out=raw[h, g][:],
-                in_=rinv.rearrange("(g p t) n -> g p t n", p=P, t=4)[g, :, :, 512 * h : 512 * (h + 1)],
-            )
+            r_raw[h, g] = keep.tile([P, 4, 512], BF16, name=f"r_raw_{h}{g}", align_bytes=64)
+            nc.sync.dma_start(out=r_raw[h, g][:], in_=rinv_view[g, :, :, 512 * h : 512 * (h + 1)])
 
-        jw = keep.tile([P, NG, 2 * R], U8, name="jw", align_bytes=64)
-        jsc_i = jsc[:].rearrange("p g n -> p (g n)").bitcast(I32)
+        j_words = keep.tile([P, NG, 2 * R], U8, name="j_words", align_bytes=64)
         b_sb = keep.tile([P, M], BF16, name="b_sb", align_bytes=64)
-        for item in X_DMA:
-            if item[0] == "a":
-                load_a(int(item[1:]))
-            elif item[0] == "r":
-                load_rinv(int(item[1]), int(item[2]))
-            elif item[0] == "b":
-                nc.sync.dma_start(out=b_sb[:], in_=b)
-            else:
-                nc.sync.dma_start(out=jw[:], in_=jl_words.rearrange("g p n -> p g n"))
-                for q in range(4):
-                    nc.sync.dma_start(
-                        out=jsc_i[32 * q : 32 * q + 4, :].rearrange("p (g n) -> p g n", g=NG),
-                        in_=jl_scales[:, 4 * q : 4 * q + 4, :].bitcast(I32).rearrange("g q n -> q g n"),
-                    )
+
+        for g in range(KG):
+            load_a(g)
+            load_rinv(0, g)
+        for g in range(KG):
+            load_rinv(1, g)
+        load_a(2)
+        nc.sync.dma_start(out=b_sb[:], in_=b)
+        load_a(3)
+        nc.sync.dma_start(out=j_words[:], in_=jl_words.rearrange("g p n -> p g n"))
+        for q in range(4):
+            nc.sync.dma_start(
+                out=j_scales_i32[32 * q : 32 * q + 4, :].rearrange("p (g n) -> p g n", g=NG),
+                in_=jl_scales[:, 4 * q : 4 * q + 4, :].bitcast(I32).rearrange("g q n -> q g n"),
+            )
+        for pair in range(4, PAIRS):
+            load_a(pair)
 
         w_sb = keep.tile([P, GROUPS * 4], F32, name="w_sb", align_bytes=64)
-        nc.gpsimd.tensor_copy(out=w_sb[:], in_=w_bf[:].rearrange("p g t -> p (g t)"))
+        nc.scalar.activation(out=w_sb[:], in_=w_bf[:].rearrange("p g t -> p (g t)"), func=COPY)
 
-        rq = keep.tile([P, KG, N], U32, name="rq", align_bytes=64)
-        rs = keep.tile([P, KG, N], U8, name="rs", align_bytes=64)
-        rg = {}
+        r_codes = keep.tile([P, KG, N], U32, name="r_codes", align_bytes=64)
+        r_scales = keep.tile([P, KG, N], U8, name="r_scales", align_bytes=64)
+        r_grouped = {}
 
-        def interleave_rinv(h, g, u, eng):
-            if (h, g) not in rg:
-                rg[h, g] = keep.tile([P, 512, 4], BF16, name=f"rg_{h}{g}", align_bytes=64)
-            dst = rg[h, g][:].rearrange("p (u q e) t -> p u q t e", u=2, e=2)[:, u]
-            src = raw[h, g][:].rearrange("p t (q u e) -> p u q t e", u=2, e=2)[:, u]
-            if eng == "v":
-                nc.vector.tensor_copy(out=dst, in_=src)
-            else:
-                nc.scalar.copy(out=dst, in_=src)
-            rdone.add((h, g, u))
-
-        rdone = set()
-
-        def quantize_rinv(h, g):
-            assert (h, g, 0) in rdone and (h, g, 1) in rdone
-            cols = slice(512 * h, 512 * (h + 1))
-            nc.vector.quantize_mx(
-                out=rq[:, g, cols].bitcast(FP8X4), scales=rs[:, g, cols], in_=rg[h, g][:].rearrange("p n t -> p (n t)")
+        def interleave_rinv(h, g, u, engine):
+            if (h, g) not in r_grouped:
+                r_grouped[h, g] = keep.tile([P, 512, 4], BF16, name=f"r_grouped_{h}{g}", align_bytes=64)
+            copy_on(
+                engine,
+                r_grouped[h, g][:].rearrange("p (u q e) t -> p u q t e", u=2, e=2)[:, u],
+                r_raw[h, g][:].rearrange("p t (q u e) -> p u q t e", u=2, e=2)[:, u],
             )
 
-        ag_pair, aq_pair, as_pair, htg_pair, hq_pair, hs_pair = {}, {}, {}, {}, {}, {}
-        ab, atr, ag, aq, asc = {}, {}, {}, {}, {}
+        def quantize_rinv(h, g):
+            cols = slice(512 * h, 512 * (h + 1))
+            nc.vector.quantize_mx(
+                out=r_codes[:, g, cols].bitcast(FP8X4),
+                scales=r_scales[:, g, cols],
+                in_=r_grouped[h, g][:].rearrange("p n t -> p (n t)"),
+            )
 
-        def product(pair):
-            ab[pair] = work.tile([P, 2, K], BF16, name="ab", tag="ab", align_bytes=64)
+        a_wide, a_bank, a_grouped, a_codes, a_scales = {}, {}, {}, {}, {}
+
+        def widen(pair, engine):
+            a_wide[pair] = work.tile([P, 2 * K], BF16, name="a_wide", tag="a_ring", align_bytes=64)
+            engine.tensor_copy(out=a_wide[pair][:], in_=a8[pair][:].rearrange("p i k -> p (i k)").bitcast(FP8))
+
+        def transpose_a(pair):
+            words = a_wide[pair][:].bitcast(F32).rearrange("p (i k) -> p i k", i=2)
+            for g in range(KG):
+                a_bank[pair, g] = take_bank()
+                for u in range(2):
+                    for i in range(2):
+                        s = 2 * u + i
+                        nc.tensor.transpose(
+                            a_bank[pair, g][:, s * P : (s + 1) * P],
+                            words[:, i, 256 * g + u : 256 * (g + 1) : 2],
+                            ident[:],
+                        )
+
+        def scale_a(pair, g):
+            if g == 0:
+                a_grouped[pair] = work.tile([P, 2 * K], BF16, name="a_grouped", tag="a_ring", align_bytes=64)
             nc.vector.tensor_tensor(
-                out=ab[pair][:].rearrange("p i k -> p (i k)"),
-                in0=a8[pair][:].rearrange("p i k -> p (i k)").bitcast(FP8),
-                in1=scale_sb[:],
+                out=a_grouped[pair][:, K * g : K * (g + 1)].rearrange("p (c u e) -> p c u e", u=2, e=2),
+                in0=a_bank[pair, g][:].bitcast(BF16).rearrange("p (u c e) -> p c u e", u=2, e=2),
+                in1=scale_p[:, g].unsqueeze(1).to_broadcast([P, 2 * P, 2, 2]),
                 op=MULT,
             )
 
-        def claim(pair):
-            if pair < X_WV:
-                return
-            ab[pair] = work.tile([P, 2, K], BF16, name="ab", tag="ab", align_bytes=64)
-            nc.vector.memset(ab[pair][:, :, 0:2], 0.0)
-
-        def widen(pair, i):
-            if pair < X_WV:
-                if i == 0:
-                    ab[pair] = work.tile([P, 2, K], BF16, name="ab", tag="ab", align_bytes=64)
-                nc.vector.tensor_copy(out=ab[pair][:, i, :], in_=a8[pair][:, i, :].bitcast(FP8))
-                return
-            assert pair in ab
-            nc.gpsimd.tensor_copy(out=ab[pair][:, i, :], in_=a8[pair][:, i, :].bitcast(FP8))
-
-        def transpose_a(pair, g):
-            atr[pair, g] = bank("tr", PTR)
-            for u in range(2):
-                for i in range(2):
-                    s = 2 * u + i
-                    words = ab[pair][:, i, :].bitcast(F32)
-                    nc.tensor.transpose(
-                        atr[pair, g][:, s * P : (s + 1) * P], words[:, 256 * g + u : 256 * (g + 1) : 2], ident[:]
-                    )
-
-        def evac_words(dst, src, eng):
-            out = dst.bitcast(F32).rearrange("p (g r u) -> p g r u", g=2, u=2)
-            in_ = src[:].rearrange("p (g u r) -> p g r u", g=2, u=2)
-            if eng == "v":
-                nc.vector.tensor_copy(out=out, in_=in_)
-            else:
-                nc.scalar.copy(out=out, in_=in_)
-
-        def evac_a(pair, g):
-            if pair not in ag:
-                ag[pair] = work.tile([P, KG, 1024], BF16, name="ag", tag="ag", align_bytes=64)
-            if MODE == 2:
-                nc.vector.tensor_tensor(
-                    out=ag[pair][:, g].rearrange("p (c u e) -> p c u e", u=2, e=2),
-                    in0=atr[pair, g][:].bitcast(BF16).rearrange("p (u c e) -> p c u e", u=2, e=2),
-                    in1=scale_p[:, g].unsqueeze(1).to_broadcast([P, 2 * P, 2, 2]),
-                    op=MULT,
-                )
-            else:
-                out = ag[pair][:, g].bitcast(F32).rearrange("p (c u) -> p c u", u=2)
-                in_ = atr[pair, g][:].rearrange("p (u c) -> p c u", u=2)
-                if eng(X_EA, 2 * pair + g) == "v":
-                    nc.vector.tensor_copy(out=out, in_=in_)
-                else:
-                    nc.scalar.copy(out=out, in_=in_)
+        def quantize(codes, scales, key, grouped, name, pool=work):
+            codes[key] = pool.tile([P, 512], U32, name=name + "_codes", tag=name + "_codes", align_bytes=64)
+            scales[key] = pool.tile([P, 512], U8, name=name + "_scales", tag=name + "_scales", align_bytes=64)
+            nc.vector.quantize_mx(out=codes[key][:].bitcast(FP8X4), scales=scales[key][:], in_=grouped)
 
         def quantize_a(pair):
-            q = work.tile([P, 512], U32, name="aq", tag="aq", align_bytes=64)
-            s = work.tile([P, 512], U8, name="asc", tag="asc", align_bytes=64)
-            nc.vector.quantize_mx(out=q[:].bitcast(FP8X4), scales=s[:], in_=ag[pair][:].rearrange("p g c -> p (g c)"))
-            for i in range(2):
-                aq[2 * pair + i] = q[:].rearrange("p (g i m) -> p i g m", g=KG, i=2)[:, i]
-                asc[2 * pair + i] = s[:].rearrange("p (g i m) -> p i g m", g=KG, i=2)[:, i]
+            quantize(a_codes, a_scales, pair, a_grouped[pair][:], "a")
 
-        hps, hb = {}, {}
+        h_bank, h_rows = {}, {}
 
-        def mm_h(i, h):
-            hps[i, h] = bank("h", PH)
+        def matmul_h(pair, i, h):
+            h_bank[pair, i, h] = take_bank()
+            cols = slice(512 * h, 512 * (h + 1))
             for g in range(KG):
-                cols = slice(512 * h, 512 * (h + 1))
+                rows = slice((2 * g + i) * P, (2 * g + i + 1) * P)
                 nc.tensor.matmul_mx(
-                    out=hps[i, h][:],
-                    lhsT=aq[i][:, g].bitcast(FP8X4),
-                    lhsT_scale=asc[i][:, g],
-                    rhs=rq[:, g, cols].bitcast(FP8X4),
-                    rhs_scale=rs[:, g, cols],
+                    out=h_bank[pair, i, h][:],
+                    lhsT=a_codes[pair][:, rows].bitcast(FP8X4),
+                    lhsT_scale=a_scales[pair][:, rows],
+                    rhs=r_codes[:, g, cols].bitcast(FP8X4),
+                    rhs_scale=r_scales[:, g, cols],
                     start=(g == 0),
                     stop=(g == KG - 1),
                 )
 
-        def evac_h(i, h, eng):
-            gg, t = i // 4, i % 4
-            if gg not in hb:
-                hb[gg] = work.tile([P, 4, N], BF16, name="hb", tag="hb", align_bytes=64)
-            dst = hb[gg][:, t, 512 * h : 512 * (h + 1)]
-            if eng == "v":
-                nc.vector.tensor_scalar(out=dst, in0=hps[i, h][:], scalar1=w_sb[:, i : i + 1], scalar2=None, op0=MULT)
+        def weigh_h(pair, i, h, engine):
+            group, t = pair // 2, 2 * (pair % 2) + i
+            if group not in h_rows:
+                h_rows[group] = work.tile([P, 4, N], BF16, name="h_rows", tag="h_rows", align_bytes=64)
+            out = h_rows[group][:, t, 512 * h : 512 * (h + 1)]
+            weight = w_sb[:, 4 * group + t : 4 * group + t + 1]
+            if engine == "vector":
+                nc.vector.tensor_scalar(out=out, in0=h_bank[pair, i, h][:], scalar1=weight, scalar2=None, op0=MULT)
             else:
-                nc.scalar.activation(out=dst, in_=hps[i, h][:], func=COPY, scale=w_sb[:, i : i + 1])
+                nc.scalar.activation(out=out, in_=h_bank[pair, i, h][:], func=COPY, scale=weight)
 
-        htr, htg, hq, hs = {}, {}, {}, {}
+        ht_bank, ht_grouped, ht_codes, ht_scales = {}, {}, {}, {}
 
-        def transpose_h(i):
-            htr[i] = bank("tr", PTR)
-            words = hb[i // 4][:, i % 4, :].bitcast(F32)
-            for s in range(4):
-                nc.tensor.transpose(htr[i][:, s * P : (s + 1) * P], words[:, s * P : (s + 1) * P], ident[:])
+        def transpose_h(pair):
+            for i in range(2):
+                ht_bank[pair, i] = take_bank()
+                words = h_rows[pair // 2][:, 2 * (pair % 2) + i, :].bitcast(F32)
+                for s in range(4):
+                    nc.tensor.transpose(
+                        ht_bank[pair, i][:, s * P : (s + 1) * P], words[:, s * P : (s + 1) * P], ident[:]
+                    )
 
-        def evac_ht(i, eng):
-            if i // 2 not in htg_pair:
-                htg_pair[i // 2] = work.tile([P, 2, 1024], BF16, name="htg", tag="htg", align_bytes=64)
-            htg[i] = htg_pair[i // 2][:, i % 2]
-            evac_words(htg[i], htr[i], eng)
+        def copy_words(engine, grouped, bank):
+            copy_on(
+                engine,
+                grouped.bitcast(F32).rearrange("p (g r u) -> p g r u", g=2, u=2),
+                bank[:].rearrange("p (g u r) -> p g r u", g=2, u=2),
+            )
+
+        def copy_ht(pair, i, engine):
+            if i == 0:
+                ht_grouped[pair] = work.tile([P, 2 * N], BF16, name="ht_grouped", tag="ht_grouped", align_bytes=64)
+            copy_words(engine, ht_grouped[pair][:, N * i : N * (i + 1)], ht_bank[pair, i])
 
         def quantize_ht(pair):
-            for i in range(2):
-                assert 2 * pair + i in htg
-            q = work.tile([P, 512], U32, name="hq", tag="hq", align_bytes=64)
-            s = work.tile([P, 512], U8, name="hs", tag="hs", align_bytes=64)
-            nc.vector.quantize_mx(
-                out=q[:].bitcast(FP8X4), scales=s[:], in_=htg_pair[pair][:].rearrange("p i c -> p (i c)")
-            )
-            for i in range(2):
-                hq[2 * pair + i] = q[:, 256 * i : 256 * (i + 1)]
-                hs[2 * pair + i] = s[:, 256 * i : 256 * (i + 1)]
+            quantize(ht_codes, ht_scales, pair, ht_grouped[pair][:], "ht")
 
-        yps = {}
+        y_bank, y_sb = {}, {}
+        y_view = y.rearrange("(g p t) n -> g t p n", p=P, t=4)
 
-        def mm_y(i):
-            yps[i] = bank("y", PY)
+        def matmul_y(pair, i):
+            y_bank[pair, i] = take_bank()
             for g in range(NG):
-                rows = slice(g * P, (g + 1) * P)
+                rows = slice((2 * i + g) * P, (2 * i + g + 1) * P)
                 nc.tensor.matmul_mx(
-                    out=yps[i][:],
-                    lhsT=hq[i][:, rows].bitcast(FP8X4),
-                    lhsT_scale=hs[i][:, rows],
-                    rhs=jw[:, g, :].bitcast(FP4X4),
-                    rhs_scale=jsc[:, g, :],
+                    out=y_bank[pair, i][:],
+                    lhsT=ht_codes[pair][:, rows].bitcast(FP8X4),
+                    lhsT_scale=ht_scales[pair][:, rows],
+                    rhs=j_words[:, g, :].bitcast(FP4X4),
+                    rhs_scale=j_scales[:, g, :],
                     start=(g == 0),
                     stop=(g == NG - 1),
                 )
 
-        y_view = y.rearrange("(g p t) n -> g t p n", p=P, t=4)
+        def store_y(pair, i, engine):
+            y_sb[pair, i] = work.tile([P, R], F32, name="y_sb", tag="y_sb", bufs=6, align_bytes=64)
+            copy_on(engine, y_sb[pair, i][:], y_bank[pair, i][:])
+            nc.sync.dma_start(out=y_view[pair // 2, 2 * (pair % 2) + i], in_=y_sb[pair, i][:])
 
-        def evac_y(i, eng):
-            y_sb = work.tile([P, R], F32, name="y_sb", tag="y_sb", bufs=5, align_bytes=64)
-            if eng == "v":
-                nc.vector.tensor_copy(out=y_sb[:], in_=yps[i][:])
+        def sum_squares(pair, i, engine="scalar"):
+            squares = work.tile([P, R], BF16, name="squares", tag="squares", align_bytes=64)
+            total = lev_sb[:, 2 * (pair % 2) + i, pair // 2 : pair // 2 + 1]
+            rows = y_sb[pair, i][:]
+            if engine == "vector":
+                nc.vector.scalar_tensor_tensor(
+                    out=squares[:], in0=rows, scalar=1.0 / R, in1=rows, op0=MULT, op1=MULT, accum_out=total
+                )
             else:
-                nc.scalar.copy(out=y_sb[:], in_=yps[i][:])
-            nc.sync.dma_start(out=y_view[i // 4, i % 4], in_=y_sb[:])
+                nc.scalar.activation(out=squares[:], in_=rows, func=SQUARE, scale=R**-0.5, accum_out=total)
 
-        def lev_y(i):
-            sq = work.tile([P, R], BF16, name="sq", tag="sq", align_bytes=64)
-            nc.scalar.activation(
-                out=sq[:], in_=yps[i][:], func=SQUARE, scale=R**-0.5,
-                accum_out=lev_sb[:, i % 4, i // 4 : i // 4 + 1],
-            )
+        hc_grouped, hc_codes, hc_scales = {}, {}, {}
 
-        cg, cq, cs = {}, {}, {}
-
-        def interleave_c(gg, h):
-            cg[gg, h] = work.tile([P, 512, 4], BF16, name="cg", tag="cg", align_bytes=64)
+        def interleave_h(group, h):
+            hc_grouped[group, h] = work.tile([P, 512, 4], BF16, name="hc_grouped", tag="hc_grouped", align_bytes=64)
             nc.vector.tensor_copy(
-                out=cg[gg, h][:].rearrange("p (c i) t -> p c t i", i=4),
-                in_=hb[gg][:, :, 512 * h : 512 * (h + 1)].rearrange("p t (c i) -> p c t i", i=4),
+                out=hc_grouped[group, h][:].rearrange("p (c i) t -> p c t i", i=4),
+                in_=h_rows[group][:, :, 512 * h : 512 * (h + 1)].rearrange("p t (c i) -> p c t i", i=4),
             )
 
-        def quantize_c(gg, h):
-            cq[gg, h] = keep.tile([P, 512], U32, name=f"cq_{gg}{h}", align_bytes=64)
-            cs[gg, h] = keep.tile([P, 512], U8, name=f"cs_{gg}{h}", align_bytes=64)
-            nc.vector.quantize_mx(
-                out=cq[gg, h][:].bitcast(FP8X4), scales=cs[gg, h][:], in_=cg[gg, h][:].rearrange("p n t -> p (n t)")
+        def quantize_hc(group, h):
+            quantize(
+                hc_codes, hc_scales, (group, h), hc_grouped[group, h][:].rearrange("p n t -> p (n t)"), f"hc{group}{h}", keep
             )
 
-        btr = {}
-        bg = keep.tile([P, 6, P, 4], BF16, name="bg", align_bytes=64)
-        bq = keep.tile([P, 6 * P], U32, name="bq", align_bytes=64)
-        bs = keep.tile([P, 6 * P], U8, name="bs", align_bytes=64)
+        b_grouped = keep.tile([P, GROUPS * 512], BF16, name="b_grouped", align_bytes=64)
+        b_codes = keep.tile([P, GROUPS * P], U32, name="b_codes", align_bytes=64)
+        b_scales = keep.tile([P, GROUPS * P], U8, name="b_scales", align_bytes=64)
+        b_bank = {}
 
         def transpose_b(j):
-            btr[j] = bank("tr", PTR)
+            b_bank[j] = take_bank()
             words = b_sb[:].bitcast(F32)
             for s in range(4):
-                g, u = 2 * j + s // 2, s % 2
-                nc.tensor.transpose(btr[j][:, s * P : (s + 1) * P], words[:, 256 * g + u : 256 * (g + 1) : 2], ident[:])
+                group, u = 2 * j + s // 2, s % 2
+                nc.tensor.transpose(
+                    b_bank[j][:, s * P : (s + 1) * P], words[:, 256 * group + u : 256 * (group + 1) : 2], ident[:]
+                )
 
-        def evac_b(j, eng):
-            out = bg[:, 2 * j : 2 * j + 2].rearrange("p g r t -> p (g r t)").bitcast(F32).rearrange(
-                "p (g r u) -> p g r u", g=2, u=2
-            )
-            in_ = btr[j][:].rearrange("p (g u r) -> p g r u", g=2, u=2)
-            if eng == "v":
-                nc.vector.tensor_copy(out=out, in_=in_)
-            else:
-                nc.scalar.copy(out=out, in_=in_)
-
-        def quantize_b(j):
-            cols = slice(256 * j, 256 * (j + 1))
+        def quantize_b(half):
+            cols = slice(384 * half, 384 * (half + 1))
             nc.vector.quantize_mx(
-                out=bq[:, cols].bitcast(FP8X4), scales=bs[:, cols],
-                in_=bg[:, 2 * j : 2 * j + 2].rearrange("p g r t -> p (g r t)"),
+                out=b_codes[:, cols].bitcast(FP8X4),
+                scales=b_scales[:, cols],
+                in_=b_grouped[:, 1536 * half : 1536 * (half + 1)],
             )
 
-        cps = {}
+        c_bank = {}
 
-        def mm_c(gg, h):
-            if gg == 0:
-                cps[h] = bank("h", PH)
-            rows = slice(gg * P, (gg + 1) * P)
+        def matmul_c(group, h):
+            if group == 0:
+                c_bank[h] = take_bank(hold=True)
+            rows = slice(group * P, (group + 1) * P)
             nc.tensor.matmul_mx(
-                out=cps[h][:],
-                lhsT=bq[:, rows].bitcast(FP8X4),
-                lhsT_scale=bs[:, rows],
-                rhs=cq[gg, h][:].bitcast(FP8X4),
-                rhs_scale=cs[gg, h][:],
-                start=(gg == 0),
-                stop=(gg == GROUPS - 1),
+                out=c_bank[h][:],
+                lhsT=b_codes[:, rows].bitcast(FP8X4),
+                lhsT_scale=b_scales[:, rows],
+                rhs=hc_codes[group, h][:].bitcast(FP8X4),
+                rhs_scale=hc_scales[group, h][:],
+                start=(group == 0),
+                stop=(group == GROUPS - 1),
             )
 
-        def evac_c(h, eng):
+        def store_c(h, engine):
             c_sb = work.tile([P, 512], F32, name="c_sb", tag="c_sb", align_bytes=64)
-            out = c_sb[:].rearrange("p (q u e) -> p q u e", u=2, e=2)
-            in_ = cps[h][:].rearrange("p (u q e) -> p q u e", u=2, e=2)
-            if eng == "v":
-                nc.vector.tensor_copy(out=out, in_=in_)
-            else:
-                nc.scalar.copy(out=out, in_=in_)
+            copy_on(
+                engine,
+                c_sb[:].rearrange("p (q u e) -> p q u e", u=2, e=2),
+                c_bank[h][:].rearrange("p (u q e) -> p q u e", u=2, e=2),
+            )
             nc.sync.dma_start(out=c[:, 512 * h : 512 * (h + 1)], in_=c_sb[:])
 
-        def eng(rule, i):
-            pattern, head, tail = rule
-            return "s" if i < head else "v" if i >= tail else pattern[i % len(pattern)]
-
-        for half in range(2 if MODE == 1 else 0):
-            sps = bank("tr", PTR)
-            for j in range(4):
-                c0 = 4 * half + j
-                nc.tensor.transpose(sps[:, j * P : (j + 1) * P], scale_v[:, c0 : c0 + 1].to_broadcast([P, P]), ident[:])
-            for i in range(2):
-                out = scale_sb[:, K * i : K * (i + 1)].rearrange("p (k c) -> p k c", c=8)[:, :, 4 * half : 4 * half + 4]
-                in_ = sps[:].rearrange("p (c k) -> p k c", c=4)
-                if X_SC[half] == "v":
-                    nc.vector.tensor_copy(out=out, in_=in_)
-                else:
-                    nc.scalar.copy(out=out, in_=in_)
-        done = set()
-        qdone = set()
-
-        def run(tok, pair):
-            d = ""
-            for j, ch in enumerate(tok):
-                if ch in "01":
-                    k, d = tok[:j], tok[j:]
-                    break
-            else:
-                k = tok
-            i = 2 * pair + int(d[0]) if d else 0
-            if k == "P":
-                if MODE == 1:
-                    product(pair)
-            elif k == "MS":
-                if MODE == 2:
-                    claim(pair)
-            elif k == "W":
-                if MODE == 2:
-                    widen(pair, int(d))
-            elif k == "TA":
-                transpose_a(pair, int(d))
-            elif k == "EA":
-                evac_a(pair, int(d))
-            elif k == "QA":
-                quantize_a(pair)
-            elif k == "M":
-                mm_h(i, int(d[1]))
-            elif k == "F":
-                h = int(d[1])
-                evac_h(i, h, eng(X_EE, 2 * i + h))
-                done.add((i, h))
-            elif k == "TH":
-                assert (i, 0) in done and (i, 1) in done
-                transpose_h(i)
-            elif k == "EH":
-                evac_ht(i, eng(X_EH, i))
-            elif k == "QH":
-                quantize_ht(pair)
-            elif k == "Y":
-                mm_y(i)
-            elif k == "EY":
-                evac_y(i, eng(X_EY, i))
-            elif k == "LV":
-                lev_y(i)
-            elif pair % 2 == 1:
-                h = int(d)
-                for j in range(4):
-                    assert (2 * pair + 1 - j, h) in done
-                (interleave_c if k == "IC" else quantize_c)(pair // 2, h)
-                if k == "QC":
-                    qdone.add((pair // 2, h))
-
-        cdone = 0
-        bdone = set()
-        for s in range(-3, TILES // 2 + 9):
-            for tok, lag, per in ORDER:
-                if tok == "R":
-                    for x in [x for x in RINV if x[0] == s]:
-                        if x[1] == "I":
-                            interleave_rinv(x[2], x[3], x[4], x[5])
-                        else:
-                            quantize_rinv(x[2], x[3])
-                elif tok == "B":
-                    if 0 <= s - BSTART < 3:
-                        transpose_b(s - BSTART)
-                        evac_b(s - BSTART, BENG)
-                elif tok == "BQ":
-                    if 0 <= s - BSTART - lag < 3:
-                        quantize_b(s - BSTART - lag)
-                        bdone.add(s - BSTART - lag)
-                elif 0 <= s - lag < TILES // 2:
-                    run(tok, s - lag)
-            while s >= CSTART and cdone < GROUPS and {(cdone, 0), (cdone, 1)} <= qdone and cdone // 2 in bdone:
-                for h in range(2):
-                    mm_c(cdone, h)
-                    if cdone == GROUPS - 1:
-                        evac_c(h, CENG[h])
-                cdone += 1
-        assert cdone == GROUPS
-
-        lev_rows = keep.tile([P, 512], F32, name="lev_rows", align_bytes=64)
-        for t0 in (0, 2):
-            lps = bank("tr", PTR)
-            for j in range(2):
-                nc.tensor.transpose(lps[:, j * P : (j + 1) * P], lev_sb[:, t0 + j, :], ident[:])
-            nc.vector.tensor_copy(
-                out=lev_rows[:GROUPS, :].rearrange("g (p t) -> g p t", t=4)[:, :, t0 : t0 + 2],
-                in_=lps[:GROUPS, : 2 * P].rearrange("g (t p) -> g p t", t=2),
+        def store_lev():
+            lev_turned = keep.tile([P, 4, 32], F32, name="lev_turned", align_bytes=64)
+            nc.vector.transpose(
+                out=lev_turned[:].rearrange("p t j -> p (t j)"), in_=lev_sb[:].rearrange("p t g -> p (t g)")
             )
-        nc.sync.dma_start(out=lev.rearrange("(g m) -> g m", g=GROUPS), in_=lev_rows[:GROUPS, :])
+            lev_rows = keep.tile([P, 32, 4], F32, name="lev_rows", align_bytes=64)
+            nc.vector.tensor_copy(out=lev_rows[:], in_=lev_turned[:].rearrange("p t j -> p j t"))
+            for group in range(GROUPS):
+                queue = nc.sync if group % 2 == 0 else nc.scalar
+                queue.dma_start(
+                    out=lev[512 * group : 512 * (group + 1)].rearrange("(q m) -> q m", q=4),
+                    in_=lev_rows[group:P:32].rearrange("p j t -> p (j t)"),
+                )
+
+        def live(pair):
+            return 0 <= pair < PAIRS
+
+        def product_h(pair, h, engines):
+            for i in range(2):
+                matmul_h(pair, i, h)
+                weigh_h(pair, i, h, engines[i])
+
+        def turn_a(pair):
+            transpose_a(pair)
+            scale_a(pair, 0)
+            if live(pair + 1):
+                widen(pair + 1, nc.gpsimd)
+            scale_a(pair, 1)
+
+        def turn_h(pair, engines):
+            transpose_h(pair)
+            for i in range(2):
+                copy_ht(pair, i, engines[i])
+
+        def turn_b(j):
+            transpose_b(j)
+            copy_words("scalar", b_grouped[:, 1024 * j : 1024 * (j + 1)], b_bank[j])
+
+        def product_y(pair, engines):
+            for i in range(2):
+                matmul_y(pair, i)
+                store_y(pair, i, engines[i])
+
+        def product_c(groups):
+            for group in groups:
+                for h in range(NG):
+                    matmul_c(group, h)
+
+        alone, shared = ("scalar", "scalar"), ("scalar", "vector")
+
+        widen(0, nc.vector)
+        interleave_rinv(0, 0, 0, "scalar")
+        interleave_rinv(0, 0, 1, "vector")
+        turn_a(0)
+        for h, g, u in ((0, 1, 0), (0, 1, 1), (1, 0, 0), (1, 0, 1), (1, 1, 0)):
+            interleave_rinv(h, g, u, "scalar")
+        quantize_rinv(0, 0)
+        quantize_a(0)
+        quantize_rinv(0, 1)
+        turn_a(1)
+        product_h(0, 0, shared[::-1])
+        turn_b(0)
+        turn_b(1)
+        quantize_rinv(1, 0)
+        interleave_rinv(1, 1, 1, "vector")
+        quantize_a(1)
+        quantize_rinv(1, 1)
+        turn_a(2)
+        product_h(1, 0, alone)
+        product_h(0, 1, shared[::-1])
+        quantize_a(2)
+        product_h(1, 1, alone)
+        turn_h(0, alone)
+        turn_b(2)
+
+        for step in range(2, PAIRS - 1):
+            turn_a(step + 1)
+            product_h(step, 0, alone)
+            if step > 2:
+                sum_squares(step - 3, 1)
+            turn_h(step - 1, alone)
+            quantize_ht(step - 2)
+            if step > 2:
+                quantize_hc((step - 3) // 2, (step - 3) % 2)
+            if step < 4:
+                quantize_b(step - 2)
+            quantize_a(step + 1)
+            interleave_h((step - 2) // 2, step % 2)
+            product_h(step, 1, alone)
+            product_y(step - 2, alone)
+            sum_squares(step - 2, 0)
+
+        end, final = PAIRS - 1, GROUPS - 1
+        quantize_ht(end - 2)
+        quantize_hc(final - 1, 0)
+        interleave_h(final - 1, 1)
+        product_h(end, 0, alone)
+        sum_squares(end - 3, 1)
+        turn_h(end - 1, alone)
+        interleave_h(final, 0)
+        quantize_hc(final - 1, 1)
+        quantize_ht(end - 1)
+        product_h(end, 1, alone)
+        for i in range(2):
+            matmul_y(end - 2, i)
+        product_c(range(3))
+        turn_h(end, alone)
+        interleave_h(final, 1)
+        quantize_ht(end)
+        for i in range(2):
+            store_y(end - 2, i, "scalar")
+        product_y(end - 1, alone)
+        for h in range(NG):
+            quantize_hc(final, h)
+        product_c(range(3, 4))
+        for i in range(2):
+            matmul_y(end, i)
+        product_c(range(4, GROUPS))
+        for i in range(2):
+            store_y(end, i, "vector")
+        for pair in (end - 2, end - 1):
+            for i in range(2):
+                sum_squares(pair, i)
+        sum_squares(end, 0)
+        for h in range(NG):
+            store_c(h, "vector")
+        sum_squares(end, 1, "vector")
+        store_lev()

@@ -370,19 +370,18 @@ def tile_weighted_leverage_sketch_s8_kernel(
         quantize_rinv(0, 1)
         turn_a(1)
         product_h(0, 0, shared[::-1])
-        turn_b(0)
-        turn_b(1)
-        quantize_rinv(1, 0)
-        interleave_rinv(1, 1, 1, "vector")
+        for j in range(3):
+            turn_b(j)
         quantize_a(1)
+        interleave_rinv(1, 1, 1, "vector")
+        quantize_rinv(1, 0)
         quantize_rinv(1, 1)
-        turn_a(2)
         product_h(1, 0, alone)
-        product_h(0, 1, shared[::-1])
+        turn_a(2)
+        product_h(0, 1, alone)
+        product_h(1, 1, shared[::-1])
         quantize_a(2)
-        product_h(1, 1, alone)
         turn_h(0, alone)
-        turn_b(2)
 
         for step in range(2, PAIRS - 1):
             turn_a(step + 1)

@@ -81,15 +81,21 @@ def tile_weighted_leverage_sketch_s8_kernel(
             nc.sync.dma_start(out=r_raw[h, g][:], in_=rinv_view[g, :, :, 512 * h : 512 * (h + 1)])
 
         j_words = keep.tile([P, NG, 2 * R], U8, name="j_words", align_bytes=64)
-        b_sb = keep.tile([P, M], BF16, name="b_sb", align_bytes=64)
+        b_sb = {}
+
+        def load_b(j):
+            b_sb[j] = keep.tile([P, 1024], BF16, name=f"b_sb_{j}", align_bytes=64)
+            nc.sync.dma_start(out=b_sb[j][:], in_=b[:, 1024 * j : 1024 * (j + 1)])
 
         for g in range(KG):
             load_a(g)
             load_rinv(0, g)
-        for g in range(KG):
-            load_rinv(1, g)
+        load_b(0)
+        load_b(1)
+        load_rinv(1, 0)
         load_a(2)
-        nc.sync.dma_start(out=b_sb[:], in_=b)
+        load_rinv(1, 1)
+        load_b(2)
         load_a(3)
         nc.sync.dma_start(out=j_words[:], in_=jl_words.rearrange("g p n -> p g n"))
         for q in range(4):
@@ -109,7 +115,7 @@ def tile_weighted_leverage_sketch_s8_kernel(
 
         def interleave_rinv(h, g, u, engine):
             if (h, g) not in r_grouped:
-                r_grouped[h, g] = keep.tile([P, 512, 4], BF16, name=f"r_grouped_{h}{g}", align_bytes=64)
+                r_grouped[h, g] = work.tile([P, 512, 4], BF16, name="r_grouped", tag="hc_grouped" if h == 0 else "ht_grouped", align_bytes=64)
             copy_on(
                 engine,
                 r_grouped[h, g][:].rearrange("p (u q e) t -> p u q t e", u=2, e=2)[:, u],
@@ -144,8 +150,8 @@ def tile_weighted_leverage_sketch_s8_kernel(
                         )
 
         def scale_a(pair, g):
-            if g == 0:
-                a_grouped[pair] = work.tile([P, 2 * K], BF16, name="a_grouped", tag="a_ring", align_bytes=64)
+            if pair not in a_grouped:
+                a_grouped[pair] = work.tile([P, 2 * K], BF16, name="a_grouped", tag="a_ring", align_bytes=64)[:]
             nc.vector.tensor_tensor(
                 out=a_grouped[pair][:, K * g : K * (g + 1)].rearrange("p (c u e) -> p c u e", u=2, e=2),
                 in0=a_bank[pair, g][:].bitcast(BF16).rearrange("p (u c e) -> p c u e", u=2, e=2),
@@ -153,13 +159,15 @@ def tile_weighted_leverage_sketch_s8_kernel(
                 op=MULT,
             )
 
-        def quantize(codes, scales, key, grouped, name, pool=work):
-            codes[key] = pool.tile([P, 512], U32, name=name + "_codes", tag=name + "_codes", align_bytes=64)
-            scales[key] = pool.tile([P, 512], U8, name=name + "_scales", tag=name + "_scales", align_bytes=64)
-            nc.vector.quantize_mx(out=codes[key][:].bitcast(FP8X4), scales=scales[key][:], in_=grouped)
+        def quantize(grouped, name, pool):
+            width = grouped.shape[1] // 4
+            codes = pool.tile([P, width], U32, name=name + "_codes", tag=name + "_codes", align_bytes=64)
+            scales = pool.tile([P, width], U8, name=name + "_scales", tag=name + "_scales", align_bytes=64)
+            nc.vector.quantize_mx(out=codes[:].bitcast(FP8X4), scales=scales[:], in_=grouped)
+            return codes, scales
 
         def quantize_a(pair):
-            quantize(a_codes, a_scales, pair, a_grouped[pair][:], "a")
+            a_codes[pair], a_scales[pair] = quantize(a_grouped[pair], "a", work)
 
         h_bank, h_rows = {}, {}
 
@@ -213,7 +221,7 @@ def tile_weighted_leverage_sketch_s8_kernel(
             copy_words(engine, ht_grouped[pair][:, N * i : N * (i + 1)], ht_bank[pair, i])
 
         def quantize_ht(pair):
-            quantize(ht_codes, ht_scales, pair, ht_grouped[pair][:], "ht")
+            ht_codes[pair], ht_scales[pair] = quantize(ht_grouped[pair][:], "ht", work)
 
         y_bank, y_sb = {}, {}
         y_view = y.rearrange("(g p t) n -> g t p n", p=P, t=4)
@@ -237,10 +245,10 @@ def tile_weighted_leverage_sketch_s8_kernel(
             copy_on(engine, y_sb[pair, i][:], y_bank[pair, i][:])
             nc.sync.dma_start(out=y_view[pair // 2, 2 * (pair % 2) + i], in_=y_sb[pair, i][:])
 
-        def sum_squares(pair, i, engine="scalar"):
-            squares = work.tile([P, R], BF16, name="squares", tag="squares", align_bytes=64)
+        def sum_squares(pair, i, engine="scalar", source=y_sb):
+            squares = work.tile([P, R], BF16, name="squares", tag="squares", bufs=2, align_bytes=64)
             total = lev_sb[:, 2 * (pair % 2) + i, pair // 2 : pair // 2 + 1]
-            rows = y_sb[pair, i][:]
+            rows = source[pair, i][:]
             if engine == "vector":
                 nc.vector.scalar_tensor_tensor(
                     out=squares[:], in0=rows, scalar=1.0 / R, in1=rows, op0=MULT, op1=MULT, accum_out=total
@@ -250,17 +258,28 @@ def tile_weighted_leverage_sketch_s8_kernel(
 
         hc_grouped, hc_codes, hc_scales = {}, {}, {}
 
-        def interleave_h(group, h):
-            hc_grouped[group, h] = work.tile([P, 512, 4], BF16, name="hc_grouped", tag="hc_grouped", align_bytes=64)
-            nc.vector.tensor_copy(
-                out=hc_grouped[group, h][:].rearrange("p (c i) t -> p c t i", i=4),
-                in_=h_rows[group][:, :, 512 * h : 512 * (h + 1)].rearrange("p t (c i) -> p c t i", i=4),
-            )
+        joint = {}
+
+        def interleave_h(group, h, partner=None):
+            if partner is None:
+                tile = work.tile([P, 2048], BF16, name="hc_grouped", tag="hc_grouped", align_bytes=64)
+                hc_grouped[group, h] = tile[:]
+            else:
+                joint[partner] = work.tile([P, 4096], BF16, name="joint", tag="a_ring", align_bytes=64)
+                a_grouped[partner], hc_grouped[group, h] = joint[partner][:, :2048], joint[partner][:, 2048:]
+            out = hc_grouped[group, h].rearrange("p (c i t) -> p c t i", i=4, t=4)
+            in_ = h_rows[group][:, :, 512 * h : 512 * (h + 1)].rearrange("p t (c i) -> p c t i", i=4)
+            nc.vector.tensor_copy(out=out, in_=in_)
 
         def quantize_hc(group, h):
-            quantize(
-                hc_codes, hc_scales, (group, h), hc_grouped[group, h][:].rearrange("p n t -> p (n t)"), f"hc{group}{h}", keep
+            hc_codes[group, h], hc_scales[group, h] = (
+                tile[:] for tile in quantize(hc_grouped[group, h], f"hc{group}{h}", keep)
             )
+
+        def quantize_joint(pair, group, h):
+            codes, scales = quantize(joint[pair][:], f"joint{pair}", keep)
+            a_codes[pair], a_scales[pair] = codes[:, :512], scales[:, :512]
+            hc_codes[group, h], hc_scales[group, h] = codes[:, 512:], scales[:, 512:]
 
         b_grouped = keep.tile([P, GROUPS * 512], BF16, name="b_grouped", align_bytes=64)
         b_codes = keep.tile([P, GROUPS * P], U32, name="b_codes", align_bytes=64)
@@ -269,9 +288,9 @@ def tile_weighted_leverage_sketch_s8_kernel(
 
         def transpose_b(j):
             b_bank[j] = take_bank()
-            words = b_sb[:].bitcast(F32)
+            words = b_sb[j][:].bitcast(F32)
             for s in range(4):
-                group, u = 2 * j + s // 2, s % 2
+                group, u = s // 2, s % 2
                 nc.tensor.transpose(
                     b_bank[j][:, s * P : (s + 1) * P], words[:, 256 * group + u : 256 * (group + 1) : 2], ident[:]
                 )
@@ -294,14 +313,14 @@ def tile_weighted_leverage_sketch_s8_kernel(
                 out=c_bank[h][:],
                 lhsT=b_codes[:, rows].bitcast(FP8X4),
                 lhsT_scale=b_scales[:, rows],
-                rhs=hc_codes[group, h][:].bitcast(FP8X4),
-                rhs_scale=hc_scales[group, h][:],
+                rhs=hc_codes[group, h].bitcast(FP8X4),
+                rhs_scale=hc_scales[group, h],
                 start=(group == 0),
                 stop=(group == GROUPS - 1),
             )
 
         def store_c(h, engine):
-            c_sb = work.tile([P, 512], F32, name="c_sb", tag="c_sb", align_bytes=64)
+            c_sb = work.tile([P, 512], F32, name="c_sb", tag="y_sb", bufs=6, align_bytes=64)
             copy_on(
                 engine,
                 c_sb[:].rearrange("p (q u e) -> p q u e", u=2, e=2),
@@ -365,21 +384,23 @@ def tile_weighted_leverage_sketch_s8_kernel(
         turn_a(0)
         for h, g, u in ((0, 1, 0), (0, 1, 1), (1, 0, 0), (1, 0, 1), (1, 1, 0)):
             interleave_rinv(h, g, u, "scalar")
+        for j in range(2):
+            turn_b(j)
         quantize_rinv(0, 0)
         quantize_a(0)
         quantize_rinv(0, 1)
         turn_a(1)
-        product_h(0, 0, shared[::-1])
-        for j in range(3):
-            turn_b(j)
+        product_h(0, 0, alone)
+        turn_b(2)
         quantize_a(1)
         interleave_rinv(1, 1, 1, "vector")
         quantize_rinv(1, 0)
         quantize_rinv(1, 1)
-        product_h(1, 0, alone)
         turn_a(2)
+        product_h(1, 0, alone)
         product_h(0, 1, alone)
-        product_h(1, 1, shared[::-1])
+        product_h(1, 1, alone)
+        quantize_b(0)
         quantize_a(2)
         turn_h(0, alone)
 
@@ -391,48 +412,46 @@ def tile_weighted_leverage_sketch_s8_kernel(
             turn_h(step - 1, alone)
             quantize_ht(step - 2)
             if step > 2:
-                quantize_hc((step - 3) // 2, (step - 3) % 2)
-            if step < 4:
-                quantize_b(step - 2)
-            quantize_a(step + 1)
-            interleave_h((step - 2) // 2, step % 2)
+                quantize_joint(step + 1, (step - 3) // 2, (step - 3) % 2)
+            else:
+                quantize_b(1)
+                quantize_a(step + 1)
+            interleave_h((step - 2) // 2, step % 2, partner=step + 2 if live(step + 2) else None)
             product_h(step, 1, alone)
+            if step >= 4:
+                matmul_c((step - 4) // 2, step % 2)
             product_y(step - 2, alone)
             sum_squares(step - 2, 0)
 
         end, final = PAIRS - 1, GROUPS - 1
         quantize_ht(end - 2)
+        product_h(end, 0, shared)
         quantize_hc(final - 1, 0)
         interleave_h(final - 1, 1)
-        product_h(end, 0, alone)
-        sum_squares(end - 3, 1)
         turn_h(end - 1, alone)
-        interleave_h(final, 0)
-        quantize_hc(final - 1, 1)
-        quantize_ht(end - 1)
         product_h(end, 1, alone)
-        for i in range(2):
-            matmul_y(end - 2, i)
-        product_c(range(3))
+        interleave_h(final, 0)
+        quantize_ht(end - 1)
+        matmul_c(3, 1)
+        product_y(end - 2, alone)
         turn_h(end, alone)
         interleave_h(final, 1)
         quantize_ht(end)
-        for i in range(2):
-            store_y(end - 2, i, "scalar")
+        quantize_hc(final - 1, 1)
+        sum_squares(end - 3, 1)
         product_y(end - 1, alone)
         for h in range(NG):
             quantize_hc(final, h)
-        product_c(range(3, 4))
         for i in range(2):
             matmul_y(end, i)
-        product_c(range(4, GROUPS))
+        product_c(range(final - 1, GROUPS))
         for i in range(2):
-            store_y(end, i, "vector")
-        for pair in (end - 2, end - 1):
-            for i in range(2):
-                sum_squares(pair, i)
-        sum_squares(end, 0)
+            sum_squares(end - 2, i)
+        for i in range(2):
+            store_y(end, i, "scalar")
         for h in range(NG):
             store_c(h, "vector")
-        sum_squares(end, 1, "vector")
+        for pair in (end - 1, end):
+            for i in range(2):
+                sum_squares(pair, i, "vector" if (pair, i) == (end, 1) else "scalar")
         store_lev()

@@ -406,10 +406,10 @@ def tile_weighted_leverage_sketch_s8_kernel(
 
         for step in range(2, PAIRS - 1):
             turn_a(step + 1)
+            turn_h(step - 1, alone)
             product_h(step, 0, alone)
             if step > 2:
                 sum_squares(step - 3, 1)
-            turn_h(step - 1, alone)
             quantize_ht(step - 2)
             if step > 2:
                 quantize_joint(step + 1, (step - 3) // 2, (step - 3) % 2)

@@ -38,12 +38,12 @@ def tile_weighted_leverage_sketch_s8_kernel(
 
         ring = list(range(BANKS))
 
-        def take_bank(hold=False):
+        def take_bank(hold=False, dtype=F32):
             number = ring[0]
             ring.remove(number)
             if not hold:
                 ring.append(number)
-            return psum.tile([P, 512], F32, name=f"bank{number}", tag=f"bank{number}")
+            return psum.tile([P, 512 if dtype is F32 else 1024], dtype, name=f"bank{number}", tag=f"bank{number}")
 
         def copy_on(engine, out, in_):
             if engine == "vector":
@@ -51,9 +51,9 @@ def tile_weighted_leverage_sketch_s8_kernel(
             else:
                 nc.scalar.copy(out=out, in_=in_)
 
-        scale_p = keep.tile([P, KG, 2, 2], F32, name="scale_p", align_bytes=64)
+        scale_p = keep.tile([P, KG, 4], F32, name="scale_p", align_bytes=64)
         nc.scalar.dma_start(
-            out=scale_p[:].rearrange("p g u e -> p g (u e)"),
+            out=scale_p[:],
             in_=a_scale.rearrange("o (g p t) -> p (o g) t", p=P, t=4),
         )
         w_bf = keep.tile([P, GROUPS, 4], BF16, name="w_bf", align_bytes=64)
@@ -66,6 +66,9 @@ def tile_weighted_leverage_sketch_s8_kernel(
         nc.vector.memset(j_scales_i32, 0)
         lev_sb = keep.tile([P, 4, 32], F32, name="lev_sb", align_bytes=64)
         nc.vector.memset(lev_sb[:], 0.0)
+
+        ident_bf = keep.tile([P, P], BF16, name="ident_bf", align_bytes=64)
+        nc.vector.tensor_copy(out=ident_bf[:], in_=ident[:])
 
         a_view = a_bytes.rearrange("(g p t) k -> g p t k", p=P, t=4)
         rinv_view = rinv.rearrange("(g p t) n -> g p t n", p=P, t=4)
@@ -137,25 +140,27 @@ def tile_weighted_leverage_sketch_s8_kernel(
             engine.tensor_copy(out=a_wide[pair][:], in_=a8[pair][:].rearrange("p i k -> p (i k)").bitcast(FP8))
 
         def transpose_a(pair):
-            words = a_wide[pair][:].bitcast(F32).rearrange("p (i k) -> p i k", i=2)
+            rows = a_wide[pair][:].rearrange("p (i k) -> p i k", i=2)
             for g in range(KG):
-                a_bank[pair, g] = take_bank()
-                for u in range(2):
+                a_bank[pair, g] = take_bank(dtype=BF16)
+                for t in range(4):
                     for i in range(2):
-                        s = 2 * u + i
-                        nc.tensor.transpose(
-                            a_bank[pair, g][:, s * P : (s + 1) * P],
-                            words[:, i, 256 * g + u : 256 * (g + 1) : 2],
-                            ident[:],
+                        s = 2 * t + i
+                        nc.tensor.matmul(
+                            out=a_bank[pair, g][:, s * P : (s + 1) * P],
+                            lhsT=rows[:, i, 512 * g + t : 512 * (g + 1) : 4],
+                            rhs=ident_bf[:],
+                            start=True,
+                            stop=True,
                         )
 
         def scale_a(pair, g):
             if pair not in a_grouped:
                 a_grouped[pair] = work.tile([P, 2 * K], BF16, name="a_grouped", tag="a_ring", align_bytes=64)[:]
             nc.vector.tensor_tensor(
-                out=a_grouped[pair][:, K * g : K * (g + 1)].rearrange("p (c u e) -> p c u e", u=2, e=2),
-                in0=a_bank[pair, g][:].bitcast(BF16).rearrange("p (u c e) -> p c u e", u=2, e=2),
-                in1=scale_p[:, g].unsqueeze(1).to_broadcast([P, 2 * P, 2, 2]),
+                out=a_grouped[pair][:, K * g : K * (g + 1)].rearrange("p (c t) -> p c t", t=4),
+                in0=a_bank[pair, g][:].rearrange("p (t c) -> p c t", t=4),
+                in1=scale_p[:, g].unsqueeze(1).to_broadcast([P, 2 * P, 4]),
                 op=MULT,
             )
 
@@ -188,9 +193,9 @@ def tile_weighted_leverage_sketch_s8_kernel(
 
         def weigh_h(pair, i, h, engine):
             group, t = pair // 2, 2 * (pair % 2) + i
-            if group not in h_rows:
-                h_rows[group] = work.tile([P, 4, N], BF16, name="h_rows", tag="h_rows", align_bytes=64)
-            out = h_rows[group][:, t, 512 * h : 512 * (h + 1)]
+            if (group, h) not in h_rows:
+                h_rows[group, h] = work.tile([P, 4, 512], BF16, name="h_rows", tag="h_rows", bufs=6, align_bytes=64)
+            out = h_rows[group, h][:, t, :]
             weight = w_sb[:, 4 * group + t : 4 * group + t + 1]
             if engine == "vector":
                 nc.vector.tensor_scalar(out=out, in0=h_bank[pair, i, h][:], scalar1=weight, scalar2=None, op0=MULT)
@@ -202,10 +207,11 @@ def tile_weighted_leverage_sketch_s8_kernel(
         def transpose_h(pair):
             for i in range(2):
                 ht_bank[pair, i] = take_bank()
-                words = h_rows[pair // 2][:, 2 * (pair % 2) + i, :].bitcast(F32)
                 for s in range(4):
+                    h, u = s // 2, s % 2
+                    words = h_rows[pair // 2, h][:, 2 * (pair % 2) + i, :].bitcast(F32)
                     nc.tensor.transpose(
-                        ht_bank[pair, i][:, s * P : (s + 1) * P], words[:, s * P : (s + 1) * P], ident[:]
+                        ht_bank[pair, i][:, s * P : (s + 1) * P], words[:, u * P : (u + 1) * P], ident[:]
                     )
 
         def copy_words(engine, grouped, bank):
@@ -268,7 +274,7 @@ def tile_weighted_leverage_sketch_s8_kernel(
                 joint[partner] = work.tile([P, 4096], BF16, name="joint", tag="a_ring", align_bytes=64)
                 a_grouped[partner], hc_grouped[group, h] = joint[partner][:, :2048], joint[partner][:, 2048:]
             out = hc_grouped[group, h].rearrange("p (c i t) -> p c t i", i=4, t=4)
-            in_ = h_rows[group][:, :, 512 * h : 512 * (h + 1)].rearrange("p t (c i) -> p c t i", i=4)
+            in_ = h_rows[group, h][:].rearrange("p t (c i) -> p c t i", i=4)
             nc.vector.tensor_copy(out=out, in_=in_)
 
         def quantize_hc(group, h):

@@ -24,6 +24,7 @@ PAIRS = M // (2 * P)
 KG = K // 512
 NG = N // 512
 BANKS = 8
+GPSIMD_COLUMNS = 1792
 
 
 def tile_weighted_leverage_sketch_s8_kernel(
@@ -137,7 +138,11 @@ def tile_weighted_leverage_sketch_s8_kernel(
 
         def widen(pair, engine):
             a_wide[pair] = work.tile([P, 2 * K], BF16, name="a_wide", tag="a_ring", align_bytes=64)
-            engine.tensor_copy(out=a_wide[pair][:], in_=a8[pair][:].rearrange("p i k -> p (i k)").bitcast(FP8))
+            widen_part(pair, slice(0, 2 * K if pair < 4 else GPSIMD_COLUMNS), engine)
+
+        def widen_part(pair, cols, engine):
+            codes = a8[pair][:].rearrange("p i k -> p (i k)")
+            engine.tensor_copy(out=a_wide[pair][:, cols], in_=codes[:, cols].bitcast(FP8))
 
         def transpose_a(pair):
             rows = a_wide[pair][:].rearrange("p (i k) -> p i k", i=2)
@@ -417,6 +422,8 @@ def tile_weighted_leverage_sketch_s8_kernel(
             if step > 2:
                 sum_squares(step - 3, 1)
             quantize_ht(step - 2)
+            if live(step + 2):
+                widen_part(step + 2, slice(GPSIMD_COLUMNS, 2 * K), nc.vector)
             if step > 2:
                 quantize_joint(step + 1, (step - 3) // 2, (step - 3) % 2)
             else:

@@ -231,6 +231,19 @@ def tile_weighted_leverage_sketch_s8_kernel(
                 ht_grouped[pair] = work.tile([P, 2 * N], BF16, name="ht_grouped", tag="ht_grouped", align_bytes=64)
             copy_words(engine, ht_grouped[pair][:, N * i : N * (i + 1)], ht_bank[pair, i])
 
+        def turn_h_half(pair, h, engine):
+            bank = take_bank()
+            for i in range(2):
+                words = h_rows[pair // 2, h][:, 2 * (pair % 2) + i, :].bitcast(F32)
+                for u in range(2):
+                    s = 2 * i + u
+                    nc.tensor.transpose(bank[:, s * P : (s + 1) * P], words[:, u * P : (u + 1) * P], ident[:])
+            ht_grouped[pair, h] = work.tile([P, N], BF16, name="ht_half", tag="ht_grouped", align_bytes=64)
+            copy_words(engine, ht_grouped[pair, h][:], bank)
+
+        def quantize_ht_half(pair, h):
+            ht_codes[pair, h], ht_scales[pair, h] = quantize(ht_grouped[pair, h][:], "ht", work)
+
         def quantize_ht(pair):
             ht_codes[pair], ht_scales[pair] = quantize(ht_grouped[pair][:], "ht", work)
 
@@ -250,6 +263,20 @@ def tile_weighted_leverage_sketch_s8_kernel(
                     start=(g == 0),
                     stop=(g == NG - 1),
                 )
+
+        def matmul_y_half(pair, i, h):
+            if h == 0:
+                y_bank[pair, i] = take_bank(hold=True)
+            rows = slice(i * P, (i + 1) * P)
+            nc.tensor.matmul_mx(
+                out=y_bank[pair, i][:],
+                lhsT=ht_codes[pair, h][:, rows].bitcast(FP8X4),
+                lhsT_scale=ht_scales[pair, h][:, rows],
+                rhs=j_words[:, h, :].bitcast(FP4X4),
+                rhs_scale=j_scales[:, h, :],
+                start=(h == 0),
+                stop=(h == NG - 1),
+            )
 
         def store_y(pair, i, engine):
             y_sb[pair, i] = work.tile([P, R], F32, name="y_sb", tag="y_sb", bufs=6, align_bytes=64)
@@ -339,11 +366,14 @@ def tile_weighted_leverage_sketch_s8_kernel(
             )
             nc.sync.dma_start(out=c[:, 512 * h : 512 * (h + 1)], in_=c_sb[:])
 
-        def store_lev():
-            lev_turned = keep.tile([P, 4, 32], F32, name="lev_turned", align_bytes=64)
+        lev_turned = keep.tile([P, 4, 32], F32, name="lev_turned", align_bytes=64)
+
+        def turn_lev():
             nc.vector.transpose(
                 out=lev_turned[:].rearrange("p t j -> p (t j)"), in_=lev_sb[:].rearrange("p t g -> p (t g)")
             )
+
+        def store_lev():
             lev_rows = keep.tile([P, 32, 4], F32, name="lev_rows", align_bytes=64)
             nc.vector.tensor_copy(out=lev_rows[:], in_=lev_turned[:].rearrange("p t j -> p j t"))
             for group in range(GROUPS):
@@ -387,6 +417,13 @@ def tile_weighted_leverage_sketch_s8_kernel(
                 for h in range(NG):
                     matmul_c(group, h)
 
+        c_done = []
+
+        def product_c_until(count):
+            for n in range(len(c_done), count):
+                matmul_c(n // 2, n % 2)
+                c_done.append(n)
+
         alone, shared = ("scalar", "scalar"), ("scalar", "vector")
 
         widen(0, nc.vector)
@@ -414,57 +451,64 @@ def tile_weighted_leverage_sketch_s8_kernel(
         quantize_b(0)
         quantize_a(2)
         turn_h(0, alone)
+        interleave_h(0, 0, partner=3)
 
         for step in range(2, PAIRS - 1):
             turn_a(step + 1)
             turn_h(step - 1, alone)
             product_h(step, 0, alone)
-            if step > 2:
-                sum_squares(step - 3, 1)
-            quantize_ht(step - 2)
+            if step == 2:
+                quantize_ht(0)
+            else:
+                sum_squares(step - 2, 1)
+            quantize_ht(step - 1)
             if live(step + 2):
                 widen_part(step + 2, slice(GPSIMD_COLUMNS, 2 * K), nc.vector)
-            if step > 2:
-                quantize_joint(step + 1, (step - 3) // 2, (step - 3) % 2)
-            else:
+            quantize_joint(step + 1, (step - 2) // 2, step % 2)
+            if step == 2:
                 quantize_b(1)
-                quantize_a(step + 1)
-            interleave_h((step - 2) // 2, step % 2, partner=step + 2 if live(step + 2) else None)
+            interleave_h((step - 1) // 2, (step - 1) % 2, partner=step + 2 if live(step + 2) else None)
             product_h(step, 1, alone)
-            if step >= 4:
-                matmul_c((step - 4) // 2, step % 2)
-            product_y(step - 2, alone)
-            sum_squares(step - 2, 0)
+            if step >= 5:
+                product_c_until(min(step - 2, 1 * (step - 5 + 1)))
+            if step == 2:
+                product_y(0, alone)
+                for i in range(2):
+                    sum_squares(0, i)
+            product_y(step - 1, alone)
+            sum_squares(step - 1, 0)
 
         end, final = PAIRS - 1, GROUPS - 1
-        quantize_ht(end - 2)
-        product_h(end, 0, shared)
-        quantize_hc(final - 1, 0)
-        interleave_h(final - 1, 1)
-        turn_h(end - 1, alone)
-        product_h(end, 1, alone)
-        interleave_h(final, 0)
-        quantize_ht(end - 1)
-        matmul_c(3, 1)
-        product_y(end - 2, alone)
-        turn_h(end, alone)
-        interleave_h(final, 1)
-        quantize_ht(end)
+        turn_h(end - 1, shared)
         quantize_hc(final - 1, 1)
-        sum_squares(end - 3, 1)
-        product_y(end - 1, alone)
+        product_h(end, 0, shared)
+        quantize_ht(end - 1)
+        product_h(end, 1, alone)
+        turn_h_half(end, 0, "scalar")
+        interleave_h(final, 0)
+        sum_squares(end - 2, 1)
+        for i in range(2):
+            matmul_y(end - 1, i)
+        store_y(end - 1, 0, "scalar")
+        turn_h_half(end, 1, "scalar")
+        store_y(end - 1, 1, "scalar")
+        quantize_ht_half(end, 0)
+        interleave_h(final, 1)
+        quantize_ht_half(end, 1)
+        product_c_until(2 * final)
+        for h in range(NG):
+            for i in range(2):
+                matmul_y_half(end, i, h)
         for h in range(NG):
             quantize_hc(final, h)
+        product_c_until(2 * GROUPS)
         for i in range(2):
-            matmul_y(end, i)
-        product_c(range(final - 1, GROUPS))
-        for i in range(2):
-            sum_squares(end - 2, i)
-        for i in range(2):
-            store_y(end, i, "scalar")
-        for h in range(NG):
-            store_c(h, "vector")
-        for pair in (end - 1, end):
-            for i in range(2):
-                sum_squares(pair, i, "vector" if (pair, i) == (end, 1) else "scalar")
+            sum_squares(end - 1, i)
+        store_y(end, 0, "scalar")
+        store_y(end, 1, "vector")
+        sum_squares(end, 0, "scalar")
+        store_c(0, "vector")
+        sum_squares(end, 1, "scalar")
+        store_c(1, "vector")
+        turn_lev()
         store_lev()

@@ -146,28 +146,42 @@ def tile_weighted_leverage_sketch_s8_kernel(
 
         def transpose_a(pair):
             rows = a_wide[pair][:].rearrange("p (i k) -> p i k", i=2)
-            for g in range(KG):
-                a_bank[pair, g] = take_bank(dtype=BF16)
-                for t in range(4):
-                    for i in range(2):
-                        s = 2 * t + i
-                        nc.tensor.matmul(
-                            out=a_bank[pair, g][:, s * P : (s + 1) * P],
-                            lhsT=rows[:, i, 512 * g + t : 512 * (g + 1) : 4],
-                            rhs=ident_bf[:],
-                            start=True,
-                            stop=True,
-                        )
+            a_bank[pair, 0] = take_bank(dtype=BF16)
+            for t in range(4):
+                for i in range(2):
+                    s = 2 * t + i
+                    nc.tensor.matmul(
+                        out=a_bank[pair, 0][:, s * P : (s + 1) * P],
+                        lhsT=rows[:, i, t:512:4],
+                        rhs=ident_bf[:],
+                        start=True,
+                        stop=True,
+                    )
+            words = a_wide[pair][:].bitcast(F32).rearrange("p (i k) -> p i k", i=2)
+            a_bank[pair, 1] = take_bank()
+            for u in range(2):
+                for i in range(2):
+                    s = 2 * u + i
+                    nc.tensor.transpose(a_bank[pair, 1][:, s * P : (s + 1) * P], words[:, i, 256 + u : 512 : 2], ident[:])
 
         def scale_a(pair, g):
             if pair not in a_grouped:
                 a_grouped[pair] = work.tile([P, 2 * K], BF16, name="a_grouped", tag="a_ring", align_bytes=64)[:]
-            nc.vector.tensor_tensor(
-                out=a_grouped[pair][:, K * g : K * (g + 1)].rearrange("p (c t) -> p c t", t=4),
-                in0=a_bank[pair, g][:].rearrange("p (t c) -> p c t", t=4),
-                in1=scale_p[:, g].unsqueeze(1).to_broadcast([P, 2 * P, 4]),
-                op=MULT,
-            )
+            out = a_grouped[pair][:, K * g : K * (g + 1)]
+            if g == 0:
+                nc.vector.tensor_tensor(
+                    out=out.rearrange("p (c t) -> p c t", t=4),
+                    in0=a_bank[pair, g][:].rearrange("p (t c) -> p c t", t=4),
+                    in1=scale_p[:, g].unsqueeze(1).to_broadcast([P, 2 * P, 4]),
+                    op=MULT,
+                )
+            else:
+                nc.vector.tensor_tensor(
+                    out=out.rearrange("p (c u e) -> p c u e", u=2, e=2),
+                    in0=a_bank[pair, g][:].bitcast(BF16).rearrange("p (u c e) -> p c u e", u=2, e=2),
+                    in1=scale_p[:, g].rearrange("p (u e) -> p u e", u=2).unsqueeze(1).to_broadcast([P, 2 * P, 2, 2]),
+                    op=MULT,
+                )
 
         def quantize(grouped, name, pool):
             width = grouped.shape[1] // 4

@@ -25,6 +25,7 @@ KG = K // 512
 NG = N // 512
 BANKS = 8
 GPSIMD_COLUMNS = 1792
+HEADG = 1536
 
 
 def tile_weighted_leverage_sketch_s8_kernel(
@@ -52,13 +53,10 @@ def tile_weighted_leverage_sketch_s8_kernel(
             else:
                 nc.scalar.copy(out=out, in_=in_)
 
-        scale_p = keep.tile([P, KG, 4], F32, name="scale_p", align_bytes=64)
-        nc.scalar.dma_start(
-            out=scale_p[:],
-            in_=a_scale.rearrange("o (g p t) -> p (o g) t", p=P, t=4),
-        )
-        w_bf = keep.tile([P, GROUPS, 4], BF16, name="w_bf", align_bytes=64)
-        nc.scalar.dma_start(out=w_bf[:], in_=w.rearrange("(g p t) -> p g t", p=P, t=4))
+        scale_rows = keep.tile([P, 512], F32, name="scale_rows", align_bytes=64)
+        nc.vector.memset(scale_rows[:], 0.0)
+        w_rows = keep.tile([P, 512], BF16, name="w_rows", align_bytes=64)
+        nc.vector.memset(w_rows[:].bitcast(I32), 0)
 
         ident = keep.tile([P, P], F32, name="ident", align_bytes=64)
         make_identity(nc, ident[:])
@@ -69,7 +67,9 @@ def tile_weighted_leverage_sketch_s8_kernel(
         nc.vector.memset(lev_sb[:], 0.0)
 
         ident_bf = keep.tile([P, P], BF16, name="ident_bf", align_bytes=64)
-        nc.vector.tensor_copy(out=ident_bf[:], in_=ident[:])
+        nc.scalar.activation(out=ident_bf[:], in_=ident[:], func=COPY)
+
+        scale_p = keep.tile([P, KG, 4], F32, name="scale_p", align_bytes=64)
 
         a_view = a_bytes.rearrange("(g p t) k -> g p t k", p=P, t=4)
         rinv_view = rinv.rearrange("(g p t) n -> g p t n", p=P, t=4)
@@ -93,9 +93,12 @@ def tile_weighted_leverage_sketch_s8_kernel(
 
         for g in range(KG):
             load_a(g)
+            if g == 0:
+                nc.sync.dma_start(out=scale_rows[:KG], in_=a_scale.rearrange("o (g k) -> (o g) k", g=KG))
             load_rinv(0, g)
         load_b(0)
         load_b(1)
+        nc.sync.dma_start(out=w_rows[:GROUPS], in_=w.rearrange("(g m) -> g m", g=GROUPS))
         load_rinv(1, 0)
         load_a(2)
         load_rinv(1, 1)
@@ -111,19 +114,30 @@ def tile_weighted_leverage_sketch_s8_kernel(
             load_a(pair)
 
         w_sb = keep.tile([P, GROUPS * 4], F32, name="w_sb", align_bytes=64)
-        nc.scalar.activation(out=w_sb[:], in_=w_bf[:].rearrange("p g t -> p (g t)"), func=COPY)
+
+        def cast_w():
+            bank = take_bank(dtype=BF16)
+            for t in range(4):
+                nc.tensor.matmul(
+                    out=bank[:, t * P : (t + 1) * P], lhsT=w_rows[:, t::4], rhs=ident_bf[:], start=True, stop=True
+                )
+            nc.scalar.activation(
+                out=w_sb[:].rearrange("p (g t) -> p g t", t=4),
+                in_=bank[:, : 4 * P].rearrange("p (t g) -> p g t", t=4)[:, :GROUPS],
+                func=COPY,
+            )
 
         r_codes = keep.tile([P, KG, N], U32, name="r_codes", align_bytes=64)
         r_scales = keep.tile([P, KG, N], U8, name="r_scales", align_bytes=64)
         r_grouped = {}
 
-        def interleave_rinv(h, g, u, engine):
+        def interleave_rinv(h, g, u, engine, part=slice(0, P)):
             if (h, g) not in r_grouped:
-                r_grouped[h, g] = work.tile([P, 512, 4], BF16, name="r_grouped", tag="hc_grouped" if h == 0 else "ht_grouped", align_bytes=64)
+                r_grouped[h, g] = work.tile([P, 512, 4], BF16, name="r_grouped", tag=f"gate{h}" if g else "hc_grouped", bufs=1 if g else 3, align_bytes=64)
             copy_on(
                 engine,
-                r_grouped[h, g][:].rearrange("p (u q e) t -> p u q t e", u=2, e=2)[:, u],
-                r_raw[h, g][:].rearrange("p t (q u e) -> p u q t e", u=2, e=2)[:, u],
+                r_grouped[h, g][:].rearrange("p (u q e) t -> p u q t e", u=2, e=2)[:, u, part],
+                r_raw[h, g][:].rearrange("p t (q u e) -> p u q t e", u=2, e=2)[:, u, part],
             )
 
         def quantize_rinv(h, g):
@@ -137,51 +151,64 @@ def tile_weighted_leverage_sketch_s8_kernel(
         a_wide, a_bank, a_grouped, a_codes, a_scales = {}, {}, {}, {}, {}
 
         def widen(pair, engine):
-            a_wide[pair] = work.tile([P, 2 * K], BF16, name="a_wide", tag="a_ring", align_bytes=64)
-            widen_part(pair, slice(0, 2 * K if pair < 4 else GPSIMD_COLUMNS), engine)
+            tag, bufs = (f"gate{pair - 2}", 1) if pair in (2, 3) else ("ht_grouped" if pair < 2 else "a_ring", 3)
+            a_wide[pair] = work.tile([P, 2 * K], BF16, name="a_wide", tag=tag, bufs=bufs, align_bytes=64)
+            widen_part(pair, slice(0, HEADG if pair == 1 else 2 * K if pair < 4 else GPSIMD_COLUMNS), engine)
 
         def widen_part(pair, cols, engine):
+            if pair not in a_wide:
+                a_wide[pair] = work.tile([P, 2 * K], BF16, name="a_wide", tag="ht_grouped", align_bytes=64)
             codes = a8[pair][:].rearrange("p i k -> p (i k)")
-            engine.tensor_copy(out=a_wide[pair][:, cols], in_=codes[:, cols].bitcast(FP8))
+            if engine is nc.scalar:
+                nc.scalar.copy(out=a_wide[pair][:, cols], in_=codes[:, cols].bitcast(FP8))
+            else:
+                engine.tensor_copy(out=a_wide[pair][:, cols], in_=codes[:, cols].bitcast(FP8))
 
         def transpose_a(pair):
             rows = a_wide[pair][:].rearrange("p (i k) -> p i k", i=2)
-            a_bank[pair, 0] = take_bank(dtype=BF16)
-            for t in range(4):
-                for i in range(2):
-                    s = 2 * t + i
+            for g in range(KG):
+                a_bank[pair, g] = take_bank(dtype=BF16)
+                for t in range(4):
+                    for i in range(2):
+                        s = 2 * t + i
+                        nc.tensor.matmul(
+                            out=a_bank[pair, g][:, s * P : (s + 1) * P],
+                            lhsT=rows[:, i, 512 * g + t : 512 * (g + 1) : 4],
+                            rhs=ident_bf[:],
+                            start=True,
+                            stop=True,
+                        )
+
+        def scale_a(pair, g):
+            if pair not in a_grouped:
+                a_grouped[pair] = work.tile([P, 2 * K], BF16, name="a_grouped", tag="h_rows" if pair == 1 else "a_ring", bufs=6 if pair == 1 else 3, align_bytes=64)[:]
+            nc.vector.tensor_tensor(
+                out=a_grouped[pair][:, K * g : K * (g + 1)].rearrange("p (c t) -> p c t", t=4),
+                in0=a_bank[pair, g][:].rearrange("p (t c) -> p c t", t=4),
+                in1=scale_p[:, g].unsqueeze(1).to_broadcast([P, 2 * P, 4]),
+                op=MULT,
+            )
+
+        def turn_first(i):
+            bank = take_bank(dtype=BF16)
+            for g in range(KG):
+                for t in range(4):
+                    s = 4 * g + t
                     nc.tensor.matmul(
-                        out=a_bank[pair, 0][:, s * P : (s + 1) * P],
-                        lhsT=rows[:, i, t:512:4],
+                        out=bank[:, s * P : (s + 1) * P],
+                        lhsT=a_wide[0][:, K * i + 512 * g + t : K * i + 512 * (g + 1) : 4],
                         rhs=ident_bf[:],
                         start=True,
                         stop=True,
                     )
-            words = a_wide[pair][:].bitcast(F32).rearrange("p (i k) -> p i k", i=2)
-            a_bank[pair, 1] = take_bank()
-            for u in range(2):
-                for i in range(2):
-                    s = 2 * u + i
-                    nc.tensor.transpose(a_bank[pair, 1][:, s * P : (s + 1) * P], words[:, i, 256 + u : 512 : 2], ident[:])
-
-        def scale_a(pair, g):
-            if pair not in a_grouped:
-                a_grouped[pair] = work.tile([P, 2 * K], BF16, name="a_grouped", tag="a_ring", align_bytes=64)[:]
-            out = a_grouped[pair][:, K * g : K * (g + 1)]
-            if g == 0:
-                nc.vector.tensor_tensor(
-                    out=out.rearrange("p (c t) -> p c t", t=4),
-                    in0=a_bank[pair, g][:].rearrange("p (t c) -> p c t", t=4),
-                    in1=scale_p[:, g].unsqueeze(1).to_broadcast([P, 2 * P, 4]),
-                    op=MULT,
-                )
-            else:
-                nc.vector.tensor_tensor(
-                    out=out.rearrange("p (c u e) -> p c u e", u=2, e=2),
-                    in0=a_bank[pair, g][:].bitcast(BF16).rearrange("p (u c e) -> p c u e", u=2, e=2),
-                    in1=scale_p[:, g].rearrange("p (u e) -> p u e", u=2).unsqueeze(1).to_broadcast([P, 2 * P, 2, 2]),
-                    op=MULT,
-                )
+            if i == 0:
+                a_grouped[0] = work.tile([P, 2 * K], BF16, name="a_grouped", tag="h_rows", bufs=6, align_bytes=64)[:]
+            nc.vector.tensor_tensor(
+                out=a_grouped[0].rearrange("p (g i c t) -> p i g c t", g=KG, i=2, t=4)[:, i],
+                in0=bank[:].rearrange("p (g t c) -> p g c t", g=KG, t=4),
+                in1=scale_p[:].unsqueeze(2).to_broadcast([P, KG, P, 4]),
+                op=MULT,
+            )
 
         def quantize(grouped, name, pool):
             width = grouped.shape[1] // 4
@@ -242,7 +269,7 @@ def tile_weighted_leverage_sketch_s8_kernel(
 
         def copy_ht(pair, i, engine):
             if i == 0:
-                ht_grouped[pair] = work.tile([P, 2 * N], BF16, name="ht_grouped", tag="ht_grouped", align_bytes=64)
+                ht_grouped[pair] = work.tile([P, 2 * N], BF16, name="ht_grouped", tag="ht_grouped" if pair else "a_ring", align_bytes=64)
             copy_words(engine, ht_grouped[pair][:, N * i : N * (i + 1)], ht_bank[pair, i])
 
         def turn_h_half(pair, h, engine):
@@ -440,27 +467,40 @@ def tile_weighted_leverage_sketch_s8_kernel(
 
         alone, shared = ("scalar", "scalar"), ("scalar", "vector")
 
-        widen(0, nc.vector)
+        scale_bank = take_bank()
+        for t in range(4):
+            nc.tensor.transpose(scale_bank[:, t * P : (t + 1) * P], scale_rows[:, t::4], ident[:])
+        for i in range(2):
+            widen_part(0, slice(K * i, K * i + 512), nc.vector)
+            widen_part(0, slice(K * i + 512, K * (i + 1)), nc.scalar)
+        nc.vector.tensor_copy(out=scale_p[:], in_=scale_bank[:].rearrange("p (t g) -> p g t", t=4)[:, :KG])
         interleave_rinv(0, 0, 0, "scalar")
         interleave_rinv(0, 0, 1, "vector")
-        turn_a(0)
-        for h, g, u in ((0, 1, 0), (0, 1, 1), (1, 0, 0), (1, 0, 1), (1, 1, 0)):
+        turn_first(0)
+        widen(1, nc.gpsimd)
+        widen_part(1, slice(HEADG, 2 * K), nc.scalar)
+        turn_first(1)
+        interleave_rinv(0, 1, 0, "scalar")
+        interleave_rinv(0, 1, 1, "scalar", slice(0, 64))
+        turn_b(0)
+        for h, g, u in ((1, 0, 0), (1, 0, 1), (1, 1, 0)):
             interleave_rinv(h, g, u, "scalar")
-        for j in range(2):
-            turn_b(j)
+        cast_w()
+        turn_b(1)
+        interleave_rinv(0, 1, 1, "vector", slice(64, P))
         quantize_rinv(0, 0)
-        quantize_a(0)
         quantize_rinv(0, 1)
+        quantize_a(0)
         turn_a(1)
         product_h(0, 0, alone)
         turn_b(2)
-        quantize_a(1)
         interleave_rinv(1, 1, 1, "vector")
         quantize_rinv(1, 0)
         quantize_rinv(1, 1)
+        quantize_a(1)
         turn_a(2)
-        product_h(1, 0, alone)
         product_h(0, 1, alone)
+        product_h(1, 0, alone)
         product_h(1, 1, alone)
         quantize_b(0)
         quantize_a(2)

@@ -24,8 +24,7 @@ PAIRS = M // (2 * P)
 KG = K // 512
 NG = N // 512
 BANKS = 8
-GPSIMD_COLUMNS = 1792
-HEADG = 1536
+AHEAD = 5
 
 
 def tile_weighted_leverage_sketch_s8_kernel(
@@ -48,32 +47,40 @@ def tile_weighted_leverage_sketch_s8_kernel(
             return psum.tile([P, 512 if dtype is F32 else 1024], dtype, name=f"bank{number}", tag=f"bank{number}")
 
         def copy_on(engine, out, in_):
-            if engine == "vector":
+            if engine == "scalar":
+                nc.scalar.copy(out=out, in_=in_)
+            elif engine == "vector":
                 nc.vector.tensor_copy(out=out, in_=in_)
             else:
-                nc.scalar.copy(out=out, in_=in_)
+                nc.gpsimd.tensor_copy(out=out, in_=in_)
 
-        scale_rows = keep.tile([P, 512], F32, name="scale_rows", align_bytes=64)
-        nc.vector.memset(scale_rows[:], 0.0)
-        w_rows = keep.tile([P, 512], BF16, name="w_rows", align_bytes=64)
-        nc.vector.memset(w_rows[:].bitcast(I32), 0)
+        def quantize(grouped, name, pool, bufs):
+            width = grouped.shape[1] // 4
+            codes = pool.tile([P, width], U32, name=name + "_codes", tag=name + "_codes", bufs=bufs, align_bytes=64)
+            scales = pool.tile([P, width], U8, name=name + "_scales", tag=name + "_scales", bufs=bufs, align_bytes=64)
+            nc.vector.quantize_mx(out=codes[:].bitcast(FP8X4), scales=scales[:], in_=grouped)
+            return codes, scales
+
+        scale_p = keep.tile([P, KG, 4], F32, name="scale_p", align_bytes=64)
+        nc.scalar.dma_start(out=scale_p[:], in_=a_scale.rearrange("o (g p t) -> p (o g) t", p=P, t=4))
+        w_bf = keep.tile([P, GROUPS, 4], BF16, name="w_bf", align_bytes=64)
+        nc.scalar.dma_start(out=w_bf[:], in_=w.rearrange("(g p t) -> p g t", p=P, t=4))
 
         ident = keep.tile([P, P], F32, name="ident", align_bytes=64)
         make_identity(nc, ident[:])
+        ident_bf = keep.tile([P, P], BF16, name="ident_bf", align_bytes=64)
+        nc.scalar.activation(out=ident_bf[:], in_=ident[:], func=COPY)
         j_scales = keep.tile([P, NG, R], U8, name="j_scales", align_bytes=64)
         j_scales_i32 = j_scales[:].rearrange("p g n -> p (g n)").bitcast(I32)
         nc.vector.memset(j_scales_i32, 0)
-        lev_sb = keep.tile([P, 4, 32], F32, name="lev_sb", align_bytes=64)
-        nc.vector.memset(lev_sb[:], 0.0)
-
-        ident_bf = keep.tile([P, P], BF16, name="ident_bf", align_bytes=64)
-        nc.scalar.activation(out=ident_bf[:], in_=ident[:], func=COPY)
-
-        scale_p = keep.tile([P, KG, 4], F32, name="scale_p", align_bytes=64)
+        lev_sb = {}
+        for part in range(2):
+            lev_sb[part] = keep.tile([P, 4, 32], F32, name=f"lev_sb{part}", align_bytes=64)
+            nc.vector.memset(lev_sb[part][:], 0.0)
 
         a_view = a_bytes.rearrange("(g p t) k -> g p t k", p=P, t=4)
         rinv_view = rinv.rearrange("(g p t) n -> g p t n", p=P, t=4)
-        a8, r_raw = {}, {}
+        a8, r_raw, b_sb = {}, {}, {}
 
         def load_a(pair):
             t0 = 2 * (pair % 2)
@@ -81,158 +88,87 @@ def tile_weighted_leverage_sketch_s8_kernel(
             nc.sync.dma_start(out=a8[pair][:], in_=a_view[pair // 2, :, t0 : t0 + 2, :])
 
         def load_rinv(h, g):
-            r_raw[h, g] = keep.tile([P, 4, 512], BF16, name=f"r_raw_{h}{g}", align_bytes=64)
+            r_raw[h, g] = work.tile([P, 4, 512], BF16, name="r_raw", tag="h_rows", bufs=6, align_bytes=64)
             nc.sync.dma_start(out=r_raw[h, g][:], in_=rinv_view[g, :, :, 512 * h : 512 * (h + 1)])
-
-        j_words = keep.tile([P, NG, 2 * R], U8, name="j_words", align_bytes=64)
-        b_sb = {}
 
         def load_b(j):
             b_sb[j] = keep.tile([P, 1024], BF16, name=f"b_sb_{j}", align_bytes=64)
             nc.sync.dma_start(out=b_sb[j][:], in_=b[:, 1024 * j : 1024 * (j + 1)])
 
-        for g in range(KG):
-            load_a(g)
-            if g == 0:
-                nc.sync.dma_start(out=scale_rows[:KG], in_=a_scale.rearrange("o (g k) -> (o g) k", g=KG))
-            load_rinv(0, g)
-        load_b(0)
-        load_b(1)
-        nc.sync.dma_start(out=w_rows[:GROUPS], in_=w.rearrange("(g m) -> g m", g=GROUPS))
-        load_rinv(1, 0)
-        load_a(2)
-        load_rinv(1, 1)
-        load_b(2)
-        load_a(3)
-        nc.sync.dma_start(out=j_words[:], in_=jl_words.rearrange("g p n -> p g n"))
-        for q in range(4):
-            nc.sync.dma_start(
-                out=j_scales_i32[32 * q : 32 * q + 4, :].rearrange("p (g n) -> p g n", g=NG),
-                in_=jl_scales[:, 4 * q : 4 * q + 4, :].bitcast(I32).rearrange("g q n -> q g n"),
-            )
-        for pair in range(4, PAIRS):
-            load_a(pair)
+        j_words = keep.tile([P, NG, 2 * R], U8, name="j_words", align_bytes=64)
+
+        def load_j():
+            nc.sync.dma_start(out=j_words[:], in_=jl_words.rearrange("g p n -> p g n"))
+            for q in range(4):
+                nc.sync.dma_start(
+                    out=j_scales_i32[32 * q : 32 * q + 4, :].rearrange("p (g n) -> p g n", g=NG),
+                    in_=jl_scales[:, 4 * q : 4 * q + 4, :].bitcast(I32).rearrange("g q n -> q g n"),
+                )
 
         w_sb = keep.tile([P, GROUPS * 4], F32, name="w_sb", align_bytes=64)
 
         def cast_w():
-            bank = take_bank(dtype=BF16)
-            for t in range(4):
-                nc.tensor.matmul(
-                    out=bank[:, t * P : (t + 1) * P], lhsT=w_rows[:, t::4], rhs=ident_bf[:], start=True, stop=True
-                )
-            nc.scalar.activation(
-                out=w_sb[:].rearrange("p (g t) -> p g t", t=4),
-                in_=bank[:, : 4 * P].rearrange("p (t g) -> p g t", t=4)[:, :GROUPS],
-                func=COPY,
-            )
+            nc.scalar.activation(out=w_sb[:], in_=w_bf[:].rearrange("p g t -> p (g t)"), func=COPY)
 
-        r_codes = keep.tile([P, KG, N], U32, name="r_codes", align_bytes=64)
-        r_scales = keep.tile([P, KG, N], U8, name="r_scales", align_bytes=64)
-        r_grouped = {}
+        r_grouped, r_codes, r_scales = {}, {}, {}
 
-        def interleave_rinv(h, g, u, engine, part=slice(0, P)):
+        def interleave_rinv(h, g, u, engine):
             if (h, g) not in r_grouped:
-                r_grouped[h, g] = work.tile([P, 512, 4], BF16, name="r_grouped", tag=f"gate{h}" if g else "hc_grouped", bufs=1 if g else 3, align_bytes=64)
-            copy_on(
-                engine,
-                r_grouped[h, g][:].rearrange("p (u q e) t -> p u q t e", u=2, e=2)[:, u, part],
-                r_raw[h, g][:].rearrange("p t (q u e) -> p u q t e", u=2, e=2)[:, u, part],
-            )
+                r_grouped[h, g] = work.tile([P, 512, 4], BF16, name="r_grouped", tag=f"r_grouped{g}", bufs=1, align_bytes=64)
+            out = r_grouped[h, g][:].rearrange("p (u q e) t -> p u q e t", u=2, e=2)[:, u]
+            in_ = r_raw[h, g][:].rearrange("p t (q u e) -> p u q e t", u=2, e=2)[:, u]
+            if engine != "gpsimd":
+                out, in_ = out.rearrange("p q e t -> p q t e"), in_.rearrange("p q e t -> p q t e")
+            copy_on(engine, out, in_)
 
         def quantize_rinv(h, g):
-            cols = slice(512 * h, 512 * (h + 1))
-            nc.vector.quantize_mx(
-                out=r_codes[:, g, cols].bitcast(FP8X4),
-                scales=r_scales[:, g, cols],
-                in_=r_grouped[h, g][:].rearrange("p n t -> p (n t)"),
-            )
+            r_codes[h, g], r_scales[h, g] = quantize(r_grouped[h, g][:].rearrange("p n t -> p (n t)"), f"r{h}{g}", keep, 1)
 
         a_wide, a_bank, a_grouped, a_codes, a_scales = {}, {}, {}, {}, {}
 
-        def widen(pair, engine):
-            tag, bufs = (f"gate{pair - 2}", 1) if pair in (2, 3) else ("ht_grouped" if pair < 2 else "a_ring", 3)
-            a_wide[pair] = work.tile([P, 2 * K], BF16, name="a_wide", tag=tag, bufs=bufs, align_bytes=64)
-            widen_part(pair, slice(0, HEADG if pair == 1 else 2 * K if pair < 4 else GPSIMD_COLUMNS), engine)
-
-        def widen_part(pair, cols, engine):
+        def widen(pair, engine, cols=slice(0, 2 * K)):
             if pair not in a_wide:
-                a_wide[pair] = work.tile([P, 2 * K], BF16, name="a_wide", tag="ht_grouped", align_bytes=64)
+                a_wide[pair] = work.tile([P, 2 * K], BF16, name="a_wide", tag="a_wide", bufs=AHEAD, align_bytes=64)
             codes = a8[pair][:].rearrange("p i k -> p (i k)")
-            if engine is nc.scalar:
-                nc.scalar.copy(out=a_wide[pair][:, cols], in_=codes[:, cols].bitcast(FP8))
-            else:
-                engine.tensor_copy(out=a_wide[pair][:, cols], in_=codes[:, cols].bitcast(FP8))
+            copy_on(engine, a_wide[pair][:, cols], codes[:, cols].bitcast(FP8))
 
-        def transpose_a(pair):
-            rows = a_wide[pair][:].rearrange("p (i k) -> p i k", i=2)
-            for g in range(KG):
-                a_bank[pair, g] = take_bank(dtype=BF16)
-                for t in range(4):
-                    for i in range(2):
-                        s = 2 * t + i
-                        nc.tensor.matmul(
-                            out=a_bank[pair, g][:, s * P : (s + 1) * P],
-                            lhsT=rows[:, i, 512 * g + t : 512 * (g + 1) : 4],
-                            rhs=ident_bf[:],
-                            start=True,
-                            stop=True,
-                        )
-
-        def scale_a(pair, g):
-            if pair not in a_grouped:
-                a_grouped[pair] = work.tile([P, 2 * K], BF16, name="a_grouped", tag="h_rows" if pair == 1 else "a_ring", bufs=6 if pair == 1 else 3, align_bytes=64)[:]
-            nc.vector.tensor_tensor(
-                out=a_grouped[pair][:, K * g : K * (g + 1)].rearrange("p (c t) -> p c t", t=4),
-                in0=a_bank[pair, g][:].rearrange("p (t c) -> p c t", t=4),
-                in1=scale_p[:, g].unsqueeze(1).to_broadcast([P, 2 * P, 4]),
-                op=MULT,
+        def turn_a_plane(pair, i, s):
+            if s == 0:
+                a_bank[pair, i] = take_bank(dtype=BF16)
+            g, t = s // 4, s % 4
+            nc.tensor.matmul(
+                out=a_bank[pair, i][:, s * P : (s + 1) * P],
+                lhsT=a_wide[pair][:, K * i + 512 * g + t : K * i + 512 * (g + 1) : 4],
+                rhs=ident_bf[:],
+                start=True,
+                stop=True,
             )
 
-        def turn_first(i):
-            bank = take_bank(dtype=BF16)
-            for g in range(KG):
-                for t in range(4):
-                    s = 4 * g + t
-                    nc.tensor.matmul(
-                        out=bank[:, s * P : (s + 1) * P],
-                        lhsT=a_wide[0][:, K * i + 512 * g + t : K * i + 512 * (g + 1) : 4],
-                        rhs=ident_bf[:],
-                        start=True,
-                        stop=True,
-                    )
+        def scale_a(pair, i):
             if i == 0:
-                a_grouped[0] = work.tile([P, 2 * K], BF16, name="a_grouped", tag="h_rows", bufs=6, align_bytes=64)[:]
+                a_grouped[pair] = work.tile([P, 2 * K], BF16, name="a_grouped", tag="a_grouped", bufs=2, align_bytes=64)
             nc.vector.tensor_tensor(
-                out=a_grouped[0].rearrange("p (g i c t) -> p i g c t", g=KG, i=2, t=4)[:, i],
-                in0=bank[:].rearrange("p (g t c) -> p g c t", g=KG, t=4),
+                out=a_grouped[pair][:, K * i : K * (i + 1)].rearrange("p (g c t) -> p g c t", g=KG, t=4),
+                in0=a_bank[pair, i][:].rearrange("p (g t c) -> p g c t", g=KG, t=4),
                 in1=scale_p[:].unsqueeze(2).to_broadcast([P, KG, P, 4]),
                 op=MULT,
             )
 
-        def quantize(grouped, name, pool):
-            width = grouped.shape[1] // 4
-            codes = pool.tile([P, width], U32, name=name + "_codes", tag=name + "_codes", align_bytes=64)
-            scales = pool.tile([P, width], U8, name=name + "_scales", tag=name + "_scales", align_bytes=64)
-            nc.vector.quantize_mx(out=codes[:].bitcast(FP8X4), scales=scales[:], in_=grouped)
-            return codes, scales
-
         def quantize_a(pair):
-            a_codes[pair], a_scales[pair] = quantize(a_grouped[pair], "a", work)
+            a_codes[pair], a_scales[pair] = quantize(a_grouped[pair][:], "a", work, 4)
 
         h_bank, h_rows = {}, {}
 
         def matmul_h(pair, i, h):
             h_bank[pair, i, h] = take_bank()
-            cols = slice(512 * h, 512 * (h + 1))
             for g in range(KG):
-                rows = slice((2 * g + i) * P, (2 * g + i + 1) * P)
+                rows = slice((2 * i + g) * P, (2 * i + g + 1) * P)
                 nc.tensor.matmul_mx(
                     out=h_bank[pair, i, h][:],
                     lhsT=a_codes[pair][:, rows].bitcast(FP8X4),
                     lhsT_scale=a_scales[pair][:, rows],
-                    rhs=r_codes[:, g, cols].bitcast(FP8X4),
-                    rhs_scale=r_scales[:, g, cols],
+                    rhs=r_codes[h, g][:].bitcast(FP8X4),
+                    rhs_scale=r_scales[h, g][:],
                     start=(g == 0),
                     stop=(g == KG - 1),
                 )
@@ -250,64 +186,37 @@ def tile_weighted_leverage_sketch_s8_kernel(
 
         ht_bank, ht_grouped, ht_codes, ht_scales = {}, {}, {}, {}
 
-        def transpose_h(pair):
-            for i in range(2):
-                ht_bank[pair, i] = take_bank()
-                for s in range(4):
-                    h, u = s // 2, s % 2
-                    words = h_rows[pair // 2, h][:, 2 * (pair % 2) + i, :].bitcast(F32)
-                    nc.tensor.transpose(
-                        ht_bank[pair, i][:, s * P : (s + 1) * P], words[:, u * P : (u + 1) * P], ident[:]
-                    )
+        def turn_h_words(pair, h, s):
+            if s == 0:
+                ht_bank[pair, h] = take_bank()
+            i, u = s // 2, s % 2
+            words = h_rows[pair // 2, h][:, 2 * (pair % 2) + i, :].bitcast(F32)
+            nc.tensor.transpose(ht_bank[pair, h][:, s * P : (s + 1) * P], words[:, u * P : (u + 1) * P], ident[:])
 
         def copy_words(engine, grouped, bank):
             copy_on(
                 engine,
-                grouped.bitcast(F32).rearrange("p (g r u) -> p g r u", g=2, u=2),
-                bank[:].rearrange("p (g u r) -> p g r u", g=2, u=2),
+                grouped.bitcast(F32).rearrange("p (i r u) -> p i r u", i=2, u=2),
+                bank[:].rearrange("p (i u r) -> p i r u", i=2, u=2),
             )
 
-        def copy_ht(pair, i, engine):
-            if i == 0:
-                ht_grouped[pair] = work.tile([P, 2 * N], BF16, name="ht_grouped", tag="ht_grouped" if pair else "a_ring", align_bytes=64)
-            copy_words(engine, ht_grouped[pair][:, N * i : N * (i + 1)], ht_bank[pair, i])
+        def copy_ht(pair, h, engine):
+            if h == 0:
+                ht_grouped[pair] = work.tile([P, 2 * N], BF16, name="ht_grouped", tag="ht_grouped", bufs=2, align_bytes=64)
+            copy_words(engine, ht_grouped[pair][:, N * h : N * (h + 1)], ht_bank[pair, h])
 
-        def turn_h_half(pair, h, engine):
-            bank = take_bank()
-            for i in range(2):
-                words = h_rows[pair // 2, h][:, 2 * (pair % 2) + i, :].bitcast(F32)
-                for u in range(2):
-                    s = 2 * i + u
-                    nc.tensor.transpose(bank[:, s * P : (s + 1) * P], words[:, u * P : (u + 1) * P], ident[:])
-            ht_grouped[pair, h] = work.tile([P, N], BF16, name="ht_half", tag="ht_grouped", align_bytes=64)
-            copy_words(engine, ht_grouped[pair, h][:], bank)
-
-        def quantize_ht_half(pair, h):
-            ht_codes[pair, h], ht_scales[pair, h] = quantize(ht_grouped[pair, h][:], "ht", work)
-
-        def quantize_ht(pair):
-            ht_codes[pair], ht_scales[pair] = quantize(ht_grouped[pair][:], "ht", work)
+        def quantize_ht(pair, halves=range(NG)):
+            cols = slice(N * halves[0], N * (halves[-1] + 1))
+            codes, scales = quantize(ht_grouped[pair][:, cols], "ht", work, 3)
+            for n, h in enumerate(halves):
+                ht_codes[pair, h], ht_scales[pair, h] = codes[:, 256 * n : 256 * (n + 1)], scales[:, 256 * n : 256 * (n + 1)]
 
         y_bank, y_sb = {}, {}
         y_view = y.rearrange("(g p t) n -> g t p n", p=P, t=4)
 
-        def matmul_y(pair, i):
-            y_bank[pair, i] = take_bank()
-            for g in range(NG):
-                rows = slice((2 * i + g) * P, (2 * i + g + 1) * P)
-                nc.tensor.matmul_mx(
-                    out=y_bank[pair, i][:],
-                    lhsT=ht_codes[pair][:, rows].bitcast(FP8X4),
-                    lhsT_scale=ht_scales[pair][:, rows],
-                    rhs=j_words[:, g, :].bitcast(FP4X4),
-                    rhs_scale=j_scales[:, g, :],
-                    start=(g == 0),
-                    stop=(g == NG - 1),
-                )
-
-        def matmul_y_half(pair, i, h):
+        def matmul_y(pair, i, h, hold=False):
             if h == 0:
-                y_bank[pair, i] = take_bank(hold=True)
+                y_bank[pair, i] = take_bank(hold=hold)
             rows = slice(i * P, (i + 1) * P)
             nc.tensor.matmul_mx(
                 out=y_bank[pair, i][:],
@@ -324,10 +233,11 @@ def tile_weighted_leverage_sketch_s8_kernel(
             copy_on(engine, y_sb[pair, i][:], y_bank[pair, i][:])
             nc.sync.dma_start(out=y_view[pair // 2, 2 * (pair % 2) + i], in_=y_sb[pair, i][:])
 
-        def sum_squares(pair, i, engine="scalar", source=y_sb):
+        def sum_squares(pair, i, engine="scalar"):
             squares = work.tile([P, R], BF16, name="squares", tag="squares", bufs=2, align_bytes=64)
-            total = lev_sb[:, 2 * (pair % 2) + i, pair // 2 : pair // 2 + 1]
-            rows = source[pair, i][:]
+            group = pair // 2
+            total = lev_sb[group // (GROUPS - 1)][:, 2 * (pair % 2) + i, group : group + 1]
+            rows = y_sb[pair, i][:]
             if engine == "vector":
                 nc.vector.scalar_tensor_tensor(
                     out=squares[:], in0=rows, scalar=1.0 / R, in1=rows, op0=MULT, op1=MULT, accum_out=total
@@ -335,44 +245,51 @@ def tile_weighted_leverage_sketch_s8_kernel(
             else:
                 nc.scalar.activation(out=squares[:], in_=rows, func=SQUARE, scale=R**-0.5, accum_out=total)
 
-        hc_grouped, hc_codes, hc_scales = {}, {}, {}
+        lev_turned = {}
 
-        joint = {}
-
-        def interleave_h(group, h, partner=None):
-            if partner is None:
-                tile = work.tile([P, 2048], BF16, name="hc_grouped", tag="hc_grouped", align_bytes=64)
-                hc_grouped[group, h] = tile[:]
-            else:
-                joint[partner] = work.tile([P, 4096], BF16, name="joint", tag="a_ring", align_bytes=64)
-                a_grouped[partner], hc_grouped[group, h] = joint[partner][:, :2048], joint[partner][:, 2048:]
-            out = hc_grouped[group, h].rearrange("p (c i t) -> p c t i", i=4, t=4)
-            in_ = h_rows[group, h][:].rearrange("p t (c i) -> p c t i", i=4)
-            nc.vector.tensor_copy(out=out, in_=in_)
-
-        def quantize_hc(group, h):
-            hc_codes[group, h], hc_scales[group, h] = (
-                tile[:] for tile in quantize(hc_grouped[group, h], f"hc{group}{h}", keep)
+        def turn_lev(part):
+            lev_turned[part] = keep.tile([P, 4, 32], F32, name=f"lev_turned{part}", align_bytes=64)
+            nc.vector.transpose(
+                out=lev_turned[part][:].rearrange("p t j -> p (t j)"), in_=lev_sb[part][:].rearrange("p t g -> p (t g)")
             )
 
-        def quantize_joint(pair, group, h):
-            codes, scales = quantize(joint[pair][:], f"joint{pair}", keep)
-            a_codes[pair], a_scales[pair] = codes[:, :512], scales[:, :512]
-            hc_codes[group, h], hc_scales[group, h] = codes[:, 512:], scales[:, 512:]
+        def store_lev(part, groups, queue):
+            lev_rows = keep.tile([P, 32, 4], F32, name=f"lev_rows{part}", align_bytes=64)
+            nc.vector.tensor_copy(out=lev_rows[:], in_=lev_turned[part][:].rearrange("p t j -> p j t"))
+            for group in groups:
+                queue.dma_start(
+                    out=lev[512 * group : 512 * (group + 1)].rearrange("(q m) -> q m", q=4),
+                    in_=lev_rows[group:P:32].rearrange("p j t -> p (j t)"),
+                )
+
+        hc_grouped, hc_codes, hc_scales = {}, {}, {}
+
+        def interleave_h(n, engine):
+            group, h = n // 2, n % 2
+            tag = "r_grouped1" if engine == "gpsimd" else "a_grouped"
+            hc_grouped[n] = work.tile([P, 2048], BF16, name="hc_grouped", tag=tag, bufs=1 if engine == "gpsimd" else 2, align_bytes=64)
+            if engine == "gpsimd":
+                out = hc_grouped[n][:].rearrange("p (c t) -> p c t", t=4)
+                in_ = h_rows[group, h][:].rearrange("p t c -> p c t")
+            else:
+                out = hc_grouped[n][:].rearrange("p (c i t) -> p c t i", i=4, t=4)
+                in_ = h_rows[group, h][:].rearrange("p t (c i) -> p c t i", i=4)
+            copy_on(engine, out, in_)
+
+        def quantize_hc(n):
+            hc_codes[n], hc_scales[n] = quantize(hc_grouped[n][:], f"hc{n}", keep, 1)
 
         b_grouped = keep.tile([P, GROUPS * 512], BF16, name="b_grouped", align_bytes=64)
         b_codes = keep.tile([P, GROUPS * P], U32, name="b_codes", align_bytes=64)
         b_scales = keep.tile([P, GROUPS * P], U8, name="b_scales", align_bytes=64)
-        b_bank = {}
 
-        def transpose_b(j):
-            b_bank[j] = take_bank()
+        def turn_b(j, engine):
+            bank = take_bank()
             words = b_sb[j][:].bitcast(F32)
             for s in range(4):
                 group, u = s // 2, s % 2
-                nc.tensor.transpose(
-                    b_bank[j][:, s * P : (s + 1) * P], words[:, 256 * group + u : 256 * (group + 1) : 2], ident[:]
-                )
+                nc.tensor.transpose(bank[:, s * P : (s + 1) * P], words[:, 256 * group + u : 256 * (group + 1) : 2], ident[:])
+            copy_words(engine, b_grouped[:, 1024 * j : 1024 * (j + 1)], bank)
 
         def quantize_b(half):
             cols = slice(384 * half, 384 * (half + 1))
@@ -384,7 +301,8 @@ def tile_weighted_leverage_sketch_s8_kernel(
 
         c_bank = {}
 
-        def matmul_c(group, h):
+        def matmul_c(n):
+            group, h = n // 2, n % 2
             if group == 0:
                 c_bank[h] = take_bank(hold=True)
             rows = slice(group * P, (group + 1) * P)
@@ -392,8 +310,8 @@ def tile_weighted_leverage_sketch_s8_kernel(
                 out=c_bank[h][:],
                 lhsT=b_codes[:, rows].bitcast(FP8X4),
                 lhsT_scale=b_scales[:, rows],
-                rhs=hc_codes[group, h].bitcast(FP8X4),
-                rhs_scale=hc_scales[group, h],
+                rhs=hc_codes[n][:].bitcast(FP8X4),
+                rhs_scale=hc_scales[n][:],
                 start=(group == 0),
                 stop=(group == GROUPS - 1),
             )
@@ -407,162 +325,150 @@ def tile_weighted_leverage_sketch_s8_kernel(
             )
             nc.sync.dma_start(out=c[:, 512 * h : 512 * (h + 1)], in_=c_sb[:])
 
-        lev_turned = keep.tile([P, 4, 32], F32, name="lev_turned", align_bytes=64)
-
-        def turn_lev():
-            nc.vector.transpose(
-                out=lev_turned[:].rearrange("p t j -> p (t j)"), in_=lev_sb[:].rearrange("p t g -> p (t g)")
-            )
-
-        def store_lev():
-            lev_rows = keep.tile([P, 32, 4], F32, name="lev_rows", align_bytes=64)
-            nc.vector.tensor_copy(out=lev_rows[:], in_=lev_turned[:].rearrange("p t j -> p j t"))
-            for group in range(GROUPS):
-                queue = nc.sync if group % 2 == 0 else nc.scalar
-                queue.dma_start(
-                    out=lev[512 * group : 512 * (group + 1)].rearrange("(q m) -> q m", q=4),
-                    in_=lev_rows[group:P:32].rearrange("p j t -> p (j t)"),
-                )
-
         def live(pair):
             return 0 <= pair < PAIRS
 
-        def product_h(pair, h, engines):
+        def turn_a(pair):
+            for i in range(2):
+                for s in range(8):
+                    turn_a_plane(pair, i, s)
+
+        def turn_h(pair, halves=range(NG)):
+            for h in halves:
+                for s in range(4):
+                    turn_h_words(pair, h, s)
+
+        def product_h(pair, h, engines=("scalar", "scalar")):
             for i in range(2):
                 matmul_h(pair, i, h)
                 weigh_h(pair, i, h, engines[i])
 
-        def turn_a(pair):
-            transpose_a(pair)
-            scale_a(pair, 0)
-            if live(pair + 1):
-                widen(pair + 1, nc.gpsimd)
-            scale_a(pair, 1)
-
-        def turn_h(pair, engines):
-            transpose_h(pair)
-            for i in range(2):
-                copy_ht(pair, i, engines[i])
-
-        def turn_b(j):
-            transpose_b(j)
-            copy_words("scalar", b_grouped[:, 1024 * j : 1024 * (j + 1)], b_bank[j])
-
         def product_y(pair, engines):
             for i in range(2):
-                matmul_y(pair, i)
+                for h in range(NG):
+                    matmul_y(pair, i, h)
                 store_y(pair, i, engines[i])
 
-        def product_c(groups):
-            for group in groups:
-                for h in range(NG):
-                    matmul_c(group, h)
 
-        c_done = []
+        load_a(0)
+        load_rinv(0, 0)
+        load_rinv(0, 1)
+        load_a(1)
+        load_rinv(1, 0)
+        load_a(2)
+        load_rinv(1, 1)
+        load_a(3)
+        load_j()
+        load_a(4)
+        for j in range(3):
+            load_b(j)
+        for pair in range(5, PAIRS):
+            load_a(pair)
 
-        def product_c_until(count):
-            for n in range(len(c_done), count):
-                matmul_c(n // 2, n % 2)
-                c_done.append(n)
-
-        alone, shared = ("scalar", "scalar"), ("scalar", "vector")
-
-        scale_bank = take_bank()
-        for t in range(4):
-            nc.tensor.transpose(scale_bank[:, t * P : (t + 1) * P], scale_rows[:, t::4], ident[:])
         for i in range(2):
-            widen_part(0, slice(K * i, K * i + 512), nc.vector)
-            widen_part(0, slice(K * i + 512, K * (i + 1)), nc.scalar)
-        nc.vector.tensor_copy(out=scale_p[:], in_=scale_bank[:].rearrange("p (t g) -> p g t", t=4)[:, :KG])
+            widen(0, "vector", slice(K * i, K * i + 512))
+            widen(0, "scalar", slice(K * i + 512, K * (i + 1)))
+        turn_a(0)
         interleave_rinv(0, 0, 0, "scalar")
-        interleave_rinv(0, 0, 1, "vector")
-        turn_first(0)
-        widen(1, nc.gpsimd)
-        widen_part(1, slice(HEADG, 2 * K), nc.scalar)
-        turn_first(1)
+        interleave_rinv(0, 0, 1, "gpsimd")
+        scale_a(0, 0)
+        scale_a(0, 1)
+        widen(1, "scalar")
         interleave_rinv(0, 1, 0, "scalar")
-        interleave_rinv(0, 1, 1, "scalar", slice(0, 64))
-        turn_b(0)
-        for h, g, u in ((1, 0, 0), (1, 0, 1), (1, 1, 0)):
-            interleave_rinv(h, g, u, "scalar")
+        interleave_rinv(0, 1, 1, "vector")
+        turn_a(1)
         cast_w()
-        turn_b(1)
-        interleave_rinv(0, 1, 1, "vector", slice(64, P))
+        quantize_a(0)
         quantize_rinv(0, 0)
         quantize_rinv(0, 1)
-        quantize_a(0)
-        turn_a(1)
-        product_h(0, 0, alone)
-        turn_b(2)
+        interleave_rinv(1, 0, 0, "gpsimd")
+        interleave_rinv(1, 0, 1, "gpsimd")
+        widen(2, "scalar")
+        interleave_rinv(1, 1, 0, "scalar")
+        scale_a(1, 0)
+        scale_a(1, 1)
+        product_h(0, 0)
+        turn_a(2)
         interleave_rinv(1, 1, 1, "vector")
+        quantize_a(1)
         quantize_rinv(1, 0)
         quantize_rinv(1, 1)
-        quantize_a(1)
-        turn_a(2)
-        product_h(0, 1, alone)
-        product_h(1, 0, alone)
-        product_h(1, 1, alone)
-        quantize_b(0)
+        widen(3, "scalar")
+        product_h(1, 0)
+        scale_a(2, 0)
+        scale_a(2, 1)
+        widen(4, "scalar")
+        product_h(0, 1)
+        product_h(1, 1)
+        turn_h(0)
+        copy_ht(0, 0, "vector")
+        copy_ht(0, 1, "vector")
         quantize_a(2)
-        turn_h(0, alone)
-        interleave_h(0, 0, partner=3)
+        quantize_ht(0)
 
-        for step in range(2, PAIRS - 1):
-            turn_a(step + 1)
-            turn_h(step - 1, alone)
-            product_h(step, 0, alone)
-            if step == 2:
-                quantize_ht(0)
-            else:
-                sum_squares(step - 2, 1)
+        for step in range(2, PAIRS):
+            interleave_h(step - 2, "gpsimd")
+            if live(step + 1):
+                turn_a(step + 1)
+            turn_h(step - 1)
+            if live(step + 1):
+                scale_a(step + 1, 0)
+                scale_a(step + 1, 1)
+            if step > 2:
+                sum_squares(step - 3, 0)
+                sum_squares(step - 3, 1)
+            if live(step + 3):
+                widen(step + 3, "scalar")
+            copy_ht(step - 1, 0, "vector")
+            copy_ht(step - 1, 1, "vector")
+            product_h(step, 0)
+            product_h(step, 1)
+            if live(step + 1):
+                quantize_a(step + 1)
+            quantize_hc(step - 2)
             quantize_ht(step - 1)
-            if live(step + 2):
-                widen_part(step + 2, slice(GPSIMD_COLUMNS, 2 * K), nc.vector)
-            quantize_joint(step + 1, (step - 2) // 2, step % 2)
-            if step == 2:
-                quantize_b(1)
-            interleave_h((step - 1) // 2, (step - 1) % 2, partner=step + 2 if live(step + 2) else None)
-            product_h(step, 1, alone)
-            if step >= 5:
-                product_c_until(min(step - 2, 1 * (step - 5 + 1)))
-            if step == 2:
-                product_y(0, alone)
-                for i in range(2):
-                    sum_squares(0, i)
-            product_y(step - 1, alone)
-            sum_squares(step - 1, 0)
+            product_y(step - 2, ("scalar", "scalar"))
+            if step in (3, 4, 5):
+                turn_b(step - 3, "scalar")
+            if step in (7, 8):
+                quantize_b(step - 7)
 
-        end, final = PAIRS - 1, GROUPS - 1
-        turn_h(end - 1, shared)
-        quantize_hc(final - 1, 1)
-        product_h(end, 0, shared)
-        quantize_ht(end - 1)
-        product_h(end, 1, alone)
-        turn_h_half(end, 0, "scalar")
-        interleave_h(final, 0)
-        sum_squares(end - 2, 1)
+        end = PAIRS - 1
+        for n in range(4):
+            matmul_c(n)
+        turn_h(end, [0])
+        sum_squares(end - 2, 0)
+        interleave_h(10, "vector")
+        copy_ht(end, 0, "scalar")
+        turn_h(end, [1])
         for i in range(2):
-            matmul_y(end - 1, i)
+            for h in range(NG):
+                matmul_y(end - 1, i, h)
+        sum_squares(end - 2, 1)
+        copy_ht(end, 1, "scalar")
+        quantize_ht(end, [0])
+        quantize_hc(10)
+        interleave_h(11, "vector")
+        quantize_ht(end, [1])
+        quantize_hc(11)
         store_y(end - 1, 0, "scalar")
-        turn_h_half(end, 1, "scalar")
         store_y(end - 1, 1, "scalar")
-        quantize_ht_half(end, 0)
-        interleave_h(final, 1)
-        quantize_ht_half(end, 1)
-        product_c_until(2 * final)
+        for n in range(4, 10):
+            matmul_c(n)
         for h in range(NG):
             for i in range(2):
-                matmul_y_half(end, i, h)
-        for h in range(NG):
-            quantize_hc(final, h)
-        product_c_until(2 * GROUPS)
-        for i in range(2):
-            sum_squares(end - 1, i)
-        store_y(end, 0, "scalar")
+                matmul_y(end, i, h, hold=True)
+        turn_lev(0)
+        matmul_c(10)
+        matmul_c(11)
+        store_lev(0, range(GROUPS - 1), nc.sync)
+        sum_squares(end - 1, 0)
         store_y(end, 1, "vector")
-        sum_squares(end, 0, "scalar")
+        store_y(end, 0, "scalar")
+        sum_squares(end - 1, 1)
         store_c(0, "vector")
-        sum_squares(end, 1, "scalar")
-        store_c(1, "vector")
-        turn_lev()
-        store_lev()
+        sum_squares(end, 0)
+        sum_squares(end, 1, "vector")
+        store_c(1, "scalar")
+        turn_lev(1)
+        store_lev(1, [GROUPS - 1], nc.scalar)

@@ -24,7 +24,9 @@ PAIRS = M // (2 * P)
 KG = K // 512
 NG = N // 512
 BANKS = 8
-AHEAD = 5
+AHEAD = 7
+EARLY_GROUPS = 3
+GPSIMD_COLUMNS = 384
 
 
 def tile_weighted_leverage_sketch_s8_kernel(
@@ -114,7 +116,8 @@ def tile_weighted_leverage_sketch_s8_kernel(
 
         def interleave_rinv(h, g, u, engine):
             if (h, g) not in r_grouped:
-                r_grouped[h, g] = work.tile([P, 512, 4], BF16, name="r_grouped", tag=f"r_grouped{g}", bufs=1, align_bytes=64)
+                tag, bufs = ("ht_grouped", 2) if h == 0 else ("r_grouped", 2) if g else ("gate", 1)
+                r_grouped[h, g] = work.tile([P, 512, 4], BF16, name="r_grouped", tag=tag, bufs=bufs, align_bytes=64)
             out = r_grouped[h, g][:].rearrange("p (u q e) t -> p u q e t", u=2, e=2)[:, u]
             in_ = r_raw[h, g][:].rearrange("p t (q u e) -> p u q e t", u=2, e=2)[:, u]
             if engine != "gpsimd":
@@ -128,7 +131,8 @@ def tile_weighted_leverage_sketch_s8_kernel(
 
         def widen(pair, engine, cols=slice(0, 2 * K)):
             if pair not in a_wide:
-                a_wide[pair] = work.tile([P, 2 * K], BF16, name="a_wide", tag="a_wide", bufs=AHEAD, align_bytes=64)
+                tag, bufs = ("gate", 1) if pair == 4 else ("a_wide", AHEAD)
+                a_wide[pair] = work.tile([P, 2 * K], BF16, name="a_wide", tag=tag, bufs=bufs, align_bytes=64)
             codes = a8[pair][:].rearrange("p i k -> p (i k)")
             copy_on(engine, a_wide[pair][:, cols], codes[:, cols].bitcast(FP8))
 
@@ -233,11 +237,11 @@ def tile_weighted_leverage_sketch_s8_kernel(
             copy_on(engine, y_sb[pair, i][:], y_bank[pair, i][:])
             nc.sync.dma_start(out=y_view[pair // 2, 2 * (pair % 2) + i], in_=y_sb[pair, i][:])
 
-        def sum_squares(pair, i, engine="scalar"):
+        def sum_squares(pair, i, engine="scalar", source=y_sb):
             squares = work.tile([P, R], BF16, name="squares", tag="squares", bufs=2, align_bytes=64)
             group = pair // 2
-            total = lev_sb[group // (GROUPS - 1)][:, 2 * (pair % 2) + i, group : group + 1]
-            rows = y_sb[pair, i][:]
+            total = lev_sb[group // EARLY_GROUPS][:, 2 * (pair % 2) + i, group : group + 1]
+            rows = source[pair, i][:]
             if engine == "vector":
                 nc.vector.scalar_tensor_tensor(
                     out=squares[:], in0=rows, scalar=1.0 / R, in1=rows, op0=MULT, op1=MULT, accum_out=total
@@ -253,10 +257,11 @@ def tile_weighted_leverage_sketch_s8_kernel(
                 out=lev_turned[part][:].rearrange("p t j -> p (t j)"), in_=lev_sb[part][:].rearrange("p t g -> p (t g)")
             )
 
-        def store_lev(part, groups, queue):
+        def store_lev(part, groups):
             lev_rows = keep.tile([P, 32, 4], F32, name=f"lev_rows{part}", align_bytes=64)
             nc.vector.tensor_copy(out=lev_rows[:], in_=lev_turned[part][:].rearrange("p t j -> p j t"))
             for group in groups:
+                queue = nc.scalar if group == GROUPS - 2 else nc.sync
                 queue.dma_start(
                     out=lev[512 * group : 512 * (group + 1)].rearrange("(q m) -> q m", q=4),
                     in_=lev_rows[group:P:32].rearrange("p j t -> p (j t)"),
@@ -264,22 +269,19 @@ def tile_weighted_leverage_sketch_s8_kernel(
 
         hc_grouped, hc_codes, hc_scales = {}, {}, {}
 
-        def interleave_h(n, engine):
-            group, h = n // 2, n % 2
-            tag = "r_grouped1" if engine == "gpsimd" else "a_grouped"
-            hc_grouped[n] = work.tile([P, 2048], BF16, name="hc_grouped", tag=tag, bufs=1 if engine == "gpsimd" else 2, align_bytes=64)
+        def interleave_h(n, engine, cols=slice(0, 512)):
+            if n not in hc_grouped:
+                hc_grouped[n] = work.tile([P, 512, 4], BF16, name="hc_grouped", tag="r_grouped", bufs=2, align_bytes=64)
+            out, in_ = hc_grouped[n][:, cols, :], h_rows[n // 2, n % 2][:, :, cols]
             if engine == "gpsimd":
-                out = hc_grouped[n][:].rearrange("p (c t) -> p c t", t=4)
-                in_ = h_rows[group, h][:].rearrange("p t c -> p c t")
+                copy_on(engine, out, in_.rearrange("p t c -> p c t"))
             else:
-                out = hc_grouped[n][:].rearrange("p (c i t) -> p c t i", i=4, t=4)
-                in_ = h_rows[group, h][:].rearrange("p t (c i) -> p c t i", i=4)
-            copy_on(engine, out, in_)
+                copy_on(engine, out.rearrange("p (c i) t -> p c t i", i=4), in_.rearrange("p t (c i) -> p c t i", i=4))
 
         def quantize_hc(n):
-            hc_codes[n], hc_scales[n] = quantize(hc_grouped[n][:], f"hc{n}", keep, 1)
+            hc_codes[n], hc_scales[n] = quantize(hc_grouped[n][:].rearrange("p c t -> p (c t)"), f"hc{n}", keep, 1)
 
-        b_grouped = keep.tile([P, GROUPS * 512], BF16, name="b_grouped", align_bytes=64)
+        b_grouped = {}
         b_codes = keep.tile([P, GROUPS * P], U32, name="b_codes", align_bytes=64)
         b_scales = keep.tile([P, GROUPS * P], U8, name="b_scales", align_bytes=64)
 
@@ -289,14 +291,15 @@ def tile_weighted_leverage_sketch_s8_kernel(
             for s in range(4):
                 group, u = s // 2, s % 2
                 nc.tensor.transpose(bank[:, s * P : (s + 1) * P], words[:, 256 * group + u : 256 * (group + 1) : 2], ident[:])
-            copy_words(engine, b_grouped[:, 1024 * j : 1024 * (j + 1)], bank)
+            if j % 2 == 0:
+                b_grouped[j // 2] = work.tile([P, 2048], BF16, name="b_grouped", tag="r_grouped", bufs=2, align_bytes=64)
+            copy_words(engine, b_grouped[j // 2][:, 1024 * (j % 2) : 1024 * (j % 2 + 1)], bank)
 
-        def quantize_b(half):
-            cols = slice(384 * half, 384 * (half + 1))
+        def quantize_b(part):
+            width = 2048 if part == 0 else 1024
+            cols = slice(512 * part, 512 * part + width // 4)
             nc.vector.quantize_mx(
-                out=b_codes[:, cols].bitcast(FP8X4),
-                scales=b_scales[:, cols],
-                in_=b_grouped[:, 1536 * half : 1536 * (half + 1)],
+                out=b_codes[:, cols].bitcast(FP8X4), scales=b_scales[:, cols], in_=b_grouped[part][:, :width]
             )
 
         c_bank = {}
@@ -338,10 +341,21 @@ def tile_weighted_leverage_sketch_s8_kernel(
                 for s in range(4):
                     turn_h_words(pair, h, s)
 
+        def turn_both(pair_a, pair_h):
+            for half in range(2):
+                for s in range(4):
+                    turn_a_plane(pair_a, half, 2 * s)
+                    turn_a_plane(pair_a, half, 2 * s + 1)
+                    turn_h_words(pair_h, half, s)
+
         def product_h(pair, h, engines=("scalar", "scalar")):
             for i in range(2):
                 matmul_h(pair, i, h)
                 weigh_h(pair, i, h, engines[i])
+
+        def product_c(first, last):
+            for n in range(first, last):
+                matmul_c(n)
 
         def product_y(pair, engines):
             for i in range(2):
@@ -352,123 +366,145 @@ def tile_weighted_leverage_sketch_s8_kernel(
 
         load_a(0)
         load_rinv(0, 0)
-        load_rinv(0, 1)
         load_a(1)
+        load_rinv(0, 1)
         load_rinv(1, 0)
         load_a(2)
         load_rinv(1, 1)
         load_a(3)
-        load_j()
-        load_a(4)
         for j in range(3):
             load_b(j)
-        for pair in range(5, PAIRS):
+        load_a(4)
+        load_a(5)
+        load_j()
+        for pair in range(6, PAIRS):
             load_a(pair)
 
         for i in range(2):
             widen(0, "vector", slice(K * i, K * i + 512))
             widen(0, "scalar", slice(K * i + 512, K * (i + 1)))
         turn_a(0)
-        interleave_rinv(0, 0, 0, "scalar")
-        interleave_rinv(0, 0, 1, "gpsimd")
+        interleave_rinv(0, 0, 0, "vector")
+        interleave_rinv(0, 0, 1, "vector")
+        widen(1, "scalar")
+        turn_a(1)
+        interleave_rinv(0, 1, 0, "scalar")
+        interleave_rinv(0, 1, 1, "gpsimd")
         scale_a(0, 0)
         scale_a(0, 1)
-        widen(1, "scalar")
-        interleave_rinv(0, 1, 0, "scalar")
-        interleave_rinv(0, 1, 1, "vector")
-        turn_a(1)
-        cast_w()
-        quantize_a(0)
-        quantize_rinv(0, 0)
-        quantize_rinv(0, 1)
-        interleave_rinv(1, 0, 0, "gpsimd")
+        interleave_rinv(1, 0, 0, "scalar")
         interleave_rinv(1, 0, 1, "gpsimd")
         widen(2, "scalar")
+        cast_w()
+        quantize_rinv(0, 0)
+        quantize_a(0)
+        quantize_rinv(0, 1)
         interleave_rinv(1, 1, 0, "scalar")
         scale_a(1, 0)
         scale_a(1, 1)
         product_h(0, 0)
         turn_a(2)
+        widen(3, "scalar")
         interleave_rinv(1, 1, 1, "vector")
-        quantize_a(1)
         quantize_rinv(1, 0)
         quantize_rinv(1, 1)
-        widen(3, "scalar")
-        product_h(1, 0)
+        quantize_a(1)
+        widen(4, "gpsimd")
+        widen(5, "gpsimd")
+        turn_b(0, "scalar")
+        turn_b(1, "scalar")
+        product_h(0, 1)
         scale_a(2, 0)
         scale_a(2, 1)
-        widen(4, "scalar")
-        product_h(0, 1)
-        product_h(1, 1)
-        turn_h(0)
-        copy_ht(0, 0, "vector")
-        copy_ht(0, 1, "vector")
+        turn_b(2, "scalar")
         quantize_a(2)
-        quantize_ht(0)
 
-        for step in range(2, PAIRS):
-            interleave_h(step - 2, "gpsimd")
-            if live(step + 1):
-                turn_a(step + 1)
+        both, alone, shared = ("vector", "vector"), ("scalar", "scalar"), ("scalar", "vector")
+        widened = 6
+        for step in range(1, PAIRS - 2):
+            if step >= 2:
+                interleave_h(step - 2, "gpsimd", slice(0, GPSIMD_COLUMNS))
+            turn_a(step + 2)
             turn_h(step - 1)
-            if live(step + 1):
-                scale_a(step + 1, 0)
-                scale_a(step + 1, 1)
+            scale_a(step + 2, 0)
+            scale_a(step + 2, 1)
             if step > 2:
                 sum_squares(step - 3, 0)
                 sum_squares(step - 3, 1)
-            if live(step + 3):
-                widen(step + 3, "scalar")
-            copy_ht(step - 1, 0, "vector")
-            copy_ht(step - 1, 1, "vector")
+            todo = [pair for pair in range(widened, widened + 1) if live(pair)]
+            for pair in todo:
+                widen(pair, "scalar")
+            widened = widened + len(todo)
+            engines = both if todo and step > 2 else shared
+            copy_ht(step - 1, 0, engines[0])
+            copy_ht(step - 1, 1, engines[1])
+            if step == PAIRS - 3:
+                turn_lev(0)
             product_h(step, 0)
             product_h(step, 1)
-            if live(step + 1):
-                quantize_a(step + 1)
-            quantize_hc(step - 2)
+            if step >= 2:
+                interleave_h(step - 2, "vector", slice(GPSIMD_COLUMNS, 512))
+            if step == PAIRS - 3:
+                store_lev(0, range(EARLY_GROUPS))
+            if step >= 3:
+                quantize_hc(step - 3)
+            else:
+                quantize_b(step - 1)
+            quantize_a(step + 2)
             quantize_ht(step - 1)
-            product_y(step - 2, ("scalar", "scalar"))
-            if step in (3, 4, 5):
-                turn_b(step - 3, "scalar")
-            if step in (7, 8):
-                quantize_b(step - 7)
+            if step >= 2:
+                product_y(step - 2, alone)
+
 
         end = PAIRS - 1
-        for n in range(4):
-            matmul_c(n)
-        turn_h(end, [0])
-        sum_squares(end - 2, 0)
+        turn_h(end - 2)
+        sum_squares(end - 4, 0)
+        sum_squares(end - 4, 1)
+        copy_ht(end - 2, 0, "vector")
+        copy_ht(end - 2, 1, "vector")
+        product_h(end - 1, 0)
+        product_h(end - 1, 1)
+        quantize_hc(7)
+        quantize_ht(end - 2)
+        interleave_h(8, "vector")
+        interleave_h(9, "vector")
+        product_y(end - 3, alone)
+        product_c(0, 2)
+        turn_h(end - 1)
+        sum_squares(end - 3, 0)
+        sum_squares(end - 3, 1)
+        copy_ht(end - 1, 0, "vector")
+        copy_ht(end - 1, 1, "vector")
+        quantize_hc(8)
+        quantize_ht(end - 1)
+        quantize_hc(9)
+        product_h(end, 0)
+        product_h(end, 1)
+        product_y(end - 2, alone)
+        product_c(2, 4)
+        turn_h(end)
         interleave_h(10, "vector")
-        copy_ht(end, 0, "scalar")
-        turn_h(end, [1])
-        for i in range(2):
-            for h in range(NG):
-                matmul_y(end - 1, i, h)
-        sum_squares(end - 2, 1)
-        copy_ht(end, 1, "scalar")
-        quantize_ht(end, [0])
-        quantize_hc(10)
         interleave_h(11, "vector")
-        quantize_ht(end, [1])
+        sum_squares(end - 2, 0)
+        copy_ht(end, 0, "scalar")
+        copy_ht(end, 1, "scalar")
+        product_y(end - 1, alone)
+        product_c(4, 10)
+        quantize_hc(10)
+        quantize_ht(end)
         quantize_hc(11)
-        store_y(end - 1, 0, "scalar")
-        store_y(end - 1, 1, "scalar")
-        for n in range(4, 10):
-            matmul_c(n)
-        for h in range(NG):
-            for i in range(2):
+        sum_squares(end - 2, 1)
+        for i in (1, 0):
+            for h in range(NG):
                 matmul_y(end, i, h, hold=True)
-        turn_lev(0)
-        matmul_c(10)
-        matmul_c(11)
-        store_lev(0, range(GROUPS - 1), nc.sync)
+        product_c(10, 12)
         sum_squares(end - 1, 0)
+        sum_squares(end - 1, 1, "vector")
         store_y(end, 1, "vector")
+        sum_squares(end, 0, "scalar", y_bank)
         store_y(end, 0, "scalar")
-        sum_squares(end - 1, 1)
         store_c(0, "vector")
-        sum_squares(end, 0)
         sum_squares(end, 1, "vector")
         store_c(1, "scalar")
         turn_lev(1)
-        store_lev(1, [GROUPS - 1], nc.scalar)
+        store_lev(1, range(EARLY_GROUPS, GROUPS))

@@ -26,7 +26,7 @@ NG = N // 512
 BANKS = 8
 AHEAD = 7
 EARLY_GROUPS = 3
-GPSIMD_COLUMNS = 384
+GPSIMD_COLUMNS = 400
 
 
 def tile_weighted_leverage_sketch_s8_kernel(
@@ -115,23 +115,38 @@ def tile_weighted_leverage_sketch_s8_kernel(
         r_grouped, r_codes, r_scales = {}, {}, {}
 
         def interleave_rinv(h, g, u, engine):
-            if (h, g) not in r_grouped:
-                tag, bufs = ("ht_grouped", 2) if h == 0 else ("r_grouped", 2) if g else ("gate", 1)
-                r_grouped[h, g] = work.tile([P, 512, 4], BF16, name="r_grouped", tag=tag, bufs=bufs, align_bytes=64)
-            out = r_grouped[h, g][:].rearrange("p (u q e) t -> p u q e t", u=2, e=2)[:, u]
+            if (h, g) == (1, 0):
+                tag, bufs = ("ht_grouped", 2) if u else ("gate4", 1)
+                r_grouped[h, g, u] = work.tile([P, 256, 4], BF16, name="r_half", tag=tag, bufs=bufs, align_bytes=64)[:]
+            else:
+                if u == 0:
+                    tag = "r_grouped" if h else "ht_grouped"
+                    r_grouped[h, g] = work.tile([P, 512, 4], BF16, name="r_grouped", tag=tag, bufs=2, align_bytes=64)
+                r_grouped[h, g, u] = r_grouped[h, g][:, 256 * u : 256 * (u + 1), :]
+            out = r_grouped[h, g, u].rearrange("p (q e) t -> p q e t", e=2)
             in_ = r_raw[h, g][:].rearrange("p t (q u e) -> p u q e t", u=2, e=2)[:, u]
             if engine != "gpsimd":
                 out, in_ = out.rearrange("p q e t -> p q t e"), in_.rearrange("p q e t -> p q t e")
             copy_on(engine, out, in_)
 
         def quantize_rinv(h, g):
-            r_codes[h, g], r_scales[h, g] = quantize(r_grouped[h, g][:].rearrange("p n t -> p (n t)"), f"r{h}{g}", keep, 1)
+            r_codes[h, g] = keep.tile([P, 512], U32, name=f"r{h}{g}_codes", align_bytes=64)
+            r_scales[h, g] = keep.tile([P, 512], U8, name=f"r{h}{g}_scales", align_bytes=64)
+            parts = [(r_grouped[h, g][:], slice(0, 512))] if (h, g) in r_grouped else [
+                (r_grouped[h, g, u], slice(256 * u, 256 * (u + 1))) for u in range(2)
+            ]
+            for grouped, cols in parts:
+                nc.vector.quantize_mx(
+                    out=r_codes[h, g][:, cols].bitcast(FP8X4),
+                    scales=r_scales[h, g][:, cols],
+                    in_=grouped.rearrange("p n t -> p (n t)"),
+                )
 
         a_wide, a_bank, a_grouped, a_codes, a_scales = {}, {}, {}, {}, {}
 
         def widen(pair, engine, cols=slice(0, 2 * K)):
             if pair not in a_wide:
-                tag, bufs = ("gate", 1) if pair == 4 else ("a_wide", AHEAD)
+                tag, bufs = (f"gate{pair}", 1) if pair in (4, 5) else ("a_wide", AHEAD)
                 a_wide[pair] = work.tile([P, 2 * K], BF16, name="a_wide", tag=tag, bufs=bufs, align_bytes=64)
             codes = a8[pair][:].rearrange("p i k -> p (i k)")
             copy_on(engine, a_wide[pair][:, cols], codes[:, cols].bitcast(FP8))
@@ -150,7 +165,8 @@ def tile_weighted_leverage_sketch_s8_kernel(
 
         def scale_a(pair, i):
             if i == 0:
-                a_grouped[pair] = work.tile([P, 2 * K], BF16, name="a_grouped", tag="a_grouped", bufs=2, align_bytes=64)
+                tag, bufs = ("gate5", 1) if pair == 2 else ("a_grouped", 2)
+                a_grouped[pair] = work.tile([P, 2 * K], BF16, name="a_grouped", tag=tag, bufs=bufs, align_bytes=64)
             nc.vector.tensor_tensor(
                 out=a_grouped[pair][:, K * i : K * (i + 1)].rearrange("p (g c t) -> p g c t", g=KG, t=4),
                 in0=a_bank[pair, i][:].rearrange("p (g t c) -> p g c t", g=KG, t=4),
@@ -393,10 +409,10 @@ def tile_weighted_leverage_sketch_s8_kernel(
         scale_a(0, 0)
         scale_a(0, 1)
         interleave_rinv(1, 0, 0, "scalar")
-        interleave_rinv(1, 0, 1, "gpsimd")
         widen(2, "scalar")
         cast_w()
         quantize_rinv(0, 0)
+        interleave_rinv(1, 0, 1, "gpsimd")
         quantize_a(0)
         quantize_rinv(0, 1)
         interleave_rinv(1, 1, 0, "scalar")
@@ -410,7 +426,6 @@ def tile_weighted_leverage_sketch_s8_kernel(
         quantize_rinv(1, 1)
         quantize_a(1)
         widen(4, "gpsimd")
-        widen(5, "gpsimd")
         turn_b(0, "scalar")
         turn_b(1, "scalar")
         product_h(0, 1)
@@ -418,6 +433,7 @@ def tile_weighted_leverage_sketch_s8_kernel(
         scale_a(2, 1)
         turn_b(2, "scalar")
         quantize_a(2)
+        widen(5, "gpsimd")
 
         both, alone, shared = ("vector", "vector"), ("scalar", "scalar"), ("scalar", "vector")
         widened = 6

@@ -440,8 +440,7 @@ def tile_weighted_leverage_sketch_s8_kernel(
         for step in range(1, PAIRS - 2):
             if step >= 2:
                 interleave_h(step - 2, "gpsimd", slice(0, GPSIMD_COLUMNS))
-            turn_a(step + 2)
-            turn_h(step - 1)
+            turn_both(step + 2, step - 1)
             scale_a(step + 2, 0)
             scale_a(step + 2, 1)
             if step > 2:

@@ -24,7 +24,7 @@ PAIRS = M // (2 * P)
 KG = K // 512
 NG = N // 512
 BANKS = 8
-AHEAD = 7
+EARLY_PAIR = 10
 EARLY_GROUPS = 3
 GPSIMD_COLUMNS = 400
 
@@ -146,7 +146,7 @@ def tile_weighted_leverage_sketch_s8_kernel(
 
         def widen(pair, engine, cols=slice(0, 2 * K)):
             if pair not in a_wide:
-                tag, bufs = (f"gate{pair}", 1) if pair in (4, 5) else ("a_wide", AHEAD)
+                tag, bufs = (f"gate{pair}", 1) if 4 <= pair < EARLY_PAIR else ("a_wide", 4)
                 a_wide[pair] = work.tile([P, 2 * K], BF16, name="a_wide", tag=tag, bufs=bufs, align_bytes=64)
             codes = a8[pair][:].rearrange("p i k -> p (i k)")
             copy_on(engine, a_wide[pair][:, cols], codes[:, cols].bitcast(FP8))
@@ -165,7 +165,8 @@ def tile_weighted_leverage_sketch_s8_kernel(
 
         def scale_a(pair, i):
             if i == 0:
-                tag, bufs = ("gate5", 1) if pair == 2 else ("a_grouped", 2)
+                freed = 5 if pair == 2 else pair + 2
+                tag, bufs = (f"gate{freed}", 1) if pair == 2 or 6 <= freed < EARLY_PAIR else ("a_grouped", 2)
                 a_grouped[pair] = work.tile([P, 2 * K], BF16, name="a_grouped", tag=tag, bufs=bufs, align_bytes=64)
             nc.vector.tensor_tensor(
                 out=a_grouped[pair][:, K * i : K * (i + 1)].rearrange("p (g c t) -> p g c t", g=KG, t=4),
@@ -392,8 +393,10 @@ def tile_weighted_leverage_sketch_s8_kernel(
             load_b(j)
         load_a(4)
         load_a(5)
+        for pair in range(EARLY_PAIR, PAIRS):
+            load_a(pair)
         load_j()
-        for pair in range(6, PAIRS):
+        for pair in range(6, EARLY_PAIR):
             load_a(pair)
 
         for i in range(2):
@@ -435,38 +438,42 @@ def tile_weighted_leverage_sketch_s8_kernel(
         quantize_a(2)
         widen(5, "gpsimd")
 
-        both, alone, shared = ("vector", "vector"), ("scalar", "scalar"), ("scalar", "vector")
-        widened = 6
+        both, alone, shared = ("vector", "vector"), ("scalar", "scalar"), ("vector", "scalar")
         for step in range(1, PAIRS - 2):
-            if step >= 2:
-                interleave_h(step - 2, "gpsimd", slice(0, GPSIMD_COLUMNS))
+            widening = 6 <= step + 3 < EARLY_PAIR
+            columns = GPSIMD_COLUMNS
+            if widening:
+                widen(step + 3, "gpsimd", slice(0, 2 * K))
+            elif step >= 2:
+                interleave_h(step - 2, "gpsimd", slice(0, columns))
             turn_both(step + 2, step - 1)
-            scale_a(step + 2, 0)
-            scale_a(step + 2, 1)
             if step > 2:
                 sum_squares(step - 3, 0)
                 sum_squares(step - 3, 1)
-            todo = [pair for pair in range(widened, widened + 1) if live(pair)]
-            for pair in todo:
+            for pair in [EARLY_PAIR + step - 1] if EARLY_PAIR + step - 1 < PAIRS else []:
                 widen(pair, "scalar")
-            widened = widened + len(todo)
-            engines = both if todo and step > 2 else shared
-            copy_ht(step - 1, 0, engines[0])
-            copy_ht(step - 1, 1, engines[1])
+            engines = alone if widening else shared
+            for half in range(2):
+                scale_a(step + 2, half)
+                copy_ht(step - 1, half, engines[half])
+            if widening and 2 * K < 2 * K:
+                widen(step + 3, "scalar", slice(2 * K, 2 * K))
             if step == PAIRS - 3:
                 turn_lev(0)
             product_h(step, 0)
             product_h(step, 1)
-            if step >= 2:
-                interleave_h(step - 2, "vector", slice(GPSIMD_COLUMNS, 512))
+            if step >= 2 and not widening and columns < 512:
+                interleave_h(step - 2, "vector", slice(columns, 512))
             if step == PAIRS - 3:
                 store_lev(0, range(EARLY_GROUPS))
-            if step >= 3:
-                quantize_hc(step - 3)
-            else:
-                quantize_b(step - 1)
-            quantize_a(step + 2)
             quantize_ht(step - 1)
+            if step <= 2:
+                quantize_b(step - 1)
+            else:
+                quantize_hc(step - 3)
+            quantize_a(step + 2)
+            if widening:
+                interleave_h(step - 2, "vector")
             if step >= 2:
                 product_y(step - 2, alone)
 
@@ -504,22 +511,22 @@ def tile_weighted_leverage_sketch_s8_kernel(
         copy_ht(end, 0, "scalar")
         copy_ht(end, 1, "scalar")
         product_y(end - 1, alone)
-        product_c(4, 10)
-        quantize_hc(10)
+        product_c(4, 9)
         quantize_ht(end)
+        quantize_hc(10)
         quantize_hc(11)
         sum_squares(end - 2, 1)
         for i in (1, 0):
             for h in range(NG):
                 matmul_y(end, i, h, hold=True)
-        product_c(10, 12)
+        product_c(9, 12)
         sum_squares(end - 1, 0)
-        sum_squares(end - 1, 1, "vector")
         store_y(end, 1, "vector")
-        sum_squares(end, 0, "scalar", y_bank)
-        store_y(end, 0, "scalar")
+        sum_squares(end - 1, 1)
+        store_y(end, 0, "vector")
+        sum_squares(end, 1)
+        sum_squares(end, 0)
         store_c(0, "vector")
-        sum_squares(end, 1, "vector")
-        store_c(1, "scalar")
+        store_c(1, "vector")
         turn_lev(1)
         store_lev(1, range(EARLY_GROUPS, GROUPS))

@@ -41,12 +41,16 @@ def tile_weighted_leverage_sketch_s8_kernel(
 
         ring = list(range(BANKS))
 
-        def take_bank(hold=False, dtype=F32):
+        bank, bank_number = {}, {}
+
+        def take_bank(key, dtype=F32):
             number = ring[0]
             ring.remove(number)
-            if not hold:
-                ring.append(number)
-            return psum.tile([P, 512 if dtype is F32 else 1024], dtype, name=f"bank{number}", tag=f"bank{number}")
+            bank_number[key] = number
+            bank[key] = psum.tile([P, 512 if dtype is F32 else 1024], dtype, name=f"bank{number}", tag=f"bank{number}")
+
+        def give_bank(key):
+            ring.append(bank_number[key])
 
         def copy_on(engine, out, in_):
             if engine == "scalar":
@@ -142,7 +146,7 @@ def tile_weighted_leverage_sketch_s8_kernel(
                     in_=grouped.rearrange("p n t -> p (n t)"),
                 )
 
-        a_wide, a_bank, a_grouped, a_codes, a_scales = {}, {}, {}, {}, {}
+        a_wide, a_grouped, a_codes, a_scales = {}, {}, {}, {}
 
         def widen(pair, engine, cols=slice(0, 2 * K)):
             if pair not in a_wide:
@@ -153,10 +157,10 @@ def tile_weighted_leverage_sketch_s8_kernel(
 
         def turn_a_plane(pair, i, s):
             if s == 0:
-                a_bank[pair, i] = take_bank(dtype=BF16)
+                take_bank(("a", pair, i), BF16)
             g, t = s // 4, s % 4
             nc.tensor.matmul(
-                out=a_bank[pair, i][:, s * P : (s + 1) * P],
+                out=bank["a", pair, i][:, s * P : (s + 1) * P],
                 lhsT=a_wide[pair][:, K * i + 512 * g + t : K * i + 512 * (g + 1) : 4],
                 rhs=ident_bf[:],
                 start=True,
@@ -170,22 +174,23 @@ def tile_weighted_leverage_sketch_s8_kernel(
                 a_grouped[pair] = work.tile([P, 2 * K], BF16, name="a_grouped", tag=tag, bufs=bufs, align_bytes=64)
             nc.vector.tensor_tensor(
                 out=a_grouped[pair][:, K * i : K * (i + 1)].rearrange("p (g c t) -> p g c t", g=KG, t=4),
-                in0=a_bank[pair, i][:].rearrange("p (g t c) -> p g c t", g=KG, t=4),
+                in0=bank["a", pair, i][:].rearrange("p (g t c) -> p g c t", g=KG, t=4),
                 in1=scale_p[:].unsqueeze(2).to_broadcast([P, KG, P, 4]),
                 op=MULT,
             )
+            give_bank(("a", pair, i))
 
         def quantize_a(pair):
             a_codes[pair], a_scales[pair] = quantize(a_grouped[pair][:], "a", work, 4)
 
-        h_bank, h_rows = {}, {}
+        h_rows = {}
 
         def matmul_h(pair, i, h):
-            h_bank[pair, i, h] = take_bank()
+            take_bank(("h", pair, i, h))
             for g in range(KG):
                 rows = slice((2 * i + g) * P, (2 * i + g + 1) * P)
                 nc.tensor.matmul_mx(
-                    out=h_bank[pair, i, h][:],
+                    out=bank["h", pair, i, h][:],
                     lhsT=a_codes[pair][:, rows].bitcast(FP8X4),
                     lhsT_scale=a_scales[pair][:, rows],
                     rhs=r_codes[h, g][:].bitcast(FP8X4),
@@ -201,30 +206,32 @@ def tile_weighted_leverage_sketch_s8_kernel(
             out = h_rows[group, h][:, t, :]
             weight = w_sb[:, 4 * group + t : 4 * group + t + 1]
             if engine == "vector":
-                nc.vector.tensor_scalar(out=out, in0=h_bank[pair, i, h][:], scalar1=weight, scalar2=None, op0=MULT)
+                nc.vector.tensor_scalar(out=out, in0=bank["h", pair, i, h][:], scalar1=weight, scalar2=None, op0=MULT)
             else:
-                nc.scalar.activation(out=out, in_=h_bank[pair, i, h][:], func=COPY, scale=weight)
+                nc.scalar.activation(out=out, in_=bank["h", pair, i, h][:], func=COPY, scale=weight)
+            give_bank(("h", pair, i, h))
 
-        ht_bank, ht_grouped, ht_codes, ht_scales = {}, {}, {}, {}
+        ht_grouped, ht_codes, ht_scales = {}, {}, {}
 
         def turn_h_words(pair, h, s):
             if s == 0:
-                ht_bank[pair, h] = take_bank()
+                take_bank(("ht", pair, h))
             i, u = s // 2, s % 2
             words = h_rows[pair // 2, h][:, 2 * (pair % 2) + i, :].bitcast(F32)
-            nc.tensor.transpose(ht_bank[pair, h][:, s * P : (s + 1) * P], words[:, u * P : (u + 1) * P], ident[:])
+            nc.tensor.transpose(bank["ht", pair, h][:, s * P : (s + 1) * P], words[:, u * P : (u + 1) * P], ident[:])
 
-        def copy_words(engine, grouped, bank):
+        def copy_words(engine, grouped, key):
             copy_on(
                 engine,
                 grouped.bitcast(F32).rearrange("p (i r u) -> p i r u", i=2, u=2),
-                bank[:].rearrange("p (i u r) -> p i r u", i=2, u=2),
+                bank[key][:].rearrange("p (i u r) -> p i r u", i=2, u=2),
             )
+            give_bank(key)
 
         def copy_ht(pair, h, engine):
             if h == 0:
                 ht_grouped[pair] = work.tile([P, 2 * N], BF16, name="ht_grouped", tag="ht_grouped", bufs=2, align_bytes=64)
-            copy_words(engine, ht_grouped[pair][:, N * h : N * (h + 1)], ht_bank[pair, h])
+            copy_words(engine, ht_grouped[pair][:, N * h : N * (h + 1)], ("ht", pair, h))
 
         def quantize_ht(pair, halves=range(NG)):
             cols = slice(N * halves[0], N * (halves[-1] + 1))
@@ -232,15 +239,15 @@ def tile_weighted_leverage_sketch_s8_kernel(
             for n, h in enumerate(halves):
                 ht_codes[pair, h], ht_scales[pair, h] = codes[:, 256 * n : 256 * (n + 1)], scales[:, 256 * n : 256 * (n + 1)]
 
-        y_bank, y_sb = {}, {}
+        y_sb = {}
         y_view = y.rearrange("(g p t) n -> g t p n", p=P, t=4)
 
-        def matmul_y(pair, i, h, hold=False):
+        def matmul_y(pair, i, h):
             if h == 0:
-                y_bank[pair, i] = take_bank(hold=hold)
+                take_bank(("y", pair, i))
             rows = slice(i * P, (i + 1) * P)
             nc.tensor.matmul_mx(
-                out=y_bank[pair, i][:],
+                out=bank["y", pair, i][:],
                 lhsT=ht_codes[pair, h][:, rows].bitcast(FP8X4),
                 lhsT_scale=ht_scales[pair, h][:, rows],
                 rhs=j_words[:, h, :].bitcast(FP4X4),
@@ -251,14 +258,15 @@ def tile_weighted_leverage_sketch_s8_kernel(
 
         def store_y(pair, i, engine):
             y_sb[pair, i] = work.tile([P, R], F32, name="y_sb", tag="y_sb", bufs=6, align_bytes=64)
-            copy_on(engine, y_sb[pair, i][:], y_bank[pair, i][:])
+            copy_on(engine, y_sb[pair, i][:], bank["y", pair, i][:])
+            give_bank(("y", pair, i))
             nc.sync.dma_start(out=y_view[pair // 2, 2 * (pair % 2) + i], in_=y_sb[pair, i][:])
 
-        def sum_squares(pair, i, engine="scalar", source=y_sb):
+        def sum_squares(pair, i, engine="scalar"):
             squares = work.tile([P, R], BF16, name="squares", tag="squares", bufs=2, align_bytes=64)
             group = pair // 2
             total = lev_sb[group // EARLY_GROUPS][:, 2 * (pair % 2) + i, group : group + 1]
-            rows = source[pair, i][:]
+            rows = y_sb[pair, i][:]
             if engine == "vector":
                 nc.vector.scalar_tensor_tensor(
                     out=squares[:], in0=rows, scalar=1.0 / R, in1=rows, op0=MULT, op1=MULT, accum_out=total
@@ -302,15 +310,21 @@ def tile_weighted_leverage_sketch_s8_kernel(
         b_codes = keep.tile([P, GROUPS * P], U32, name="b_codes", align_bytes=64)
         b_scales = keep.tile([P, GROUPS * P], U8, name="b_scales", align_bytes=64)
 
-        def turn_b(j, engine):
-            bank = take_bank()
-            words = b_sb[j][:].bitcast(F32)
+        def turn_b_words(j, s):
+            if s == 0:
+                take_bank(("b", j))
+            group, u = s // 2, s % 2
+            words = b_sb[j][:].bitcast(F32)[:, 256 * group + u : 256 * (group + 1) : 2]
+            nc.tensor.transpose(bank["b", j][:, s * P : (s + 1) * P], words, ident[:])
+
+        def turn_b(j):
             for s in range(4):
-                group, u = s // 2, s % 2
-                nc.tensor.transpose(bank[:, s * P : (s + 1) * P], words[:, 256 * group + u : 256 * (group + 1) : 2], ident[:])
+                turn_b_words(j, s)
+
+        def copy_b(j, engine):
             if j % 2 == 0:
                 b_grouped[j // 2] = work.tile([P, 2048], BF16, name="b_grouped", tag="r_grouped", bufs=2, align_bytes=64)
-            copy_words(engine, b_grouped[j // 2][:, 1024 * (j % 2) : 1024 * (j % 2 + 1)], bank)
+            copy_words(engine, b_grouped[j // 2][:, 1024 * (j % 2) : 1024 * (j % 2 + 1)], ("b", j))
 
         def quantize_b(part):
             width = 2048 if part == 0 else 1024
@@ -319,15 +333,13 @@ def tile_weighted_leverage_sketch_s8_kernel(
                 out=b_codes[:, cols].bitcast(FP8X4), scales=b_scales[:, cols], in_=b_grouped[part][:, :width]
             )
 
-        c_bank = {}
-
         def matmul_c(n):
             group, h = n // 2, n % 2
             if group == 0:
-                c_bank[h] = take_bank(hold=True)
+                take_bank(("c", h))
             rows = slice(group * P, (group + 1) * P)
             nc.tensor.matmul_mx(
-                out=c_bank[h][:],
+                out=bank["c", h][:],
                 lhsT=b_codes[:, rows].bitcast(FP8X4),
                 lhsT_scale=b_scales[:, rows],
                 rhs=hc_codes[n][:].bitcast(FP8X4),
@@ -341,7 +353,7 @@ def tile_weighted_leverage_sketch_s8_kernel(
             copy_on(
                 engine,
                 c_sb[:].rearrange("p (q u e) -> p q u e", u=2, e=2),
-                c_bank[h][:].rearrange("p (u q e) -> p q u e", u=2, e=2),
+                bank["c", h][:].rearrange("p (u q e) -> p q u e", u=2, e=2),
             )
             nc.sync.dma_start(out=c[:, 512 * h : 512 * (h + 1)], in_=c_sb[:])
 
@@ -358,12 +370,15 @@ def tile_weighted_leverage_sketch_s8_kernel(
                 for s in range(4):
                     turn_h_words(pair, h, s)
 
-        def turn_both(pair_a, pair_h):
+        def turn_a_with(pair, turn_words):
             for half in range(2):
                 for s in range(4):
-                    turn_a_plane(pair_a, half, 2 * s)
-                    turn_a_plane(pair_a, half, 2 * s + 1)
-                    turn_h_words(pair_h, half, s)
+                    turn_a_plane(pair, half, 2 * s)
+                    turn_words(half, s)
+                    turn_a_plane(pair, half, 2 * s + 1)
+
+        def turn_both(pair_a, pair_h):
+            turn_a_with(pair_a, lambda half, s: turn_h_words(pair_h, half, s))
 
         def product_h(pair, h, engines=("scalar", "scalar")):
             for i in range(2):
@@ -383,8 +398,8 @@ def tile_weighted_leverage_sketch_s8_kernel(
 
         load_a(0)
         load_rinv(0, 0)
-        load_a(1)
         load_rinv(0, 1)
+        load_a(1)
         load_rinv(1, 0)
         load_a(2)
         load_rinv(1, 1)
@@ -405,10 +420,10 @@ def tile_weighted_leverage_sketch_s8_kernel(
         turn_a(0)
         interleave_rinv(0, 0, 0, "vector")
         interleave_rinv(0, 0, 1, "vector")
-        widen(1, "scalar")
-        turn_a(1)
         interleave_rinv(0, 1, 0, "scalar")
         interleave_rinv(0, 1, 1, "gpsimd")
+        widen(1, "scalar")
+        turn_a(1)
         scale_a(0, 0)
         scale_a(0, 1)
         interleave_rinv(1, 0, 0, "scalar")
@@ -429,12 +444,15 @@ def tile_weighted_leverage_sketch_s8_kernel(
         quantize_rinv(1, 1)
         quantize_a(1)
         widen(4, "gpsimd")
-        turn_b(0, "scalar")
-        turn_b(1, "scalar")
+        turn_b(0)
+        copy_b(0, "scalar")
+        turn_b(1)
+        copy_b(1, "scalar")
         product_h(0, 1)
         scale_a(2, 0)
         scale_a(2, 1)
-        turn_b(2, "scalar")
+        turn_b(2)
+        copy_b(2, "scalar")
         quantize_a(2)
         widen(5, "gpsimd")
 
@@ -503,23 +521,24 @@ def tile_weighted_leverage_sketch_s8_kernel(
         product_h(end, 0)
         product_h(end, 1)
         product_y(end - 2, alone)
-        product_c(2, 4)
         turn_h(end)
         interleave_h(10, "vector")
         interleave_h(11, "vector")
-        sum_squares(end - 2, 0)
         copy_ht(end, 0, "scalar")
         copy_ht(end, 1, "scalar")
+        sum_squares(end - 2, 0)
         product_y(end - 1, alone)
-        product_c(4, 9)
+        product_c(2, 6)
         quantize_ht(end)
         quantize_hc(10)
         quantize_hc(11)
         sum_squares(end - 2, 1)
         for i in (1, 0):
             for h in range(NG):
-                matmul_y(end, i, h, hold=True)
-        product_c(9, 12)
+                matmul_y(end, i, h)
+        for h in range(NG):
+            for group in range(3, GROUPS):
+                matmul_c(2 * group + h)
         sum_squares(end - 1, 0)
         store_y(end, 1, "vector")
         sum_squares(end - 1, 1)
@@ -527,6 +546,6 @@ def tile_weighted_leverage_sketch_s8_kernel(
         sum_squares(end, 1)
         sum_squares(end, 0)
         store_c(0, "vector")
-        store_c(1, "vector")
         turn_lev(1)
+        store_c(1, "scalar")
         store_lev(1, range(EARLY_GROUPS, GROUPS))

@@ -70,7 +70,6 @@ def tile_weighted_leverage_sketch_s8_kernel(
         scale_p = keep.tile([P, KG, 4], F32, name="scale_p", align_bytes=64)
         nc.scalar.dma_start(out=scale_p[:], in_=a_scale.rearrange("o (g p t) -> p (o g) t", p=P, t=4))
         w_bf = keep.tile([P, GROUPS, 4], BF16, name="w_bf", align_bytes=64)
-        nc.scalar.dma_start(out=w_bf[:], in_=w.rearrange("(g p t) -> p g t", p=P, t=4))
 
         ident = keep.tile([P, P], F32, name="ident", align_bytes=64)
         make_identity(nc, ident[:])
@@ -112,6 +111,9 @@ def tile_weighted_leverage_sketch_s8_kernel(
                 )
 
         w_sb = keep.tile([P, GROUPS * 4], F32, name="w_sb", align_bytes=64)
+
+        def load_w():
+            nc.sync.dma_start(out=w_bf[:], in_=w.rearrange("(g p t) -> p g t", p=P, t=4))
 
         def cast_w():
             nc.scalar.activation(out=w_sb[:], in_=w_bf[:].rearrange("p g t -> p (g t)"), func=COPY)
@@ -403,6 +405,7 @@ def tile_weighted_leverage_sketch_s8_kernel(
         load_rinv(1, 0)
         load_a(2)
         load_rinv(1, 1)
+        load_w()
         load_a(3)
         for j in range(3):
             load_b(j)
@@ -428,12 +431,12 @@ def tile_weighted_leverage_sketch_s8_kernel(
         scale_a(0, 1)
         interleave_rinv(1, 0, 0, "scalar")
         widen(2, "scalar")
-        cast_w()
         quantize_rinv(0, 0)
         interleave_rinv(1, 0, 1, "gpsimd")
         quantize_a(0)
         quantize_rinv(0, 1)
         interleave_rinv(1, 1, 0, "scalar")
+        cast_w()
         scale_a(1, 0)
         scale_a(1, 1)
         product_h(0, 0)

from contextlib import ExitStack

import concourse.mybir as mybir
from concourse.masks import make_identity

M, K, N, R, T = 3072, 1024, 1024, 512, 128
FLOPS = 2 * M * K * N + 2 * M * N * R + 2 * T * M * N

F32 = mybir.dt.float32
BF16 = mybir.dt.bfloat16
I32 = mybir.dt.int32
U32 = mybir.dt.uint32
U8 = mybir.dt.uint8
FP8 = mybir.dt.float8_e4m3fn
FP8X4 = mybir.dt.float8_e4m3fn_x4
FP4X4 = mybir.dt.float4_e2m1fn_x4
MULT = mybir.AluOpType.mult
COPY = mybir.ActivationFunctionType.Copy
SQUARE = mybir.ActivationFunctionType.Square

P = 128
GROUPS = M // 512
PAIRS = M // (2 * P)
KG = K // 512
NG = N // 512
BANKS = 8
EARLY_PAIR = 10
EARLY_GROUPS = 3
GPSIMD_COLUMNS = 400


def tile_weighted_leverage_sketch_s8_kernel(
    tc, a_bytes, a_scale, rinv, w, jl_words, jl_scales, b, y, lev, c
):
    nc = tc.nc
    with ExitStack() as ctx:
        keep = ctx.enter_context(tc.tile_pool(name="keep", bufs=1))
        work = ctx.enter_context(tc.tile_pool(name="work", bufs=3))
        psum = ctx.enter_context(tc.psum_pool(name="psum", bufs=1))
        ctx.enter_context(tc.manual_schedule())

        ring = list(range(BANKS))

        bank, bank_number = {}, {}

        def take_bank(key, dtype=F32):
            number = ring[0]
            ring.remove(number)
            bank_number[key] = number
            bank[key] = psum.tile([P, 512 if dtype is F32 else 1024], dtype, name=f"bank{number}", tag=f"bank{number}")

        def give_bank(key):
            ring.append(bank_number[key])

        def copy_on(engine, out, in_):
            if engine == "scalar":
                nc.scalar.copy(out=out, in_=in_)
            elif engine == "vector":
                nc.vector.tensor_copy(out=out, in_=in_)
            else:
                nc.gpsimd.tensor_copy(out=out, in_=in_)

        def quantize(grouped, name, pool, bufs):
            width = grouped.shape[1] // 4
            codes = pool.tile([P, width], U32, name=name + "_codes", tag=name + "_codes", bufs=bufs, align_bytes=64)
            scales = pool.tile([P, width], U8, name=name + "_scales", tag=name + "_scales", bufs=bufs, align_bytes=64)
            nc.vector.quantize_mx(out=codes[:].bitcast(FP8X4), scales=scales[:], in_=grouped)
            return codes, scales

        scale_p = keep.tile([P, KG, 4], F32, name="scale_p", align_bytes=64)
        nc.scalar.dma_start(out=scale_p[:], in_=a_scale.rearrange("o (g p t) -> p (o g) t", p=P, t=4))
        w_bf = keep.tile([P, GROUPS, 4], BF16, name="w_bf", align_bytes=64)

        ident = keep.tile([P, P], F32, name="ident", align_bytes=64)
        make_identity(nc, ident[:])
        ident_bf = keep.tile([P, P], BF16, name="ident_bf", align_bytes=64)
        nc.scalar.activation(out=ident_bf[:], in_=ident[:], func=COPY)
        j_scales = keep.tile([P, NG, R], U8, name="j_scales", align_bytes=64)
        j_scales_i32 = j_scales[:].rearrange("p g n -> p (g n)").bitcast(I32)
        nc.vector.memset(j_scales_i32, 0)
        lev_sb = {}
        for part in range(2):
            lev_sb[part] = keep.tile([P, 4, 32], F32, name=f"lev_sb{part}", align_bytes=64)
            nc.vector.memset(lev_sb[part][:], 0.0)

        a_view = a_bytes.rearrange("(g p t) k -> g p t k", p=P, t=4)
        rinv_view = rinv.rearrange("(g p t) n -> g p t n", p=P, t=4)
        a8, r_raw, b_sb = {}, {}, {}

        def load_a(pair):
            t0 = 2 * (pair % 2)
            a8[pair] = keep.tile([P, 2, K], U8, name=f"a8_{pair}", align_bytes=64)
            nc.sync.dma_start(out=a8[pair][:], in_=a_view[pair // 2, :, t0 : t0 + 2, :])

        def load_rinv(h, g):
            r_raw[h, g] = work.tile([P, 4, 512], BF16, name="r_raw", tag="h_rows", bufs=6, align_bytes=64)
            nc.sync.dma_start(out=r_raw[h, g][:], in_=rinv_view[g, :, :, 512 * h : 512 * (h + 1)])

        def load_b(j):
            b_sb[j] = keep.tile([P, 1024], BF16, name=f"b_sb_{j}", align_bytes=64)
            nc.sync.dma_start(out=b_sb[j][:], in_=b[:, 1024 * j : 1024 * (j + 1)])

        j_words = keep.tile([P, NG, 2 * R], U8, name="j_words", align_bytes=64)

        def load_j():
            nc.sync.dma_start(out=j_words[:], in_=jl_words.rearrange("g p n -> p g n"))
            for q in range(4):
                nc.sync.dma_start(
                    out=j_scales_i32[32 * q : 32 * q + 4, :].rearrange("p (g n) -> p g n", g=NG),
                    in_=jl_scales[:, 4 * q : 4 * q + 4, :].bitcast(I32).rearrange("g q n -> q g n"),
                )

        w_sb = keep.tile([P, GROUPS * 4], F32, name="w_sb", align_bytes=64)

        def load_w():
            nc.sync.dma_start(out=w_bf[:], in_=w.rearrange("(g p t) -> p g t", p=P, t=4))

        def cast_w():
            nc.scalar.activation(out=w_sb[:], in_=w_bf[:].rearrange("p g t -> p (g t)"), func=COPY)

        r_grouped, r_codes, r_scales = {}, {}, {}

        def interleave_rinv(h, g, u, engine):
            if (h, g) == (1, 0):
                tag, bufs = ("ht_grouped", 2) if u else ("gate4", 1)
                r_grouped[h, g, u] = work.tile([P, 256, 4], BF16, name="r_half", tag=tag, bufs=bufs, align_bytes=64)[:]
            else:
                if u == 0:
                    tag = "r_grouped" if h else "ht_grouped"
                    r_grouped[h, g] = work.tile([P, 512, 4], BF16, name="r_grouped", tag=tag, bufs=2, align_bytes=64)
                r_grouped[h, g, u] = r_grouped[h, g][:, 256 * u : 256 * (u + 1), :]
            out = r_grouped[h, g, u].rearrange("p (q e) t -> p q e t", e=2)
            in_ = r_raw[h, g][:].rearrange("p t (q u e) -> p u q e t", u=2, e=2)[:, u]
            if engine != "gpsimd":
                out, in_ = out.rearrange("p q e t -> p q t e"), in_.rearrange("p q e t -> p q t e")
            copy_on(engine, out, in_)

        def quantize_rinv(h, g):
            r_codes[h, g] = keep.tile([P, 512], U32, name=f"r{h}{g}_codes", align_bytes=64)
            r_scales[h, g] = keep.tile([P, 512], U8, name=f"r{h}{g}_scales", align_bytes=64)
            parts = [(r_grouped[h, g][:], slice(0, 512))] if (h, g) in r_grouped else [
                (r_grouped[h, g, u], slice(256 * u, 256 * (u + 1))) for u in range(2)
            ]
            for grouped, cols in parts:
                nc.vector.quantize_mx(
                    out=r_codes[h, g][:, cols].bitcast(FP8X4),
                    scales=r_scales[h, g][:, cols],
                    in_=grouped.rearrange("p n t -> p (n t)"),
                )

        a_wide, a_grouped, a_codes, a_scales = {}, {}, {}, {}

        def widen(pair, engine, cols=slice(0, 2 * K)):
            if pair not in a_wide:
                tag, bufs = (f"gate{pair}", 1) if 4 <= pair < EARLY_PAIR else ("a_wide", 4)
                a_wide[pair] = work.tile([P, 2 * K], BF16, name="a_wide", tag=tag, bufs=bufs, align_bytes=64)
            codes = a8[pair][:].rearrange("p i k -> p (i k)")
            copy_on(engine, a_wide[pair][:, cols], codes[:, cols].bitcast(FP8))

        def turn_a_plane(pair, i, s):
            if s == 0:
                take_bank(("a", pair, i), BF16)
            g, t = s // 4, s % 4
            nc.tensor.matmul(
                out=bank["a", pair, i][:, s * P : (s + 1) * P],
                lhsT=a_wide[pair][:, K * i + 512 * g + t : K * i + 512 * (g + 1) : 4],
                rhs=ident_bf[:],
                start=True,
                stop=True,
            )

        def scale_a(pair, i):
            if i == 0:
                freed = 5 if pair == 2 else pair + 2
                tag, bufs = (f"gate{freed}", 1) if pair == 2 or 6 <= freed < EARLY_PAIR else ("a_grouped", 2)
                a_grouped[pair] = work.tile([P, 2 * K], BF16, name="a_grouped", tag=tag, bufs=bufs, align_bytes=64)
            nc.vector.tensor_tensor(
                out=a_grouped[pair][:, K * i : K * (i + 1)].rearrange("p (g c t) -> p g c t", g=KG, t=4),
                in0=bank["a", pair, i][:].rearrange("p (g t c) -> p g c t", g=KG, t=4),
                in1=scale_p[:].unsqueeze(2).to_broadcast([P, KG, P, 4]),
                op=MULT,
            )
            give_bank(("a", pair, i))

        def quantize_a(pair):
            a_codes[pair], a_scales[pair] = quantize(a_grouped[pair][:], "a", work, 4)

        h_rows = {}

        def matmul_h(pair, i, h):
            take_bank(("h", pair, i, h))
            for g in range(KG):
                rows = slice((2 * i + g) * P, (2 * i + g + 1) * P)
                nc.tensor.matmul_mx(
                    out=bank["h", pair, i, h][:],
                    lhsT=a_codes[pair][:, rows].bitcast(FP8X4),
                    lhsT_scale=a_scales[pair][:, rows],
                    rhs=r_codes[h, g][:].bitcast(FP8X4),
                    rhs_scale=r_scales[h, g][:],
                    start=(g == 0),
                    stop=(g == KG - 1),
                )

        def weigh_h(pair, i, h, engine):
            group, t = pair // 2, 2 * (pair % 2) + i
            if (group, h) not in h_rows:
                h_rows[group, h] = work.tile([P, 4, 512], BF16, name="h_rows", tag="h_rows", bufs=6, align_bytes=64)
            out = h_rows[group, h][:, t, :]
            weight = w_sb[:, 4 * group + t : 4 * group + t + 1]
            if engine == "vector":
                nc.vector.tensor_scalar(out=out, in0=bank["h", pair, i, h][:], scalar1=weight, scalar2=None, op0=MULT)
            else:
                nc.scalar.activation(out=out, in_=bank["h", pair, i, h][:], func=COPY, scale=weight)
            give_bank(("h", pair, i, h))

        ht_grouped, ht_codes, ht_scales = {}, {}, {}

        def turn_h_words(pair, h, s):
            if s == 0:
                take_bank(("ht", pair, h))
            i, u = s // 2, s % 2
            words = h_rows[pair // 2, h][:, 2 * (pair % 2) + i, :].bitcast(F32)
            nc.tensor.transpose(bank["ht", pair, h][:, s * P : (s + 1) * P], words[:, u * P : (u + 1) * P], ident[:])

        def copy_words(engine, grouped, key):
            copy_on(
                engine,
                grouped.bitcast(F32).rearrange("p (i r u) -> p i r u", i=2, u=2),
                bank[key][:].rearrange("p (i u r) -> p i r u", i=2, u=2),
            )
            give_bank(key)

        def copy_ht(pair, h, engine):
            if h == 0:
                ht_grouped[pair] = work.tile([P, 2 * N], BF16, name="ht_grouped", tag="ht_grouped", bufs=2, align_bytes=64)
            copy_words(engine, ht_grouped[pair][:, N * h : N * (h + 1)], ("ht", pair, h))

        def quantize_ht(pair, halves=range(NG)):
            cols = slice(N * halves[0], N * (halves[-1] + 1))
            codes, scales = quantize(ht_grouped[pair][:, cols], "ht", work, 3)
            for n, h in enumerate(halves):
                ht_codes[pair, h], ht_scales[pair, h] = codes[:, 256 * n : 256 * (n + 1)], scales[:, 256 * n : 256 * (n + 1)]

        y_sb = {}
        y_view = y.rearrange("(g p t) n -> g t p n", p=P, t=4)

        def matmul_y(pair, i, h):
            if h == 0:
                take_bank(("y", pair, i))
            rows = slice(i * P, (i + 1) * P)
            nc.tensor.matmul_mx(
                out=bank["y", pair, i][:],
                lhsT=ht_codes[pair, h][:, rows].bitcast(FP8X4),
                lhsT_scale=ht_scales[pair, h][:, rows],
                rhs=j_words[:, h, :].bitcast(FP4X4),
                rhs_scale=j_scales[:, h, :],
                start=(h == 0),
                stop=(h == NG - 1),
            )

        def store_y(pair, i, engine):
            y_sb[pair, i] = work.tile([P, R], F32, name="y_sb", tag="y_sb", bufs=6, align_bytes=64)
            copy_on(engine, y_sb[pair, i][:], bank["y", pair, i][:])
            give_bank(("y", pair, i))
            nc.sync.dma_start(out=y_view[pair // 2, 2 * (pair % 2) + i], in_=y_sb[pair, i][:])

        def sum_squares(pair, i, engine="scalar"):
            squares = work.tile([P, R], BF16, name="squares", tag="squares", bufs=2, align_bytes=64)
            group = pair // 2
            total = lev_sb[group // EARLY_GROUPS][:, 2 * (pair % 2) + i, group : group + 1]
            rows = y_sb[pair, i][:]
            if engine == "vector":
                nc.vector.scalar_tensor_tensor(
                    out=squares[:], in0=rows, scalar=1.0 / R, in1=rows, op0=MULT, op1=MULT, accum_out=total
                )
            else:
                nc.scalar.activation(out=squares[:], in_=rows, func=SQUARE, scale=R**-0.5, accum_out=total)

        lev_turned = {}

        def turn_lev(part):
            lev_turned[part] = keep.tile([P, 4, 32], F32, name=f"lev_turned{part}", align_bytes=64)
            nc.vector.transpose(
                out=lev_turned[part][:].rearrange("p t j -> p (t j)"), in_=lev_sb[part][:].rearrange("p t g -> p (t g)")
            )

        def store_lev(part, groups):
            lev_rows = keep.tile([P, 32, 4], F32, name=f"lev_rows{part}", align_bytes=64)
            nc.vector.tensor_copy(out=lev_rows[:], in_=lev_turned[part][:].rearrange("p t j -> p j t"))
            for group in groups:
                queue = nc.scalar if group == GROUPS - 2 else nc.sync
                queue.dma_start(
                    out=lev[512 * group : 512 * (group + 1)].rearrange("(q m) -> q m", q=4),
                    in_=lev_rows[group:P:32].rearrange("p j t -> p (j t)"),
                )

        hc_grouped, hc_codes, hc_scales = {}, {}, {}

        def interleave_h(n, engine, cols=slice(0, 512)):
            if n not in hc_grouped:
                hc_grouped[n] = work.tile([P, 512, 4], BF16, name="hc_grouped", tag="r_grouped", bufs=2, align_bytes=64)
            out, in_ = hc_grouped[n][:, cols, :], h_rows[n // 2, n % 2][:, :, cols]
            if engine == "gpsimd":
                copy_on(engine, out, in_.rearrange("p t c -> p c t"))
            else:
                copy_on(engine, out.rearrange("p (c i) t -> p c t i", i=4), in_.rearrange("p t (c i) -> p c t i", i=4))

        def quantize_hc(n):
            hc_codes[n], hc_scales[n] = quantize(hc_grouped[n][:].rearrange("p c t -> p (c t)"), f"hc{n}", keep, 1)

        b_grouped = {}
        b_codes = keep.tile([P, GROUPS * P], U32, name="b_codes", align_bytes=64)
        b_scales = keep.tile([P, GROUPS * P], U8, name="b_scales", align_bytes=64)

        def turn_b_words(j, s):
            if s == 0:
                take_bank(("b", j))
            group, u = s // 2, s % 2
            words = b_sb[j][:].bitcast(F32)[:, 256 * group + u : 256 * (group + 1) : 2]
            nc.tensor.transpose(bank["b", j][:, s * P : (s + 1) * P], words, ident[:])

        def turn_b(j):
            for s in range(4):
                turn_b_words(j, s)

        def copy_b(j, engine):
            if j % 2 == 0:
                b_grouped[j // 2] = work.tile([P, 2048], BF16, name="b_grouped", tag="r_grouped", bufs=2, align_bytes=64)
            copy_words(engine, b_grouped[j // 2][:, 1024 * (j % 2) : 1024 * (j % 2 + 1)], ("b", j))

        def quantize_b(part):
            width = 2048 if part == 0 else 1024
            cols = slice(512 * part, 512 * part + width // 4)
            nc.vector.quantize_mx(
                out=b_codes[:, cols].bitcast(FP8X4), scales=b_scales[:, cols], in_=b_grouped[part][:, :width]
            )

        def matmul_c(n):
            group, h = n // 2, n % 2
            if group == 0:
                take_bank(("c", h))
            rows = slice(group * P, (group + 1) * P)
            nc.tensor.matmul_mx(
                out=bank["c", h][:],
                lhsT=b_codes[:, rows].bitcast(FP8X4),
                lhsT_scale=b_scales[:, rows],
                rhs=hc_codes[n][:].bitcast(FP8X4),
                rhs_scale=hc_scales[n][:],
                start=(group == 0),
                stop=(group == GROUPS - 1),
            )

        def store_c(h, engine):
            c_sb = work.tile([P, 512], F32, name="c_sb", tag="y_sb", bufs=6, align_bytes=64)
            copy_on(
                engine,
                c_sb[:].rearrange("p (q u e) -> p q u e", u=2, e=2),
                bank["c", h][:].rearrange("p (u q e) -> p q u e", u=2, e=2),
            )
            nc.sync.dma_start(out=c[:, 512 * h : 512 * (h + 1)], in_=c_sb[:])

        def live(pair):
            return 0 <= pair < PAIRS

        def turn_a(pair):
            for i in range(2):
                for s in range(8):
                    turn_a_plane(pair, i, s)

        def turn_h(pair, halves=range(NG)):
            for h in halves:
                for s in range(4):
                    turn_h_words(pair, h, s)

        def turn_a_with(pair, turn_words):
            for half in range(2):
                for s in range(4):
                    turn_a_plane(pair, half, 2 * s)
                    turn_words(half, s)
                    turn_a_plane(pair, half, 2 * s + 1)

        def turn_both(pair_a, pair_h):
            turn_a_with(pair_a, lambda half, s: turn_h_words(pair_h, half, s))

        def product_h(pair, h, engines=("scalar", "scalar")):
            for i in range(2):
                matmul_h(pair, i, h)
                weigh_h(pair, i, h, engines[i])

        def product_c(first, last):
            for n in range(first, last):
                matmul_c(n)

        def product_y(pair, engines):
            for i in range(2):
                for h in range(NG):
                    matmul_y(pair, i, h)
                store_y(pair, i, engines[i])


        load_a(0)
        load_rinv(0, 0)
        load_rinv(0, 1)
        load_a(1)
        load_rinv(1, 0)
        load_a(2)
        load_rinv(1, 1)
        load_w()
        load_a(3)
        for j in range(3):
            load_b(j)
        load_a(4)
        load_a(5)
        for pair in range(EARLY_PAIR, PAIRS):
            load_a(pair)
        load_j()
        for pair in range(6, EARLY_PAIR):
            load_a(pair)

        for i in range(2):
            widen(0, "vector", slice(K * i, K * i + 512))
            widen(0, "scalar", slice(K * i + 512, K * (i + 1)))
        turn_a(0)
        interleave_rinv(0, 0, 0, "vector")
        interleave_rinv(0, 0, 1, "vector")
        interleave_rinv(0, 1, 0, "scalar")
        interleave_rinv(0, 1, 1, "gpsimd")
        widen(1, "scalar")
        turn_a(1)
        scale_a(0, 0)
        scale_a(0, 1)
        interleave_rinv(1, 0, 0, "scalar")
        widen(2, "scalar")
        quantize_rinv(0, 0)
        interleave_rinv(1, 0, 1, "gpsimd")
        quantize_a(0)
        quantize_rinv(0, 1)
        interleave_rinv(1, 1, 0, "scalar")
        cast_w()
        scale_a(1, 0)
        scale_a(1, 1)
        product_h(0, 0)
        turn_a(2)
        widen(3, "scalar")
        interleave_rinv(1, 1, 1, "vector")
        quantize_rinv(1, 0)
        quantize_rinv(1, 1)
        quantize_a(1)
        widen(4, "gpsimd")
        turn_b(0)
        copy_b(0, "scalar")
        turn_b(1)
        copy_b(1, "scalar")
        product_h(0, 1)
        scale_a(2, 0)
        scale_a(2, 1)
        turn_b(2)
        copy_b(2, "scalar")
        quantize_a(2)
        widen(5, "gpsimd")

        both, alone, shared = ("vector", "vector"), ("scalar", "scalar"), ("vector", "scalar")
        for step in range(1, PAIRS - 2):
            widening = 6 <= step + 3 < EARLY_PAIR
            columns = GPSIMD_COLUMNS
            if widening:
                widen(step + 3, "gpsimd", slice(0, 2 * K))
            elif step >= 2:
                interleave_h(step - 2, "gpsimd", slice(0, columns))
            turn_both(step + 2, step - 1)
            if step > 2:
                sum_squares(step - 3, 0)
                sum_squares(step - 3, 1)
            for pair in [EARLY_PAIR + step - 1] if EARLY_PAIR + step - 1 < PAIRS else []:
                widen(pair, "scalar")
            engines = alone if widening else shared
            for half in range(2):
                scale_a(step + 2, half)
                copy_ht(step - 1, half, engines[half])
            if widening and 2 * K < 2 * K:
                widen(step + 3, "scalar", slice(2 * K, 2 * K))
            if step == PAIRS - 3:
                turn_lev(0)
            product_h(step, 0)
            product_h(step, 1)
            if step >= 2 and not widening and columns < 512:
                interleave_h(step - 2, "vector", slice(columns, 512))
            if step == PAIRS - 3:
                store_lev(0, range(EARLY_GROUPS))
            quantize_ht(step - 1)
            if step <= 2:
                quantize_b(step - 1)
            else:
                quantize_hc(step - 3)
            quantize_a(step + 2)
            if widening:
                interleave_h(step - 2, "vector")
            if step >= 2:
                product_y(step - 2, alone)


        end = PAIRS - 1
        turn_h(end - 2)
        sum_squares(end - 4, 0)
        sum_squares(end - 4, 1)
        copy_ht(end - 2, 0, "vector")
        copy_ht(end - 2, 1, "vector")
        product_h(end - 1, 0)
        product_h(end - 1, 1)
        quantize_hc(7)
        quantize_ht(end - 2)
        interleave_h(8, "vector")
        interleave_h(9, "vector")
        product_y(end - 3, alone)
        product_c(0, 2)
        turn_h(end - 1)
        sum_squares(end - 3, 0)
        sum_squares(end - 3, 1)
        copy_ht(end - 1, 0, "vector")
        copy_ht(end - 1, 1, "vector")
        quantize_hc(8)
        quantize_ht(end - 1)
        quantize_hc(9)
        product_h(end, 0)
        product_h(end, 1)
        product_y(end - 2, alone)
        turn_h(end)
        interleave_h(10, "vector")
        interleave_h(11, "vector")
        copy_ht(end, 0, "scalar")
        copy_ht(end, 1, "scalar")
        sum_squares(end - 2, 0)
        product_y(end - 1, alone)
        product_c(2, 6)
        quantize_ht(end)
        quantize_hc(10)
        quantize_hc(11)
        sum_squares(end - 2, 1)
        for i in (1, 0):
            for h in range(NG):
                matmul_y(end, i, h)
        for h in range(NG):
            for group in range(3, GROUPS):
                matmul_c(2 * group + h)
        sum_squares(end - 1, 0)
        store_y(end, 1, "vector")
        sum_squares(end - 1, 1)
        store_y(end, 0, "vector")
        sum_squares(end, 1)
        sum_squares(end, 0)
        store_c(0, "vector")
        turn_lev(1)
        store_c(1, "scalar")
        store_lev(1, range(EARLY_GROUPS, GROUPS))
